import numpy as np
import ml_dtypes


def mxq(x, axis, fmt="e4m3"):
    dtype, down = {"e4m3": (ml_dtypes.float8_e4m3fn, 7), "e5m2": (ml_dtypes.float8_e5m2, 14)}[fmt]
    v = np.moveaxis(np.asarray(x, np.float32).astype(ml_dtypes.bfloat16).astype(np.float64), axis, -1)
    blocks = v.reshape(v.shape[:-1] + (-1, 32))
    amax = np.abs(blocks).max(-1, keepdims=True)
    byte = np.maximum(np.where(amax > 0, np.frexp(amax)[1] - 1 + 127, 0) - down, 1)
    scale = np.exp2(byte - 127.0)
    codes = (blocks / scale).astype(np.float32).astype(dtype).astype(np.float64)
    return np.moveaxis((codes * scale).reshape(v.shape), -1, axis)


WIDE = False


def mx_kscale(k):
    if not WIDE:
        return np.ones(k)
    levels = np.array([10, -10, 5, -5, 0])
    if k % 512:
        return np.exp2(np.random.permutation(np.resize(levels, k // 32))).repeat(32)
    a = np.empty((k // 512, 16))
    for p in range(k // 512):
        a[p, :8] = np.random.permutation(np.resize(levels, 8))
        for g in range(8):
            far = levels[np.abs(levels - a[p, g]) >= 10]
            a[p, g + 8] = far[np.random.randint(len(far))]
    return np.exp2(a.ravel()).repeat(32)


def f64(x):
    return np.asarray(x).astype(np.float64)


def striped(idx):
    return np.tile(idx.reshape(-1, 16).T, (8, 1)).astype(np.uint16)


def unstriped(offs):
    return offs[:16].T.reshape(-1).astype(np.int64)


E2M1 = np.array([0.0, 0.5, 1.0, 1.5, 2.0, 3.0, 4.0, 6.0, -0.0, -0.5, -1.0, -1.5, -2.0, -3.0, -4.0, -6.0])


def pack_weight(w, fmt):
    k, n = w.shape
    w = f64(np.asarray(w, np.float32).astype(ml_dtypes.bfloat16)).reshape(k // 32, 32, n)
    amax = np.abs(w).max(1)
    if fmt == "e4m3":
        byte = np.frexp(amax)[1] - 1 + 127 - 7
    else:
        mant, ex = np.frexp(amax / 6.0)
        byte = np.where(mant > 0.5, ex, ex - 1) + 127
    byte = np.clip(np.where(amax > 0, byte, 1), 1, 254)
    scaled = (w * np.exp2(127.0 - byte)[:, None, :]).reshape(k, n).astype(np.float32)
    by_word = np.ascontiguousarray(scaled.reshape(k // 512, 128, 4, n).transpose(0, 1, 3, 2))
    if fmt == "e4m3":
        words = by_word.astype(ml_dtypes.float8_e4m3fn).view(np.uint8)
    else:
        c = by_word.astype(ml_dtypes.float4_e2m1fn).view(np.uint8) & 0xF
        words = (c[..., 0::2] | (c[..., 1::2] << 4)).reshape(k // 512, 128, 2 * n)
    return np.ascontiguousarray(words), np.ascontiguousarray(byte.astype(np.uint8).reshape(k // 512, 16, n))


def unpack_weight(words, scales, fmt):
    g, _, n = scales.shape
    words = np.ascontiguousarray(words).reshape(g, 128, n, -1)
    if fmt == "e4m3":
        vals = words.view(ml_dtypes.float8_e4m3fn).astype(np.float64)
    else:
        nib = np.empty((g, 128, n, 4), np.uint8)
        nib[..., 0::2] = words & 0xF
        nib[..., 1::2] = words >> 4
        vals = E2M1[nib]
    vals = vals * np.repeat(np.exp2(scales.astype(np.float64) - 127.0), 8, axis=1)[..., None]
    return vals.transpose(0, 1, 3, 2).reshape(g * 512, n)


def gelu(v):
    return 0.5 * v * (1.0 + np.tanh(np.sqrt(2.0 / np.pi) * (v + 0.044715 * v**3)))


K, T, S, R, N = 1024, 2048, 1024, 1024, 512

def setup_inputs():
    n = np.random.standard_normal
    s = mx_kscale(K)[:, None]
    u = mx_kscale(R)[:, None]
    tab_words, tab_scales = pack_weight(n((K, T)) * s, "e4m3")
    w4_words, w4_scales = pack_weight(0.8 * n((R, N)) / np.sqrt(R) / u, "e2m1")
    return {
        "tab_words": tab_words, "tab_scales": tab_scales,
        "offs": striped(np.random.permutation(T)[:S]),
        "w1": (n((K, R)) / np.sqrt(K) / s).astype(np.float32),
        "cap": (np.exp(0.2 * n(R)) * u[:, 0]).astype(np.float32),
        "w4_words": w4_words, "w4_scales": w4_scales,
        "gT": np.exp(0.3 * n((N, T)) - 0.1).astype(np.float32),
    }

def reference(tab_words, tab_scales, offs, w1, cap, w4_words, w4_scales, gT):
    v = unpack_weight(tab_words, tab_scales, "e4m3")[:, unstriped(offs)]
    g = f64(gT)[:, unstriped(offs)]
    a = mxq(f64(w1), 0, "e4m3").T @ v
    h = f64(cap)[:, None] * np.tanh(a)
    w4 = unpack_weight(w4_words, w4_scales, "e2m1")
    y = w4.T @ mxq(h, 0, "e4m3")
    price = np.exp(y)
    return np.maximum(price - g, 0.0)

@@ -1,0 +1,264 @@
+from contextlib import ExitStack
+
+import concourse.mybir as mybir
+
+K, T, S, R, N = 1024, 2048, 1024, 1024, 512
+FLOPS = 2 * K * R * S + 2 * R * N * S
+
+F32 = mybir.dt.float32
+BF16 = mybir.dt.bfloat16
+I32 = mybir.dt.int32
+U32 = mybir.dt.uint32
+U16 = mybir.dt.uint16
+U8 = mybir.dt.uint8
+FP8X4 = mybir.dt.float8_e4m3fn_x4
+FP4X4 = mybir.dt.float4_e2m1fn_x4
+ACT = mybir.ActivationFunctionType
+ALU = mybir.AluOpType
+
+P = 128
+PACK = 4
+PASS = P * PACK
+JB = 128
+JC = 512
+LIST_ROWS = 16
+EARLY = 6
+V_SHARE = (0,0,0,0)
+CAPW = 256
+
+
+def tile_list_floating_strike_payoffs_kernel(tc, tab_words, tab_scales, offs, w1, cap, w4_words, w4_scales, gT, out):
+    nc = tc.nc
+    with ExitStack() as ctx:
+        keep = ctx.enter_context(tc.tile_pool(name="keep", bufs=1))
+        ring = ctx.enter_context(tc.tile_pool(name="ring", bufs=10))
+        ps1 = ctx.enter_context(tc.psum_pool(name="ps1", bufs=EARLY))
+        ps2 = ctx.enter_context(tc.psum_pool(name="ps2", bufs=8 - EARLY))
+
+        offsets = keep.tile([P, S // LIST_ROWS], U16, name="offsets")
+        nc.sync.dma_start(offsets[:], offs)
+
+        def picks(j0, n):
+            return offsets[:, j0 // LIST_ROWS : (j0 + n) // LIST_ROWS]
+
+        tab_plane = keep.tile([P, T], U8, name="tab_plane", align_bytes=64)
+        w4_plane = keep.tile([P, 2 * N], U8, name="w4_plane", align_bytes=64)
+        nc.gpsimd.memset(tab_plane[:].bitcast(I32), 0)
+        nc.vector.memset(w4_plane[:].bitcast(I32), 0)
+
+        def load_tab_plane():
+            for q in range(4):
+                nc.sync.dma_start(
+                    out=tab_plane[32 * q : 32 * q + 8, :].bitcast(I32),
+                    in_=tab_scales[:, 4 * q : 4 * q + 4, :].bitcast(I32),
+                )
+
+        tab = [keep.tile([P, T], I32, name="tab%d" % a, align_bytes=64) for a in range(2)]
+        pieces = {(0, 0): 1, (1, 0): 2, (0, 1): 2, (1, 1): 2}
+        raw = {
+            (a, b, u): keep.tile([P, PACK, PASS // n], F32, name="raw%d%d%d" % (a, b, u), align_bytes=64)
+            for (a, b), n in pieces.items() for u in range(n)
+        }
+        strikes = [keep.tile([P, T], F32, name="strikes%d" % n, align_bytes=64) for n in range(N // P)]
+        caps = keep.tile([P, 2, PACK], F32, name="caps")
+        w4_codes = keep.tile([P, 2, 2 * N], U8, name="w4_codes", align_bytes=64)
+
+        def load_tab(a):
+            nc.sync.dma_start(out=tab[a][:], in_=tab_words[a].rearrange("p t i -> p (t i)").bitcast(I32))
+
+        def load_w1(a, b):
+            width = PASS // pieces[a, b]
+            for u in range(pieces[a, b]):
+                c0 = b * PASS + u * width
+                nc.sync.dma_start(
+                    out=raw[a, b, u][:],
+                    in_=w1[a * PASS : (a + 1) * PASS, c0 : c0 + width].rearrange("(p i) c -> p i c", i=PACK),
+                )
+
+        def load_caps():
+            nc.sync.dma_start(out=caps[:], in_=cap.rearrange("(b p t) -> p b t", b=2, t=PACK))
+
+        def load_w4():
+            nc.sync.dma_start(out=w4_codes[:].bitcast(I32), in_=w4_words.rearrange("a p c -> p a c").bitcast(I32))
+
+        def load_w4_plane():
+            for q in range(4):
+                nc.sync.dma_start(
+                    out=w4_plane[32 * q : 32 * q + 4, :].rearrange("p (a c) -> p a c", a=2).bitcast(I32),
+                    in_=w4_scales[:, 4 * q : 4 * q + 4, :].rearrange("a r c -> r a c").bitcast(I32),
+                )
+
+        def load_strikes(n):
+            nc.sync.dma_start(out=strikes[n][:], in_=gT[n * P : (n + 1) * P, :])
+
+        load_tab(0)
+        load_tab_plane()
+        load_w1(0, 0)
+        load_tab(1)
+        load_w1(1, 0)
+        load_caps()
+        load_w1(0, 1)
+        load_w1(1, 1)
+        load_w4()
+        load_w4_plane()
+        for n in range(4):
+            load_strikes(n)
+
+        v_codes = [keep.tile([P, S], U32, name="v_codes%d" % a, align_bytes=64) for a in range(2)]
+        v_plane = keep.tile([P, S], U8, name="v_plane", align_bytes=64)
+        w1_bf = {k: keep.tile([P, PASS * PACK], BF16, name="w1_bf%d%d" % k, align_bytes=64) for k in pieces}
+        w1_codes = {k: keep.tile([P, PASS], U32, name="w1_codes%d%d" % k, align_bytes=64) for k in pieces}
+        w1_plane = {k: keep.tile([P, PASS], U8, name="w1_plane%d%d" % k, align_bytes=64) for k in pieces}
+
+        def gather_words(a, j0, n):
+            nc.vector.tensor_copy(v_codes[a][:, j0 : j0 + n], tab[a][:].bitcast(U32).indirect(picks(j0, n)))
+
+        def round_w1(a, b, m0, m1, on_vector):
+            rows = P // pieces[a, b]
+            u = m0 // rows
+            dst = w1_bf[a, b][:].rearrange("p (t m i) -> p m t i", t=PACK, i=PACK)[:, m0:m1]
+            src = raw[a, b, u][:].rearrange("p i (m t) -> p m t i", t=PACK)[:, m0 - u * rows : m1 - u * rows]
+            if on_vector:
+                nc.vector.tensor_copy(dst, src)
+            else:
+                nc.scalar.activation(dst, src, ACT.Copy)
+
+        def quantise_w1(a, b):
+            nc.vector.quantize_mx(out=w1_codes[a, b][:].bitcast(FP8X4), scales=w1_plane[a, b][:], in_=w1_bf[a, b][:])
+
+        def first_pass(bank, a, b, jb):
+            cols = slice(jb * JB, (jb + 1) * JB)
+            for t in range(PACK):
+                nc.tensor.matmul_mx(
+                    out=bank[:, t * JB : (t + 1) * JB],
+                    lhsT=w1_codes[a, b][:, t * P : (t + 1) * P].bitcast(FP8X4),
+                    lhsT_scale=w1_plane[a, b][:, t * P : (t + 1) * P],
+                    rhs=v_codes[a][:, cols].bitcast(FP8X4),
+                    rhs_scale=v_plane[4 * a :, cols],
+                    start=(a == 0 and t == 0),
+                    stop=(a == 1 and t == PACK - 1),
+                )
+
+        halves = [(b, jc) for b in range(2) for jc in range(S // JC)]
+        th = {k: keep.tile([P, JC * PACK], F32, name="th%d%d" % k, align_bytes=64) for k in halves}
+        h_bf = {k: keep.tile([P, JC * PACK], BF16, name="h_bf%d%d" % k, align_bytes=64) for k in halves}
+        h_codes = {k: keep.tile([P, JC], U32, name="h_codes%d%d" % k, align_bytes=64) for k in halves}
+        h_plane = {k: keep.tile([P, JC], U8, name="h_plane%d%d" % k, align_bytes=64) for k in halves}
+
+        def saturate_bank(bank, b, jb):
+            jc, part = divmod(jb, JC // JB)
+            dst = th[b, jc][:, part * JB * PACK : (part + 1) * JB * PACK]
+            nc.scalar.activation(
+                dst.rearrange("p (j t) -> p j t", t=PACK), bank[:].rearrange("p (t j) -> p j t", t=PACK), ACT.Tanh
+            )
+
+        def cap_paths(b, j0, n):
+            jc, off = divmod(j0, JC)
+            cols = slice(off * PACK, (off + n) * PACK)
+            nc.vector.tensor_tensor(
+                h_bf[b, jc][:, cols].rearrange("p (j t) -> p j t", t=PACK),
+                th[b, jc][:, cols].rearrange("p (j t) -> p j t", t=PACK),
+                caps[:, b : b + 1, :].to_broadcast([P, n, PACK]),
+                ALU.mult,
+            )
+
+        def quantise_h(b, jc):
+            nc.vector.quantize_mx(out=h_codes[b, jc][:].bitcast(FP8X4), scales=h_plane[b, jc][:], in_=h_bf[b, jc][:])
+
+        prices = {}
+
+        def second_stage(jc, n):
+            bank = ps2.tile([P, JC], F32, name="bank2")
+            for b in range(2):
+                nc.tensor.matmul_mx(
+                    out=bank[:],
+                    lhsT=w4_codes[:, b, 2 * n * P : 2 * (n + 1) * P].bitcast(FP4X4),
+                    lhsT_scale=w4_plane[:, b * N + n * P : b * N + (n + 1) * P],
+                    rhs=h_codes[b, jc][:].bitcast(FP8X4),
+                    rhs_scale=h_plane[b, jc][:],
+                    start=(b == 0),
+                    stop=(b == 1),
+                )
+            prices[jc, n] = keep.tile([P, JC], F32, name="price%d%d" % (jc, n), align_bytes=64)
+            nc.scalar.activation(prices[jc, n][:], bank[:], ACT.Exp)
+
+        def payoff(j0, n, width):
+            jc, off = divmod(j0, JC)
+            gap = ring.tile([P, width], F32, name="gap", align_bytes=64)
+            nc.vector.tensor_tensor(gap[:], strikes[n][:].indirect(picks(j0, width)), prices[jc, n][:, off : off + width], ALU.subtract)
+            pay = ring.tile([P, width], F32, name="pay", align_bytes=64)
+            nc.scalar.activation(pay[:], gap[:], ACT.Relu, scale=-1.0)
+            nc.sync.dma_start(out=out[n * P : (n + 1) * P, j0 : j0 + width], in_=pay[:])
+
+        banks = {}
+
+        def open_bank(b, jb):
+            banks[b, jb] = ps1.tile([P, PACK * JB], F32, name="bank1")
+            first_pass(banks[b, jb], 0, b, jb)
+
+        def close_bank(b, jb):
+            if (b, jb) not in banks:
+                open_bank(b, jb)
+            first_pass(banks[b, jb], 1, b, jb)
+            saturate_bank(banks[b, jb], b, jb)
+
+        def gather_plane():
+            nc.vector.tensor_copy(v_plane[:], tab_plane[:].indirect(offsets[:]))
+
+        gather_words(0, 0, S)
+        gather_plane()
+        round_w1(0, 0, 0, 128, False)
+        quantise_w1(0, 0)
+        for jb in range(EARLY):
+            open_bank(0, jb)
+        gather_words(1, 0, 512)
+        gather_words(1, 512, 512)
+        round_w1(1, 0, 0, 64, False)
+        round_w1(1, 0, 64, 88, False)
+        round_w1(1, 0, 88, 128, True)
+        quantise_w1(1, 0)
+        round_w1(0, 1, 0, 64, True)
+        round_w1(0, 1, 64, 128, True)
+        quantise_w1(0, 1)
+        close_bank(0, 0)
+        close_bank(0, 1)
+        cap_paths(0, 0, 256)
+        round_w1(1, 1, 0, 64, False)
+        close_bank(0, 2)
+        close_bank(0, 3)
+        cap_paths(0, 256, 256)
+        round_w1(1, 1, 64, 128, False)
+        quantise_w1(1, 1)
+        quantise_h(0, 0)
+        close_bank(0, 4)
+        close_bank(0, 5)
+        cap_paths(0, 512, 256)
+        close_bank(0, 6)
+        close_bank(0, 7)
+        cap_paths(0, 768, 256)
+        quantise_h(0, 1)
+        close_bank(1, 0)
+        close_bank(1, 1)
+        cap_paths(1, 0, 256)
+        close_bank(1, 2)
+        close_bank(1, 3)
+        cap_paths(1, 256, 256)
+        quantise_h(1, 0)
+        for n in range(4):
+            second_stage(0, n)
+        close_bank(1, 4)
+        close_bank(1, 5)
+        cap_paths(1, 512, 256)
+        close_bank(1, 6)
+        close_bank(1, 7)
+        cap_paths(1, 768, 256)
+        quantise_h(1, 1)
+        for n in range(4):
+            second_stage(1, n)
+        for n in range(4):
+            payoff(0, n, 512)
+        for n in range(3):
+            payoff(512, n, 512)
+        payoff(512, 3, 256)
+        payoff(768, 3, 128)
+        payoff(896, 3, 128)

@@ -19,7 +19,7 @@ ALU = mybir.AluOpType
 P = 128
 PACK = 4
 PASS = P * PACK
-JB = 128
+JB = 256
 JC = 512
 LIST_ROWS = 16
 EARLY = 6
@@ -31,7 +31,7 @@ def tile_list_floating_strike_payoffs_kernel(tc, tab_words, tab_scales, offs, w1
     nc = tc.nc
     with ExitStack() as ctx:
         keep = ctx.enter_context(tc.tile_pool(name="keep", bufs=1))
-        ring = ctx.enter_context(tc.tile_pool(name="ring", bufs=10))
+        ring = ctx.enter_context(tc.tile_pool(name="ring", bufs=11))
         ps1 = ctx.enter_context(tc.psum_pool(name="ps1", bufs=EARLY))
         ps2 = ctx.enter_context(tc.psum_pool(name="ps2", bufs=8 - EARLY))
 
@@ -42,6 +42,7 @@ def tile_list_floating_strike_payoffs_kernel(tc, tab_words, tab_scales, offs, w1
             return offsets[:, j0 // LIST_ROWS : (j0 + n) // LIST_ROWS]
 
         tab_plane = keep.tile([P, T], U8, name="tab_plane", align_bytes=64)
+        tab_rows = keep.tile([P, T // 4], I32, name="tab_rows", align_bytes=64)
         w4_plane = keep.tile([P, 2 * N], U8, name="w4_plane", align_bytes=64)
         nc.gpsimd.memset(tab_plane[:].bitcast(I32), 0)
         nc.vector.memset(w4_plane[:].bitcast(I32), 0)
@@ -49,15 +50,15 @@ def tile_list_floating_strike_payoffs_kernel(tc, tab_words, tab_scales, offs, w1
         def load_tab_plane():
             for q in range(4):
                 nc.sync.dma_start(
-                    out=tab_plane[32 * q : 32 * q + 8, :].bitcast(I32),
+                    out=tab_rows[32 * q : 32 * q + 8, :],
                     in_=tab_scales[:, 4 * q : 4 * q + 4, :].bitcast(I32),
                 )
 
         tab = [keep.tile([P, T], I32, name="tab%d" % a, align_bytes=64) for a in range(2)]
-        pieces = {(0, 0): 1, (1, 0): 2, (0, 1): 2, (1, 1): 2}
+        pieces = {(0, 0): (0, 32, 128), (1, 0): (0, 128), (0, 1): (0, 64, 128), (1, 1): (0, 128)}
         raw = {
-            (a, b, u): keep.tile([P, PACK, PASS // n], F32, name="raw%d%d%d" % (a, b, u), align_bytes=64)
-            for (a, b), n in pieces.items() for u in range(n)
+            (a, b, m0): keep.tile([P, PACK, PACK * (m1 - m0)], F32, name="raw%d%d_%d" % (a, b, m0), align_bytes=64)
+            for (a, b), cuts in pieces.items() for m0, m1 in zip(cuts, cuts[1:])
         }
         strikes = [keep.tile([P, T], F32, name="strikes%d" % n, align_bytes=64) for n in range(N // P)]
         caps = keep.tile([P, 2, PACK], F32, name="caps")
@@ -66,14 +67,13 @@ def tile_list_floating_strike_payoffs_kernel(tc, tab_words, tab_scales, offs, w1
         def load_tab(a):
             nc.sync.dma_start(out=tab[a][:], in_=tab_words[a].rearrange("p t i -> p (t i)").bitcast(I32))
 
-        def load_w1(a, b):
-            width = PASS // pieces[a, b]
-            for u in range(pieces[a, b]):
-                c0 = b * PASS + u * width
-                nc.sync.dma_start(
-                    out=raw[a, b, u][:],
-                    in_=w1[a * PASS : (a + 1) * PASS, c0 : c0 + width].rearrange("(p i) c -> p i c", i=PACK),
-                )
+        def load_w1(a, b, m0=0):
+            width = raw[a, b, m0].shape[2]
+            c0 = b * PASS + PACK * m0
+            nc.sync.dma_start(
+                out=raw[a, b, m0][:],
+                in_=w1[a * PASS : (a + 1) * PASS, c0 : c0 + width].rearrange("(p i) c -> p i c", i=PACK),
+            )
 
         def load_caps():
             nc.sync.dma_start(out=caps[:], in_=cap.rearrange("(b p t) -> p b t", b=2, t=PACK))
@@ -91,14 +91,16 @@ def tile_list_floating_strike_payoffs_kernel(tc, tab_words, tab_scales, offs, w1
         def load_strikes(n):
             nc.sync.dma_start(out=strikes[n][:], in_=gT[n * P : (n + 1) * P, :])
 
-        load_tab(0)
         load_tab_plane()
-        load_w1(0, 0)
+        load_w1(0, 0, 0)
+        load_tab(0)
+        load_w1(0, 0, 32)
         load_tab(1)
-        load_w1(1, 0)
+        load_w1(1, 0, 0)
+        load_w1(0, 1, 0)
+        load_w1(0, 1, 64)
         load_caps()
-        load_w1(0, 1)
-        load_w1(1, 1)
+        load_w1(1, 1, 0)
         load_w4()
         load_w4_plane()
         for n in range(4):
@@ -114,29 +116,35 @@ def tile_list_floating_strike_payoffs_kernel(tc, tab_words, tab_scales, offs, w1
             nc.vector.tensor_copy(v_codes[a][:, j0 : j0 + n], tab[a][:].bitcast(U32).indirect(picks(j0, n)))
 
         def round_w1(a, b, m0, m1, on_vector):
-            rows = P // pieces[a, b]
-            u = m0 // rows
-            dst = w1_bf[a, b][:].rearrange("p (t m i) -> p m t i", t=PACK, i=PACK)[:, m0:m1]
-            src = raw[a, b, u][:].rearrange("p i (m t) -> p m t i", t=PACK)[:, m0 - u * rows : m1 - u * rows]
+            u = max(c for c in pieces[a, b] if c <= m0)
+            dst = w1_bf[a, b][:].rearrange("p (t m i) -> p m i t", t=PACK, i=PACK)[:, m0:m1]
+            src = raw[a, b, u][:].rearrange("p i (m t) -> p m i t", t=PACK)[:, m0 - u : m1 - u]
             if on_vector:
                 nc.vector.tensor_copy(dst, src)
             else:
                 nc.scalar.activation(dst, src, ACT.Copy)
 
-        def quantise_w1(a, b):
-            nc.vector.quantize_mx(out=w1_codes[a, b][:].bitcast(FP8X4), scales=w1_plane[a, b][:], in_=w1_bf[a, b][:])
+        def quantise_w1(a, b, half=None):
+            c0, c1 = (0, PASS) if half is None else (half * PASS // 2, (half + 1) * PASS // 2)
+            nc.vector.quantize_mx(
+                out=w1_codes[a, b][:, c0:c1].bitcast(FP8X4),
+                scales=w1_plane[a, b][:, c0:c1],
+                in_=w1_bf[a, b][:, PACK * c0 : PACK * c1],
+            )
 
-        def first_pass(bank, a, b, jb):
+        def first_pass(bank, a, b, q):
+            jb, u = divmod(q, 2)
             cols = slice(jb * JB, (jb + 1) * JB)
-            for t in range(PACK):
+            for e in range(2):
+                t = 2 * u + e
                 nc.tensor.matmul_mx(
-                    out=bank[:, t * JB : (t + 1) * JB],
+                    out=bank[:, e * JB : (e + 1) * JB],
                     lhsT=w1_codes[a, b][:, t * P : (t + 1) * P].bitcast(FP8X4),
                     lhsT_scale=w1_plane[a, b][:, t * P : (t + 1) * P],
                     rhs=v_codes[a][:, cols].bitcast(FP8X4),
                     rhs_scale=v_plane[4 * a :, cols],
-                    start=(a == 0 and t == 0),
-                    stop=(a == 1 and t == PACK - 1),
+                    start=(a == 0 and e == 0),
+                    stop=(a == 1 and e == 1),
                 )
 
         halves = [(b, jc) for b in range(2) for jc in range(S // JC)]
@@ -145,20 +153,20 @@ def tile_list_floating_strike_payoffs_kernel(tc, tab_words, tab_scales, offs, w1
         h_codes = {k: keep.tile([P, JC], U32, name="h_codes%d%d" % k, align_bytes=64) for k in halves}
         h_plane = {k: keep.tile([P, JC], U8, name="h_plane%d%d" % k, align_bytes=64) for k in halves}
 
-        def saturate_bank(bank, b, jb):
-            jc, part = divmod(jb, JC // JB)
-            dst = th[b, jc][:, part * JB * PACK : (part + 1) * JB * PACK]
+        def saturate_bank(bank, b, q):
+            jc, part = divmod(q, 4)
+            dst = th[b, jc][:, part * 2 * JB : (part + 1) * 2 * JB]
             nc.scalar.activation(
-                dst.rearrange("p (j t) -> p j t", t=PACK), bank[:].rearrange("p (t j) -> p j t", t=PACK), ACT.Tanh
+                dst.rearrange("p (j e) -> p j e", e=2), bank[:].rearrange("p (e j) -> p j e", e=2), ACT.Tanh
             )
 
         def cap_paths(b, j0, n):
             jc, off = divmod(j0, JC)
             cols = slice(off * PACK, (off + n) * PACK)
             nc.vector.tensor_tensor(
-                h_bf[b, jc][:, cols].rearrange("p (j t) -> p j t", t=PACK),
-                th[b, jc][:, cols].rearrange("p (j t) -> p j t", t=PACK),
-                caps[:, b : b + 1, :].to_broadcast([P, n, PACK]),
+                h_bf[b, jc][:, cols].rearrange("p (j u e) -> p j u e", u=2, e=2),
+                th[b, jc][:, cols].rearrange("p (u j e) -> p j u e", u=2, e=2),
+                caps[:, b : b + 1, :].rearrange("p o (u e) -> p o u e", u=2).to_broadcast([P, n, 2, 2]),
                 ALU.mult,
             )
 
@@ -184,7 +192,7 @@ def tile_list_floating_strike_payoffs_kernel(tc, tab_words, tab_scales, offs, w1
 
         def payoff(j0, n, width):
             jc, off = divmod(j0, JC)
-            gap = ring.tile([P, width], F32, name="gap", align_bytes=64)
+            gap = ring.tile([P, width], F32, name="gap", align_bytes=64, bufs=8)
             nc.vector.tensor_tensor(gap[:], strikes[n][:].indirect(picks(j0, width)), prices[jc, n][:, off : off + width], ALU.subtract)
             pay = ring.tile([P, width], F32, name="pay", align_bytes=64)
             nc.scalar.activation(pay[:], gap[:], ACT.Relu, scale=-1.0)
@@ -193,7 +201,7 @@ def tile_list_floating_strike_payoffs_kernel(tc, tab_words, tab_scales, offs, w1
         banks = {}
 
         def open_bank(b, jb):
-            banks[b, jb] = ps1.tile([P, PACK * JB], F32, name="bank1")
+            banks[b, jb] = ps1.tile([P, 2 * JB], F32, name="bank1")
             first_pass(banks[b, jb], 0, b, jb)
 
         def close_bank(b, jb):
@@ -203,62 +211,68 @@ def tile_list_floating_strike_payoffs_kernel(tc, tab_words, tab_scales, offs, w1
             saturate_bank(banks[b, jb], b, jb)
 
         def gather_plane():
+            for q in range(4):
+                nc.vector.tensor_copy(tab_plane[32 * q : 32 * q + 8, :].bitcast(I32), tab_rows[32 * q : 32 * q + 8, :])
             nc.vector.tensor_copy(v_plane[:], tab_plane[:].indirect(offsets[:]))
 
-        gather_words(0, 0, S)
         gather_plane()
-        round_w1(0, 0, 0, 128, False)
+        gather_words(0, 0, S)
+        round_w1(0, 0, 0, 32, False)
+        round_w1(0, 0, 32, 96, False)
+        round_w1(0, 0, 96, 128, True)
         quantise_w1(0, 0)
         for jb in range(EARLY):
             open_bank(0, jb)
-        gather_words(1, 0, 512)
-        gather_words(1, 512, 512)
-        round_w1(1, 0, 0, 64, False)
-        round_w1(1, 0, 64, 88, False)
-        round_w1(1, 0, 88, 128, True)
-        quantise_w1(1, 0)
-        round_w1(0, 1, 0, 64, True)
+        gather_words(1, 0, S)
+        round_w1(1, 0, 0, 44, False)
+        round_w1(1, 0, 44, 128, True)
+        quantise_w1(1, 0, 0)
+        quantise_w1(1, 0, 1)
+        round_w1(0, 1, 0, 64, False)
         round_w1(0, 1, 64, 128, True)
-        quantise_w1(0, 1)
         close_bank(0, 0)
         close_bank(0, 1)
         cap_paths(0, 0, 256)
-        round_w1(1, 1, 0, 64, False)
+        quantise_w1(0, 1)
         close_bank(0, 2)
         close_bank(0, 3)
+        round_w1(1, 1, 0, 64, False)
+        round_w1(1, 1, 64, 128, True)
         cap_paths(0, 256, 256)
-        round_w1(1, 1, 64, 128, False)
-        quantise_w1(1, 1)
-        quantise_h(0, 0)
         close_bank(0, 4)
         close_bank(0, 5)
         cap_paths(0, 512, 256)
+        quantise_w1(1, 1)
+        quantise_h(0, 0)
         close_bank(0, 6)
         close_bank(0, 7)
         cap_paths(0, 768, 256)
-        quantise_h(0, 1)
         close_bank(1, 0)
         close_bank(1, 1)
         cap_paths(1, 0, 256)
+        quantise_h(0, 1)
         close_bank(1, 2)
         close_bank(1, 3)
         cap_paths(1, 256, 256)
-        quantise_h(1, 0)
-        for n in range(4):
-            second_stage(0, n)
         close_bank(1, 4)
         close_bank(1, 5)
         cap_paths(1, 512, 256)
+        quantise_h(1, 0)
         close_bank(1, 6)
         close_bank(1, 7)
+        for n in range(4):
+            second_stage(0, n)
         cap_paths(1, 768, 256)
+        payoff(0, 0, 512)
         quantise_h(1, 1)
         for n in range(4):
             second_stage(1, n)
-        for n in range(4):
+        for n in range(1, 4):
             payoff(0, n, 512)
-        for n in range(3):
+        for n in range(2):
             payoff(512, n, 512)
+        payoff(512, 2, 256)
+        payoff(768, 2, 256)
         payoff(512, 3, 256)
         payoff(768, 3, 128)
         payoff(896, 3, 128)

@@ -117,12 +117,17 @@ def tile_list_floating_strike_payoffs_kernel(tc, tab_words, tab_scales, offs, w1
 
         def round_w1(a, b, m0, m1, on_vector):
             u = max(c for c in pieces[a, b] if c <= m0)
-            dst = w1_bf[a, b][:].rearrange("p (t m i) -> p m i t", t=PACK, i=PACK)[:, m0:m1]
-            src = raw[a, b, u][:].rearrange("p i (m t) -> p m i t", t=PACK)[:, m0 - u : m1 - u]
+            if (a, b, m0) == (0, 0, 0):
+                dst = w1_bf[a, b][:].rearrange("p (t m i) -> p m i t", t=PACK, i=PACK)[:, m0:m1]
+                src = raw[a, b, u][:].rearrange("p i (m t) -> p m i t", t=PACK)[:, m0 - u : m1 - u]
+                nc.scalar.activation(dst, src, ACT.Copy)
+                return
+            dst = w1_bf[a, b][:].rearrange("p (t m g e) -> p m g t e", t=PACK, g=2, e=2)[:, m0:m1]
+            src = raw[a, b, u][:].rearrange("p (g e) (m t) -> p m g t e", g=2, t=PACK)[:, m0 - u : m1 - u]
             if on_vector:
                 nc.vector.tensor_copy(dst, src)
             else:
-                nc.scalar.activation(dst, src, ACT.Copy)
+                nc.scalar.copy(dst, src)
 
         def quantise_w1(a, b, half=None):
             c0, c1 = (0, PASS) if half is None else (half * PASS // 2, (half + 1) * PASS // 2)

@@ -1,6 +1,7 @@
 from contextlib import ExitStack
 
 import concourse.mybir as mybir
+from concourse.masks import make_identity
 
 K, T, S, R, N = 1024, 2048, 1024, 1024, 512
 FLOPS = 2 * K * R * S + 2 * R * N * S
@@ -22,18 +23,17 @@ PASS = P * PACK
 JB = 256
 JC = 512
 LIST_ROWS = 16
-EARLY = 6
-V_SHARE = (0,0,0,0)
-CAPW = 256
+W1_CUTS = {(0, 0): (0, 32, 128), (1, 0): (0, 48, 96, 128), (0, 1): (0, 64, 128), (1, 1): (0, 64, 128)}
 
 
 def tile_list_floating_strike_payoffs_kernel(tc, tab_words, tab_scales, offs, w1, cap, w4_words, w4_scales, gT, out):
     nc = tc.nc
     with ExitStack() as ctx:
         keep = ctx.enter_context(tc.tile_pool(name="keep", bufs=1))
-        ring = ctx.enter_context(tc.tile_pool(name="ring", bufs=11))
-        ps1 = ctx.enter_context(tc.psum_pool(name="ps1", bufs=EARLY))
-        ps2 = ctx.enter_context(tc.psum_pool(name="ps2", bufs=8 - EARLY))
+        ring = ctx.enter_context(tc.tile_pool(name="ring", bufs=10))
+        ps1 = ctx.enter_context(tc.psum_pool(name="ps1", bufs=7))
+        ps2 = ps1
+        ps0 = ctx.enter_context(tc.psum_pool(name="ps0", bufs=1))
 
         offsets = keep.tile([P, S // LIST_ROWS], U16, name="offsets")
         nc.sync.dma_start(offsets[:], offs)
@@ -55,14 +55,25 @@ def tile_list_floating_strike_payoffs_kernel(tc, tab_words, tab_scales, offs, w1
                 )
 
         tab = [keep.tile([P, T], I32, name="tab%d" % a, align_bytes=64) for a in range(2)]
-        pieces = {(0, 0): (0, 32, 128), (1, 0): (0, 128), (0, 1): (0, 64, 128), (1, 1): (0, 128)}
         raw = {
             (a, b, m0): keep.tile([P, PACK, PACK * (m1 - m0)], F32, name="raw%d%d_%d" % (a, b, m0), align_bytes=64)
-            for (a, b), cuts in pieces.items() for m0, m1 in zip(cuts, cuts[1:])
+            for (a, b), cuts in W1_CUTS.items() for m0, m1 in zip(cuts, cuts[1:])
         }
         strikes = [keep.tile([P, T], F32, name="strikes%d" % n, align_bytes=64) for n in range(N // P)]
         caps = keep.tile([P, 2, PACK], F32, name="caps")
         w4_codes = keep.tile([P, 2, 2 * N], U8, name="w4_codes", align_bytes=64)
+        cap_rows = keep.tile([P, PASS], F32, name="cap_rows", align_bytes=64)
+        identity = keep.tile([P, P], F32, name="identity", align_bytes=64)
+        caps_ps = ps0.tile([P, PACK, P], F32, name="caps_ps")
+        nc.gpsimd.memset(cap_rows[:], 0.0)
+        make_identity(nc, identity[:])
+
+        def load_cap_rows():
+            nc.sync.dma_start(out=cap_rows[0:2, :], in_=cap.rearrange("(b c) -> b c", b=2))
+
+        def caps_to_psum():
+            for t in range(PACK):
+                nc.tensor.transpose(caps_ps[:, t, :], cap_rows[:, t:PASS:PACK], identity[:])
 
         def load_tab(a):
             nc.sync.dma_start(out=tab[a][:], in_=tab_words[a].rearrange("p t i -> p (t i)").bitcast(I32))
@@ -96,11 +107,13 @@ def tile_list_floating_strike_payoffs_kernel(tc, tab_words, tab_scales, offs, w1
         load_tab(0)
         load_w1(0, 0, 32)
         load_tab(1)
-        load_w1(1, 0, 0)
-        load_w1(0, 1, 0)
-        load_w1(0, 1, 64)
+        load_cap_rows()
+        for m0 in W1_CUTS[1, 0][:-1]:
+            load_w1(1, 0, m0)
         load_caps()
-        load_w1(1, 1, 0)
+        for a in range(2):
+            for m0 in W1_CUTS[a, 1][:-1]:
+                load_w1(a, 1, m0)
         load_w4()
         load_w4_plane()
         for n in range(4):
@@ -108,28 +121,31 @@ def tile_list_floating_strike_payoffs_kernel(tc, tab_words, tab_scales, offs, w1
 
         v_codes = [keep.tile([P, S], U32, name="v_codes%d" % a, align_bytes=64) for a in range(2)]
         v_plane = keep.tile([P, S], U8, name="v_plane", align_bytes=64)
-        w1_bf = {k: keep.tile([P, PASS * PACK], BF16, name="w1_bf%d%d" % k, align_bytes=64) for k in pieces}
-        w1_codes = {k: keep.tile([P, PASS], U32, name="w1_codes%d%d" % k, align_bytes=64) for k in pieces}
-        w1_plane = {k: keep.tile([P, PASS], U8, name="w1_plane%d%d" % k, align_bytes=64) for k in pieces}
+        w1_bf = {}
+        w1_codes = {}
+        bf_names = {(0, 1): "w1_bf10"}
+        code_names = {(0, 1): "th01", (1, 1): "th02"}
+        w1_plane = {k: keep.tile([P, PASS], U8, name="w1_plane%d%d" % k, align_bytes=64) for k in W1_CUTS}
 
         def gather_words(a, j0, n):
             nc.vector.tensor_copy(v_codes[a][:, j0 : j0 + n], tab[a][:].bitcast(U32).indirect(picks(j0, n)))
 
-        def round_w1(a, b, m0, m1, on_vector):
-            u = max(c for c in pieces[a, b] if c <= m0)
-            if (a, b, m0) == (0, 0, 0):
-                dst = w1_bf[a, b][:].rearrange("p (t m i) -> p m i t", t=PACK, i=PACK)[:, m0:m1]
-                src = raw[a, b, u][:].rearrange("p i (m t) -> p m i t", t=PACK)[:, m0 - u : m1 - u]
+        def round_w1(a, b, m0, m1, how):
+            if (a, b) not in w1_bf:
+                w1_bf[a, b] = keep.tile([P, PASS * PACK], BF16, name=bf_names.get((a, b), "w1_bf%d%d" % (a, b)), align_bytes=64)
+            u = max(c for c in W1_CUTS[a, b] if c <= m0)
+            dst = w1_bf[a, b][:].rearrange("p (t m i) -> p m i t", t=PACK, i=PACK)[:, m0:m1]
+            src = raw[a, b, u][:].rearrange("p i (m t) -> p m i t", t=PACK)[:, m0 - u : m1 - u]
+            if how == "S":
                 nc.scalar.activation(dst, src, ACT.Copy)
-                return
-            dst = w1_bf[a, b][:].rearrange("p (t m g e) -> p m g t e", t=PACK, g=2, e=2)[:, m0:m1]
-            src = raw[a, b, u][:].rearrange("p (g e) (m t) -> p m g t e", g=2, t=PACK)[:, m0 - u : m1 - u]
-            if on_vector:
+            elif how == "V":
                 nc.vector.tensor_copy(dst, src)
             else:
-                nc.scalar.copy(dst, src)
+                nc.gpsimd.tensor_scalar(dst.rearrange("p m i t -> p m t i"), src.rearrange("p m i t -> p m t i"), 1.0, 0.0, ALU.mult, ALU.add)
 
         def quantise_w1(a, b, half=None):
+            if (a, b) not in w1_codes:
+                w1_codes[a, b] = keep.tile([P, PASS], U32, name=code_names.get((a, b), "w1_codes%d%d" % (a, b)), align_bytes=64)
             c0, c1 = (0, PASS) if half is None else (half * PASS // 2, (half + 1) * PASS // 2)
             nc.vector.quantize_mx(
                 out=w1_codes[a, b][:, c0:c1].bitcast(FP8X4),
@@ -153,35 +169,40 @@ def tile_list_floating_strike_payoffs_kernel(tc, tab_words, tab_scales, offs, w1
                 )
 
         halves = [(b, jc) for b in range(2) for jc in range(S // JC)]
-        th = {k: keep.tile([P, JC * PACK], F32, name="th%d%d" % k, align_bytes=64) for k in halves}
-        h_bf = {k: keep.tile([P, JC * PACK], BF16, name="h_bf%d%d" % k, align_bytes=64) for k in halves}
+        th = {(b, jb): keep.tile([P, 2, JB, 2], F32, name="th%d%d" % (b, jb), align_bytes=64) for b in range(2) for jb in range(S // JB)}
+        h_bf = {}
+        reused = {(0, 2): "w1_bf10", (0, 3): "w1_bf11"}
         h_codes = {k: keep.tile([P, JC], U32, name="h_codes%d%d" % k, align_bytes=64) for k in halves}
         h_plane = {k: keep.tile([P, JC], U8, name="h_plane%d%d" % k, align_bytes=64) for k in halves}
 
         def saturate_bank(bank, b, q):
-            jc, part = divmod(q, 4)
-            dst = th[b, jc][:, part * 2 * JB : (part + 1) * 2 * JB]
+            jb, u = divmod(q, 2)
             nc.scalar.activation(
-                dst.rearrange("p (j e) -> p j e", e=2), bank[:].rearrange("p (e j) -> p j e", e=2), ACT.Tanh
+                th[b, jb][:, u, :, :], bank[:].rearrange("p (e j) -> p j e", e=2), ACT.Tanh
             )
 
-        def cap_paths(b, j0, n):
-            jc, off = divmod(j0, JC)
-            cols = slice(off * PACK, (off + n) * PACK)
-            nc.vector.tensor_tensor(
-                h_bf[b, jc][:, cols].rearrange("p (j u e) -> p j u e", u=2, e=2),
-                th[b, jc][:, cols].rearrange("p (u j e) -> p j u e", u=2, e=2),
-                caps[:, b : b + 1, :].rearrange("p o (u e) -> p o u e", u=2).to_broadcast([P, n, 2, 2]),
-                ALU.mult,
-            )
+        def cap_paths(b, j0, n, how="V"):
+            jb, inner = divmod(j0, JB)
+            if (b, jb) not in h_bf:
+                h_bf[b, jb] = keep.tile([P, JB * PACK], BF16, name=reused.get((b, jb), "h_bf%d%d" % (b, jb)), align_bytes=64)
+            dst = h_bf[b, jb][:, inner * PACK : (inner + n) * PACK].rearrange("p (j u e) -> p j u e", u=2, e=2)
+            src = th[b, jb][:, :, inner : inner + n, :].rearrange("p u j e -> p j u e")
+            in_sbuf = caps[:, b : b + 1, :].rearrange("p o (u e) -> p o u e", u=2).to_broadcast([P, n, 2, 2])
+            if how == "V":
+                in_psum = caps_ps[:, :, b : b + 1].rearrange("p (u e) o -> p o u e", u=2).to_broadcast([P, n, 2, 2])
+                nc.vector.tensor_tensor(dst, src, in_psum, ALU.mult)
+            else:
+                nc.gpsimd.tensor_tensor(dst, src, in_sbuf, ALU.mult)
 
-        def quantise_h(b, jc):
-            nc.vector.quantize_mx(out=h_codes[b, jc][:].bitcast(FP8X4), scales=h_plane[b, jc][:], in_=h_bf[b, jc][:])
+        def quantise_h(b, jb):
+            jc, part = divmod(jb, 2)
+            cols = slice(part * JB, (part + 1) * JB)
+            nc.vector.quantize_mx(out=h_codes[b, jc][:, cols].bitcast(FP8X4), scales=h_plane[b, jc][:, cols], in_=h_bf[b, jb][:])
 
         prices = {}
 
         def second_stage(jc, n):
-            bank = ps2.tile([P, JC], F32, name="bank2")
+            bank = ps2.tile([P, JC], F32, name="bank")
             for b in range(2):
                 nc.tensor.matmul_mx(
                     out=bank[:],
@@ -195,25 +216,32 @@ def tile_list_floating_strike_payoffs_kernel(tc, tab_words, tab_scales, offs, w1
             prices[jc, n] = keep.tile([P, JC], F32, name="price%d%d" % (jc, n), align_bytes=64)
             nc.scalar.activation(prices[jc, n][:], bank[:], ACT.Exp)
 
-        def payoff(j0, n, width):
+        def payoff(j0, n, width, how="S"):
             jc, off = divmod(j0, JC)
             gap = ring.tile([P, width], F32, name="gap", align_bytes=64, bufs=8)
             nc.vector.tensor_tensor(gap[:], strikes[n][:].indirect(picks(j0, width)), prices[jc, n][:, off : off + width], ALU.subtract)
             pay = ring.tile([P, width], F32, name="pay", align_bytes=64)
-            nc.scalar.activation(pay[:], gap[:], ACT.Relu, scale=-1.0)
+            if how == "S":
+                nc.scalar.activation(pay[:], gap[:], ACT.Relu, scale=-1.0)
+            else:
+                nc.vector.tensor_scalar(pay[:], gap[:], -1.0, 0.0, ALU.mult, ALU.max)
             nc.sync.dma_start(out=out[n * P : (n + 1) * P, j0 : j0 + width], in_=pay[:])
 
         banks = {}
 
-        def open_bank(b, jb):
-            banks[b, jb] = ps1.tile([P, 2 * JB], F32, name="bank1")
-            first_pass(banks[b, jb], 0, b, jb)
+        def open_bank(b, q):
+            banks[b, q] = ps1.tile([P, 2 * JB], F32, name="bank")
+            first_pass(banks[b, q], 0, b, q)
 
-        def close_bank(b, jb):
-            if (b, jb) not in banks:
-                open_bank(b, jb)
-            first_pass(banks[b, jb], 1, b, jb)
-            saturate_bank(banks[b, jb], b, jb)
+        def close_bank(b, q):
+            if (b, q) not in banks:
+                open_bank(b, q)
+            first_pass(banks[b, q], 1, b, q)
+            saturate_bank(banks[b, q], b, q)
+
+        def close_block(b, jb):
+            close_bank(b, 2 * jb)
+            close_bank(b, 2 * jb + 1)
 
         def gather_plane():
             for q in range(4):
@@ -222,56 +250,54 @@ def tile_list_floating_strike_payoffs_kernel(tc, tab_words, tab_scales, offs, w1
 
         gather_plane()
         gather_words(0, 0, S)
-        round_w1(0, 0, 0, 32, False)
-        round_w1(0, 0, 32, 96, False)
-        round_w1(0, 0, 96, 128, True)
+        round_w1(0, 0, 0, 32, "S")
+        round_w1(0, 0, 32, 80, "S")
+        round_w1(0, 0, 80, 128, "G")
         quantise_w1(0, 0)
-        for jb in range(EARLY):
-            open_bank(0, jb)
+        for q in range(7):
+            open_bank(0, q)
+        caps_to_psum()
         gather_words(1, 0, S)
-        round_w1(1, 0, 0, 44, False)
-        round_w1(1, 0, 44, 128, True)
+        round_w1(1, 0, 0, 48, "S")
+        round_w1(1, 0, 48, 96, "G")
+        round_w1(1, 0, 96, 128, "S")
         quantise_w1(1, 0, 0)
         quantise_w1(1, 0, 1)
-        round_w1(0, 1, 0, 64, False)
-        round_w1(0, 1, 64, 128, True)
-        close_bank(0, 0)
-        close_bank(0, 1)
+        round_w1(0, 1, 0, 64, "G")
+        round_w1(0, 1, 64, 128, "G")
+        round_w1(1, 1, 0, 64, "G")
+        round_w1(1, 1, 64, 128, "G")
+        for jb in range(4):
+            close_block(0, jb)
         cap_paths(0, 0, 256)
-        quantise_w1(0, 1)
-        close_bank(0, 2)
-        close_bank(0, 3)
-        round_w1(1, 1, 0, 64, False)
-        round_w1(1, 1, 64, 128, True)
         cap_paths(0, 256, 256)
-        close_bank(0, 4)
-        close_bank(0, 5)
+        quantise_w1(0, 1)
+        for q in range(7):
+            open_bank(1, q)
         cap_paths(0, 512, 256)
-        quantise_w1(1, 1)
         quantise_h(0, 0)
-        close_bank(0, 6)
-        close_bank(0, 7)
+        quantise_w1(1, 1, 0)
+        quantise_w1(1, 1, 1)
+        for jb in range(4):
+            close_block(1, jb)
         cap_paths(0, 768, 256)
-        close_bank(1, 0)
-        close_bank(1, 1)
-        cap_paths(1, 0, 256)
         quantise_h(0, 1)
-        close_bank(1, 2)
-        close_bank(1, 3)
+        quantise_h(0, 2)
+        quantise_h(0, 3)
+        cap_paths(1, 0, 256)
         cap_paths(1, 256, 256)
-        close_bank(1, 4)
-        close_bank(1, 5)
-        cap_paths(1, 512, 256)
         quantise_h(1, 0)
-        close_bank(1, 6)
-        close_bank(1, 7)
+        cap_paths(1, 512, 256)
+        quantise_h(1, 1)
         for n in range(4):
             second_stage(0, n)
         cap_paths(1, 768, 256)
+        quantise_h(1, 2)
         payoff(0, 0, 512)
-        quantise_h(1, 1)
+        quantise_h(1, 3)
         for n in range(4):
             second_stage(1, n)
+
         for n in range(1, 4):
             payoff(0, n, 512)
         for n in range(2):

@@ -23,7 +23,7 @@ PASS = P * PACK
 JB = 256
 JC = 512
 LIST_ROWS = 16
-W1_CUTS = {(0, 0): (0, 32, 128), (1, 0): (0, 48, 96, 128), (0, 1): (0, 64, 128), (1, 1): (0, 64, 128)}
+W1_CUTS = {(0, 0): (0, 32, 128), (1, 0): (0, 48, 96, 128), (0, 1): (0, 48, 96, 128), (1, 1): (0, 64, 128)}
 
 
 def tile_list_floating_strike_payoffs_kernel(tc, tab_words, tab_scales, offs, w1, cap, w4_words, w4_scales, gT, out):
@@ -123,8 +123,8 @@ def tile_list_floating_strike_payoffs_kernel(tc, tab_words, tab_scales, offs, w1
         v_plane = keep.tile([P, S], U8, name="v_plane", align_bytes=64)
         w1_bf = {}
         w1_codes = {}
-        bf_names = {(0, 1): "w1_bf10"}
-        code_names = {(0, 1): "th01", (1, 1): "th02"}
+        bf_names = {}
+        code_names = {}
         w1_plane = {k: keep.tile([P, PASS], U8, name="w1_plane%d%d" % k, align_bytes=64) for k in W1_CUTS}
 
         def gather_words(a, j0, n):
@@ -141,7 +141,7 @@ def tile_list_floating_strike_payoffs_kernel(tc, tab_words, tab_scales, offs, w1
             elif how == "V":
                 nc.vector.tensor_copy(dst, src)
             else:
-                nc.gpsimd.tensor_scalar(dst.rearrange("p m i t -> p m t i"), src.rearrange("p m i t -> p m t i"), 1.0, 0.0, ALU.mult, ALU.add)
+                nc.gpsimd.tensor_scalar(dst, src, 1.0, 0.0, ALU.mult, ALU.add)
 
         def quantise_w1(a, b, half=None):
             if (a, b) not in w1_codes:
@@ -171,7 +171,7 @@ def tile_list_floating_strike_payoffs_kernel(tc, tab_words, tab_scales, offs, w1
         halves = [(b, jc) for b in range(2) for jc in range(S // JC)]
         th = {(b, jb): keep.tile([P, 2, JB, 2], F32, name="th%d%d" % (b, jb), align_bytes=64) for b in range(2) for jb in range(S // JB)}
         h_bf = {}
-        reused = {(0, 2): "w1_bf10", (0, 3): "w1_bf11"}
+        reused = {(0, 2): "h_bf01", (1, 2): "h_bf03"}
         h_codes = {k: keep.tile([P, JC], U32, name="h_codes%d%d" % k, align_bytes=64) for k in halves}
         h_plane = {k: keep.tile([P, JC], U8, name="h_plane%d%d" % k, align_bytes=64) for k in halves}
 
@@ -252,49 +252,54 @@ def tile_list_floating_strike_payoffs_kernel(tc, tab_words, tab_scales, offs, w1
         gather_words(0, 0, S)
         round_w1(0, 0, 0, 32, "S")
         round_w1(0, 0, 32, 80, "S")
-        round_w1(0, 0, 80, 128, "G")
+        round_w1(0, 0, 80, 128, "V")
         quantise_w1(0, 0)
-        for q in range(7):
+        for q in range(4):
             open_bank(0, q)
         caps_to_psum()
         gather_words(1, 0, S)
         round_w1(1, 0, 0, 48, "S")
-        round_w1(1, 0, 48, 96, "G")
-        round_w1(1, 0, 96, 128, "S")
+        round_w1(1, 0, 48, 96, "S")
+        round_w1(1, 0, 96, 128, "V")
         quantise_w1(1, 0, 0)
         quantise_w1(1, 0, 1)
-        round_w1(0, 1, 0, 64, "G")
-        round_w1(0, 1, 64, 128, "G")
-        round_w1(1, 1, 0, 64, "G")
-        round_w1(1, 1, 64, 128, "G")
-        for jb in range(4):
-            close_block(0, jb)
+        round_w1(0, 1, 0, 48, "V")
+        round_w1(0, 1, 48, 96, "V")
+        round_w1(0, 1, 96, 128, "V")
+        close_block(0, 0)
+        close_block(0, 1)
         cap_paths(0, 0, 256)
-        cap_paths(0, 256, 256)
         quantise_w1(0, 1)
-        for q in range(7):
+        round_w1(1, 1, 0, 64, "S")
+        close_block(0, 2)
+        close_block(0, 3)
+        for q in range(3):
             open_bank(1, q)
-        cap_paths(0, 512, 256)
+        cap_paths(0, 256, 256)
+        round_w1(1, 1, 64, 128, "V")
         quantise_h(0, 0)
         quantise_w1(1, 1, 0)
         quantise_w1(1, 1, 1)
         for jb in range(4):
             close_block(1, jb)
-        cap_paths(0, 768, 256)
         quantise_h(0, 1)
-        quantise_h(0, 2)
-        quantise_h(0, 3)
+        cap_paths(0, 512, 256, "G")
+        cap_paths(0, 768, 176)
+        cap_paths(0, 944, 80, "G")
         cap_paths(1, 0, 256)
         cap_paths(1, 256, 256)
         quantise_h(1, 0)
-        cap_paths(1, 512, 256)
+        quantise_h(0, 2)
         quantise_h(1, 1)
         for n in range(4):
             second_stage(0, n)
+        quantise_h(0, 3)
+        cap_paths(1, 512, 160, "G")
         cap_paths(1, 768, 256)
-        quantise_h(1, 2)
-        payoff(0, 0, 512)
+        cap_paths(1, 672, 96)
         quantise_h(1, 3)
+        payoff(0, 0, 512)
+        quantise_h(1, 2)
         for n in range(4):
             second_stage(1, n)
 

@@ -23,7 +23,7 @@ PASS = P * PACK
 JB = 256
 JC = 512
 LIST_ROWS = 16
-W1_CUTS = {(0, 0): (0, 32, 128), (1, 0): (0, 48, 96, 128), (0, 1): (0, 48, 96, 128), (1, 1): (0, 64, 128)}
+W1_CUTS = {(0, 0): (0, 128), (1, 0): (0, 64, 128), (0, 1): (0, 128), (1, 1): (0, 128)}
 
 
 def tile_list_floating_strike_payoffs_kernel(tc, tab_words, tab_scales, offs, w1, cap, w4_words, w4_scales, gT, out):
@@ -44,6 +44,8 @@ def tile_list_floating_strike_payoffs_kernel(tc, tab_words, tab_scales, offs, w1
         tab_plane = keep.tile([P, T], U8, name="tab_plane", align_bytes=64)
         tab_rows = keep.tile([P, T // 4], I32, name="tab_rows", align_bytes=64)
         w4_plane = keep.tile([P, 2 * N], U8, name="w4_plane", align_bytes=64)
+        cap_rows = keep.tile([P, PASS], F32, name="cap_rows", align_bytes=64)
+        nc.gpsimd.memset(cap_rows[:], 0.0)
         nc.gpsimd.memset(tab_plane[:].bitcast(I32), 0)
         nc.vector.memset(w4_plane[:].bitcast(I32), 0)
 
@@ -62,10 +64,8 @@ def tile_list_floating_strike_payoffs_kernel(tc, tab_words, tab_scales, offs, w1
         strikes = [keep.tile([P, T], F32, name="strikes%d" % n, align_bytes=64) for n in range(N // P)]
         caps = keep.tile([P, 2, PACK], F32, name="caps")
         w4_codes = keep.tile([P, 2, 2 * N], U8, name="w4_codes", align_bytes=64)
-        cap_rows = keep.tile([P, PASS], F32, name="cap_rows", align_bytes=64)
         identity = keep.tile([P, P], F32, name="identity", align_bytes=64)
         caps_ps = ps0.tile([P, PACK, P], F32, name="caps_ps")
-        nc.gpsimd.memset(cap_rows[:], 0.0)
         make_identity(nc, identity[:])
 
         def load_cap_rows():
@@ -74,6 +74,7 @@ def tile_list_floating_strike_payoffs_kernel(tc, tab_words, tab_scales, offs, w1
         def caps_to_psum():
             for t in range(PACK):
                 nc.tensor.transpose(caps_ps[:, t, :], cap_rows[:, t:PASS:PACK], identity[:])
+            nc.scalar.activation(caps[:], caps_ps[:, :, 0:2].rearrange("p t b -> p b t"), ACT.Copy)
 
         def load_tab(a):
             nc.sync.dma_start(out=tab[a][:], in_=tab_words[a].rearrange("p t i -> p (t i)").bitcast(I32))
@@ -85,9 +86,6 @@ def tile_list_floating_strike_payoffs_kernel(tc, tab_words, tab_scales, offs, w1
                 out=raw[a, b, m0][:],
                 in_=w1[a * PASS : (a + 1) * PASS, c0 : c0 + width].rearrange("(p i) c -> p i c", i=PACK),
             )
-
-        def load_caps():
-            nc.sync.dma_start(out=caps[:], in_=cap.rearrange("(b p t) -> p b t", b=2, t=PACK))
 
         def load_w4():
             nc.sync.dma_start(out=w4_codes[:].bitcast(I32), in_=w4_words.rearrange("a p c -> p a c").bitcast(I32))
@@ -103,23 +101,20 @@ def tile_list_floating_strike_payoffs_kernel(tc, tab_words, tab_scales, offs, w1
             nc.sync.dma_start(out=strikes[n][:], in_=gT[n * P : (n + 1) * P, :])
 
         load_tab_plane()
-        load_w1(0, 0, 0)
-        load_tab(0)
-        load_w1(0, 0, 32)
-        load_tab(1)
         load_cap_rows()
-        for m0 in W1_CUTS[1, 0][:-1]:
-            load_w1(1, 0, m0)
-        load_caps()
-        for a in range(2):
-            for m0 in W1_CUTS[a, 1][:-1]:
-                load_w1(a, 1, m0)
+        load_tab(0)
+        load_w1(0, 0)
+        load_tab(1)
+        load_w1(1, 0, 0)
+        load_w1(1, 0, 64)
+        load_w1(0, 1)
+        load_w1(1, 1)
         load_w4()
         load_w4_plane()
         for n in range(4):
             load_strikes(n)
 
-        v_codes = [keep.tile([P, S], U32, name="v_codes%d" % a, align_bytes=64) for a in range(2)]
+        v_codes = {}
         v_plane = keep.tile([P, S], U8, name="v_plane", align_bytes=64)
         w1_bf = {}
         w1_codes = {}
@@ -128,6 +123,8 @@ def tile_list_floating_strike_payoffs_kernel(tc, tab_words, tab_scales, offs, w1
         w1_plane = {k: keep.tile([P, PASS], U8, name="w1_plane%d%d" % k, align_bytes=64) for k in W1_CUTS}
 
         def gather_words(a, j0, n):
+            if a not in v_codes:
+                v_codes[a] = keep.tile([P, S], U32, name=("v_codes0", "w1_bf00")[a], align_bytes=64)
             nc.vector.tensor_copy(v_codes[a][:, j0 : j0 + n], tab[a][:].bitcast(U32).indirect(picks(j0, n)))
 
         def round_w1(a, b, m0, m1, how):
@@ -250,22 +247,19 @@ def tile_list_floating_strike_payoffs_kernel(tc, tab_words, tab_scales, offs, w1
 
         gather_plane()
         gather_words(0, 0, S)
-        round_w1(0, 0, 0, 32, "S")
-        round_w1(0, 0, 32, 80, "S")
+        caps_to_psum()
+        round_w1(0, 0, 0, 80, "S")
         round_w1(0, 0, 80, 128, "V")
         quantise_w1(0, 0)
         for q in range(4):
             open_bank(0, q)
-        caps_to_psum()
         gather_words(1, 0, S)
-        round_w1(1, 0, 0, 48, "S")
-        round_w1(1, 0, 48, 96, "S")
-        round_w1(1, 0, 96, 128, "V")
+        round_w1(1, 0, 0, 64, "S")
+        round_w1(1, 0, 64, 84, "S")
+        round_w1(1, 0, 84, 128, "V")
         quantise_w1(1, 0, 0)
         quantise_w1(1, 0, 1)
-        round_w1(0, 1, 0, 48, "V")
-        round_w1(0, 1, 48, 96, "V")
-        round_w1(0, 1, 96, 128, "V")
+        round_w1(0, 1, 0, 128, "V")
         close_block(0, 0)
         close_block(0, 1)
         cap_paths(0, 0, 256)

@@ -65,7 +65,7 @@ def tile_list_floating_strike_payoffs_kernel(tc, tab_words, tab_scales, offs, w1
         caps = keep.tile([P, 2, PACK], F32, name="caps")
         w4_codes = keep.tile([P, 2, 2 * N], U8, name="w4_codes", align_bytes=64)
         identity = keep.tile([P, P], F32, name="identity", align_bytes=64)
-        caps_ps = ps0.tile([P, PACK, P], F32, name="caps_ps")
+        caps_ps = ps0.tile([P, P, PACK], F32, name="caps_ps")
         make_identity(nc, identity[:])
 
         def load_cap_rows():
@@ -73,8 +73,8 @@ def tile_list_floating_strike_payoffs_kernel(tc, tab_words, tab_scales, offs, w1
 
         def caps_to_psum():
             for t in range(PACK):
-                nc.tensor.transpose(caps_ps[:, t, :], cap_rows[:, t:PASS:PACK], identity[:])
-            nc.scalar.activation(caps[:], caps_ps[:, :, 0:2].rearrange("p t b -> p b t"), ACT.Copy)
+                nc.tensor.transpose(caps_ps[:, :, t], cap_rows[:, t:PASS:PACK], identity[:])
+            nc.scalar.activation(caps[:], caps_ps[:, 0:2, :], ACT.Copy)
 
         def load_tab(a):
             nc.sync.dma_start(out=tab[a][:], in_=tab_words[a].rearrange("p t i -> p (t i)").bitcast(I32))
@@ -186,7 +186,7 @@ def tile_list_floating_strike_payoffs_kernel(tc, tab_words, tab_scales, offs, w1
             src = th[b, jb][:, :, inner : inner + n, :].rearrange("p u j e -> p j u e")
             in_sbuf = caps[:, b : b + 1, :].rearrange("p o (u e) -> p o u e", u=2).to_broadcast([P, n, 2, 2])
             if how == "V":
-                in_psum = caps_ps[:, :, b : b + 1].rearrange("p (u e) o -> p o u e", u=2).to_broadcast([P, n, 2, 2])
+                in_psum = caps_ps[:, b : b + 1, :].rearrange("p o (u e) -> p o u e", u=2).to_broadcast([P, n, 2, 2])
                 nc.vector.tensor_tensor(dst, src, in_psum, ALU.mult)
             else:
                 nc.gpsimd.tensor_tensor(dst, src, in_sbuf, ALU.mult)

@@ -23,6 +23,7 @@ PASS = P * PACK
 JB = 256
 JC = 512
 LIST_ROWS = 16
+REPEAT = 16
 W1_CUTS = {(0, 0): (0, 128), (1, 0): (0, 64, 128), (0, 1): (0, 128), (1, 1): (0, 128)}
 
 
@@ -62,7 +63,7 @@ def tile_list_floating_strike_payoffs_kernel(tc, tab_words, tab_scales, offs, w1
             for (a, b), cuts in W1_CUTS.items() for m0, m1 in zip(cuts, cuts[1:])
         }
         strikes = [keep.tile([P, T], F32, name="strikes%d" % n, align_bytes=64) for n in range(N // P)]
-        caps = keep.tile([P, 2, PACK], F32, name="caps")
+        caps = keep.tile([P, 2, REPEAT * PACK], F32, name="caps", align_bytes=64)
         w4_codes = keep.tile([P, 2, 2 * N], U8, name="w4_codes", align_bytes=64)
         identity = keep.tile([P, P], F32, name="identity", align_bytes=64)
         caps_ps = ps0.tile([P, P, PACK], F32, name="caps_ps")
@@ -74,7 +75,11 @@ def tile_list_floating_strike_payoffs_kernel(tc, tab_words, tab_scales, offs, w1
         def caps_to_psum():
             for t in range(PACK):
                 nc.tensor.transpose(caps_ps[:, :, t], cap_rows[:, t:PASS:PACK], identity[:])
-            nc.scalar.activation(caps[:], caps_ps[:, 0:2, :], ACT.Copy)
+            nc.scalar.activation(
+                caps[:].rearrange("p b (j t) -> p b j t", t=PACK),
+                caps_ps[:, 0:2, :].unsqueeze(2).to_broadcast([P, 2, REPEAT, PACK]),
+                ACT.Copy,
+            )
 
         def load_tab(a):
             nc.sync.dma_start(out=tab[a][:], in_=tab_words[a].rearrange("p t i -> p (t i)").bitcast(I32))
@@ -150,8 +155,23 @@ def tile_list_floating_strike_payoffs_kernel(tc, tab_words, tab_scales, offs, w1
                 in_=w1_bf[a, b][:, PACK * c0 : PACK * c1],
             )
 
+        narrow = {(0, 2), (0, 3), (1, 2)}
+
         def first_pass(bank, a, b, q):
             jb, u = divmod(q, 2)
+            if (b, jb) in narrow:
+                cols = slice(q * P, (q + 1) * P)
+                for t in range(PACK):
+                    nc.tensor.matmul_mx(
+                        out=bank[:, t * P : (t + 1) * P],
+                        lhsT=w1_codes[a, b][:, t * P : (t + 1) * P].bitcast(FP8X4),
+                        lhsT_scale=w1_plane[a, b][:, t * P : (t + 1) * P],
+                        rhs=v_codes[a][:, cols].bitcast(FP8X4),
+                        rhs_scale=v_plane[4 * a :, cols],
+                        start=(a == 0 and t == 0),
+                        stop=(a == 1 and t == PACK - 1),
+                    )
+                return
             cols = slice(jb * JB, (jb + 1) * JB)
             for e in range(2):
                 t = 2 * u + e
@@ -174,6 +194,13 @@ def tile_list_floating_strike_payoffs_kernel(tc, tab_words, tab_scales, offs, w1
 
         def saturate_bank(bank, b, q):
             jb, u = divmod(q, 2)
+            if (b, jb) in narrow:
+                nc.scalar.activation(
+                    th[b, jb][:, u].rearrange("p j e -> p (j e)").rearrange("p (j t) -> p j t", t=PACK),
+                    bank[:].rearrange("p (t j) -> p j t", t=PACK),
+                    ACT.Tanh,
+                )
+                return
             nc.scalar.activation(
                 th[b, jb][:, u, :, :], bank[:].rearrange("p (e j) -> p j e", e=2), ACT.Tanh
             )
@@ -184,12 +211,19 @@ def tile_list_floating_strike_payoffs_kernel(tc, tab_words, tab_scales, offs, w1
                 h_bf[b, jb] = keep.tile([P, JB * PACK], BF16, name=reused.get((b, jb), "h_bf%d%d" % (b, jb)), align_bytes=64)
             dst = h_bf[b, jb][:, inner * PACK : (inner + n) * PACK].rearrange("p (j u e) -> p j u e", u=2, e=2)
             src = th[b, jb][:, :, inner : inner + n, :].rearrange("p u j e -> p j u e")
-            in_sbuf = caps[:, b : b + 1, :].rearrange("p o (u e) -> p o u e", u=2).to_broadcast([P, n, 2, 2])
+            if (b, jb) in narrow:
+                src = th[b, jb][:].rearrange("p x j e -> p (x j e)").rearrange("p (j u e) -> p j u e", u=2, e=2)[:, inner : inner + n]
             if how == "V":
                 in_psum = caps_ps[:, b : b + 1, :].rearrange("p o (u e) -> p o u e", u=2).to_broadcast([P, n, 2, 2])
                 nc.vector.tensor_tensor(dst, src, in_psum, ALU.mult)
             else:
-                nc.gpsimd.tensor_tensor(dst, src, in_sbuf, ALU.mult)
+                rows = "p (x j) u e -> p x (j u e)"
+                nc.gpsimd.tensor_tensor(
+                    dst.rearrange(rows, j=REPEAT),
+                    src.rearrange(rows, j=REPEAT),
+                    caps[:, b : b + 1, :].to_broadcast([P, n // REPEAT, REPEAT * PACK]),
+                    ALU.mult,
+                )
 
         def quantise_h(b, jb):
             jc, part = divmod(jb, 2)
@@ -248,8 +282,8 @@ def tile_list_floating_strike_payoffs_kernel(tc, tab_words, tab_scales, offs, w1
         gather_plane()
         gather_words(0, 0, S)
         caps_to_psum()
-        round_w1(0, 0, 0, 80, "S")
-        round_w1(0, 0, 80, 128, "V")
+        round_w1(0, 0, 0, 64, "S")
+        round_w1(0, 0, 64, 128, "V")
         quantise_w1(0, 0)
         for q in range(4):
             open_bank(0, q)

@@ -24,7 +24,7 @@ JB = 256
 JC = 512
 LIST_ROWS = 16
 REPEAT = 16
-W1_CUTS = {(0, 0): (0, 128), (1, 0): (0, 64, 128), (0, 1): (0, 128), (1, 1): (0, 128)}
+W1_CUTS = {(0, 0): (0, 64, 128), (1, 0): (0, 64, 96, 128), (0, 1): (0, 64, 128), (1, 1): (0, 64, 128)}
 
 
 def tile_list_floating_strike_payoffs_kernel(tc, tab_words, tab_scales, offs, w1, cap, w4_words, w4_scales, gT, out):
@@ -108,12 +108,12 @@ def tile_list_floating_strike_payoffs_kernel(tc, tab_words, tab_scales, offs, w1
         load_tab_plane()
         load_cap_rows()
         load_tab(0)
-        load_w1(0, 0)
+        load_w1(0, 0, 0)
+        load_w1(0, 0, 64)
         load_tab(1)
-        load_w1(1, 0, 0)
-        load_w1(1, 0, 64)
-        load_w1(0, 1)
-        load_w1(1, 1)
+        for a, b in ((1, 0), (0, 1), (1, 1)):
+            for m0 in W1_CUTS[a, b][:-1]:
+                load_w1(a, b, m0)
         load_w4()
         load_w4_plane()
         for n in range(4):
@@ -213,7 +213,10 @@ def tile_list_floating_strike_payoffs_kernel(tc, tab_words, tab_scales, offs, w1
             src = th[b, jb][:, :, inner : inner + n, :].rearrange("p u j e -> p j u e")
             if (b, jb) in narrow:
                 src = th[b, jb][:].rearrange("p x j e -> p (x j e)").rearrange("p (j u e) -> p j u e", u=2, e=2)[:, inner : inner + n]
-            if how == "V":
+            if how == "W":
+                in_sbuf = caps[:, b : b + 1, 0:PACK].rearrange("p o (u e) -> p o u e", u=2).to_broadcast([P, n, 2, 2])
+                nc.vector.tensor_tensor(dst, src, in_sbuf, ALU.mult)
+            elif how == "V":
                 in_psum = caps_ps[:, b : b + 1, :].rearrange("p o (u e) -> p o u e", u=2).to_broadcast([P, n, 2, 2])
                 nc.vector.tensor_tensor(dst, src, in_psum, ALU.mult)
             else:
@@ -289,21 +292,22 @@ def tile_list_floating_strike_payoffs_kernel(tc, tab_words, tab_scales, offs, w1
             open_bank(0, q)
         gather_words(1, 0, S)
         round_w1(1, 0, 0, 64, "S")
-        round_w1(1, 0, 64, 84, "S")
-        round_w1(1, 0, 84, 128, "V")
+        round_w1(1, 0, 64, 96, "V")
+        round_w1(1, 0, 96, 128, "S")
         quantise_w1(1, 0, 0)
         quantise_w1(1, 0, 1)
-        round_w1(0, 1, 0, 128, "V")
+        round_w1(0, 1, 0, 64, "V")
+        round_w1(0, 1, 64, 128, "V")
         close_block(0, 0)
         close_block(0, 1)
-        cap_paths(0, 0, 256)
+        cap_paths(0, 0, 256, "W")
         quantise_w1(0, 1)
         round_w1(1, 1, 0, 64, "S")
         close_block(0, 2)
         close_block(0, 3)
         for q in range(3):
             open_bank(1, q)
-        cap_paths(0, 256, 256)
+        cap_paths(0, 256, 256, "W")
         round_w1(1, 1, 64, 128, "V")
         quantise_h(0, 0)
         quantise_w1(1, 1, 0)

@@ -46,7 +46,7 @@ def tile_list_floating_strike_payoffs_kernel(tc, tab_words, tab_scales, offs, w1
         tab_rows = keep.tile([P, T // 4], I32, name="tab_rows", align_bytes=64)
         w4_plane = keep.tile([P, 2 * N], U8, name="w4_plane", align_bytes=64)
         cap_rows = keep.tile([P, PASS], F32, name="cap_rows", align_bytes=64)
-        nc.gpsimd.memset(cap_rows[:], 0.0)
+        nc.vector.memset(cap_rows[:], 0.0)
         nc.gpsimd.memset(tab_plane[:].bitcast(I32), 0)
         nc.vector.memset(w4_plane[:].bitcast(I32), 0)
 
@@ -106,9 +106,9 @@ def tile_list_floating_strike_payoffs_kernel(tc, tab_words, tab_scales, offs, w1
             nc.sync.dma_start(out=strikes[n][:], in_=gT[n * P : (n + 1) * P, :])
 
         load_tab_plane()
-        load_cap_rows()
         load_tab(0)
         load_w1(0, 0, 0)
+        load_cap_rows()
         load_w1(0, 0, 64)
         load_tab(1)
         for a, b in ((1, 0), (0, 1), (1, 1)):
@@ -286,7 +286,8 @@ def tile_list_floating_strike_payoffs_kernel(tc, tab_words, tab_scales, offs, w1
         gather_words(0, 0, S)
         caps_to_psum()
         round_w1(0, 0, 0, 64, "S")
-        round_w1(0, 0, 64, 128, "V")
+        round_w1(0, 0, 64, 112, "S")
+        round_w1(0, 0, 112, 128, "V")
         quantise_w1(0, 0)
         for q in range(4):
             open_bank(0, q)

@@ -1,7 +1,6 @@
 from contextlib import ExitStack
 
 import concourse.mybir as mybir
-from concourse.masks import make_identity
 
 K, T, S, R, N = 1024, 2048, 1024, 1024, 512
 FLOPS = 2 * K * R * S + 2 * R * N * S
@@ -23,18 +22,15 @@ PASS = P * PACK
 JB = 256
 JC = 512
 LIST_ROWS = 16
-REPEAT = 16
-W1_CUTS = {(0, 0): (0, 64, 128), (1, 0): (0, 64, 96, 128), (0, 1): (0, 64, 128), (1, 1): (0, 64, 128)}
+W1_CUTS = {(0, 0): (0, 64, 128), (1, 0): (0, 64, 128), (0, 1): (0, 128), (1, 1): (0, 128)}
 
 
 def tile_list_floating_strike_payoffs_kernel(tc, tab_words, tab_scales, offs, w1, cap, w4_words, w4_scales, gT, out):
     nc = tc.nc
     with ExitStack() as ctx:
         keep = ctx.enter_context(tc.tile_pool(name="keep", bufs=1))
-        ring = ctx.enter_context(tc.tile_pool(name="ring", bufs=10))
-        ps1 = ctx.enter_context(tc.psum_pool(name="ps1", bufs=7))
-        ps2 = ps1
-        ps0 = ctx.enter_context(tc.psum_pool(name="ps0", bufs=1))
+        ring = ctx.enter_context(tc.tile_pool(name="ring", bufs=8))
+        psum = ctx.enter_context(tc.psum_pool(name="psum", bufs=8))
 
         offsets = keep.tile([P, S // LIST_ROWS], U16, name="offsets")
         nc.sync.dma_start(offsets[:], offs)
@@ -43,19 +39,9 @@ def tile_list_floating_strike_payoffs_kernel(tc, tab_words, tab_scales, offs, w1
             return offsets[:, j0 // LIST_ROWS : (j0 + n) // LIST_ROWS]
 
         tab_plane = keep.tile([P, T], U8, name="tab_plane", align_bytes=64)
-        tab_rows = keep.tile([P, T // 4], I32, name="tab_rows", align_bytes=64)
         w4_plane = keep.tile([P, 2 * N], U8, name="w4_plane", align_bytes=64)
-        cap_rows = keep.tile([P, PASS], F32, name="cap_rows", align_bytes=64)
-        nc.vector.memset(cap_rows[:], 0.0)
-        nc.gpsimd.memset(tab_plane[:].bitcast(I32), 0)
+        nc.vector.memset(tab_plane[:].bitcast(I32), 0)
         nc.vector.memset(w4_plane[:].bitcast(I32), 0)
-
-        def load_tab_plane():
-            for q in range(4):
-                nc.sync.dma_start(
-                    out=tab_rows[32 * q : 32 * q + 8, :],
-                    in_=tab_scales[:, 4 * q : 4 * q + 4, :].bitcast(I32),
-                )
 
         tab = [keep.tile([P, T], I32, name="tab%d" % a, align_bytes=64) for a in range(2)]
         raw = {
@@ -63,23 +49,18 @@ def tile_list_floating_strike_payoffs_kernel(tc, tab_words, tab_scales, offs, w1
             for (a, b), cuts in W1_CUTS.items() for m0, m1 in zip(cuts, cuts[1:])
         }
         strikes = [keep.tile([P, T], F32, name="strikes%d" % n, align_bytes=64) for n in range(N // P)]
-        caps = keep.tile([P, 2, REPEAT * PACK], F32, name="caps", align_bytes=64)
+        caps = keep.tile([P, 2, PACK], F32, name="caps", align_bytes=64)
         w4_codes = keep.tile([P, 2, 2 * N], U8, name="w4_codes", align_bytes=64)
-        identity = keep.tile([P, P], F32, name="identity", align_bytes=64)
-        caps_ps = ps0.tile([P, P, PACK], F32, name="caps_ps")
-        make_identity(nc, identity[:])
 
-        def load_cap_rows():
-            nc.sync.dma_start(out=cap_rows[0:2, :], in_=cap.rearrange("(b c) -> b c", b=2))
+        def load_tab_plane():
+            for q in range(4):
+                nc.sync.dma_start(
+                    out=tab_plane[32 * q : 32 * q + 8, :].bitcast(I32),
+                    in_=tab_scales[:, 4 * q : 4 * q + 4, :].bitcast(I32),
+                )
 
-        def caps_to_psum():
-            for t in range(PACK):
-                nc.tensor.transpose(caps_ps[:, :, t], cap_rows[:, t:PASS:PACK], identity[:])
-            nc.scalar.activation(
-                caps[:].rearrange("p b (j t) -> p b j t", t=PACK),
-                caps_ps[:, 0:2, :].unsqueeze(2).to_broadcast([P, 2, REPEAT, PACK]),
-                ACT.Copy,
-            )
+        def load_caps():
+            nc.sync.dma_start(out=caps[:], in_=cap.rearrange("(b p t) -> p b t", b=2, t=PACK))
 
         def load_tab(a):
             nc.sync.dma_start(out=tab[a][:], in_=tab_words[a].rearrange("p t i -> p (t i)").bitcast(I32))
@@ -94,8 +75,6 @@ def tile_list_floating_strike_payoffs_kernel(tc, tab_words, tab_scales, offs, w1
 
         def load_w4():
             nc.sync.dma_start(out=w4_codes[:].bitcast(I32), in_=w4_words.rearrange("a p c -> p a c").bitcast(I32))
-
-        def load_w4_plane():
             for q in range(4):
                 nc.sync.dma_start(
                     out=w4_plane[32 * q : 32 * q + 4, :].rearrange("p (a c) -> p a c", a=2).bitcast(I32),
@@ -105,78 +84,64 @@ def tile_list_floating_strike_payoffs_kernel(tc, tab_words, tab_scales, offs, w1
         def load_strikes(n):
             nc.sync.dma_start(out=strikes[n][:], in_=gT[n * P : (n + 1) * P, :])
 
-        load_tab_plane()
-        load_tab(0)
         load_w1(0, 0, 0)
-        load_cap_rows()
+        load_tab_plane()
         load_w1(0, 0, 64)
+        load_tab(0)
+        load_w1(1, 0, 0)
+        load_w1(1, 0, 64)
         load_tab(1)
-        for a, b in ((1, 0), (0, 1), (1, 1)):
-            for m0 in W1_CUTS[a, b][:-1]:
-                load_w1(a, b, m0)
+        load_caps()
+        load_w1(0, 1)
+        load_w1(1, 1)
         load_w4()
-        load_w4_plane()
         for n in range(4):
             load_strikes(n)
+
+        tenants = {"w1_codes00": "tab_plane", "th03": "raw11_0", "h_bf01": "w1_bf11", "h_codes01": "th10", "h_bf11": "h_bf01", "h_bf00": "raw01_0"}
+
+        def late_tile(shape, dtype, name):
+            return keep.tile(shape, dtype, name=tenants.get(name, name), align_bytes=64)
 
         v_codes = {}
         v_plane = keep.tile([P, S], U8, name="v_plane", align_bytes=64)
         w1_bf = {}
         w1_codes = {}
-        bf_names = {}
-        code_names = {}
         w1_plane = {k: keep.tile([P, PASS], U8, name="w1_plane%d%d" % k, align_bytes=64) for k in W1_CUTS}
+
+        def gather_plane():
+            nc.vector.tensor_copy(v_plane[:], tab_plane[:].indirect(offsets[:]))
 
         def gather_words(a, j0, n):
             if a not in v_codes:
-                v_codes[a] = keep.tile([P, S], U32, name=("v_codes0", "w1_bf00")[a], align_bytes=64)
+                v_codes[a] = late_tile([P, S], U32, "v_codes%d" % a)
             nc.vector.tensor_copy(v_codes[a][:, j0 : j0 + n], tab[a][:].bitcast(U32).indirect(picks(j0, n)))
 
         def round_w1(a, b, m0, m1, how):
             if (a, b) not in w1_bf:
-                w1_bf[a, b] = keep.tile([P, PASS * PACK], BF16, name=bf_names.get((a, b), "w1_bf%d%d" % (a, b)), align_bytes=64)
+                w1_bf[a, b] = late_tile([P, PASS * PACK], BF16, "w1_bf%d%d" % (a, b))
             u = max(c for c in W1_CUTS[a, b] if c <= m0)
             dst = w1_bf[a, b][:].rearrange("p (t m i) -> p m i t", t=PACK, i=PACK)[:, m0:m1]
             src = raw[a, b, u][:].rearrange("p i (m t) -> p m i t", t=PACK)[:, m0 - u : m1 - u]
             if how == "S":
                 nc.scalar.activation(dst, src, ACT.Copy)
-            elif how == "V":
-                nc.vector.tensor_copy(dst, src)
             else:
-                nc.gpsimd.tensor_scalar(dst, src, 1.0, 0.0, ALU.mult, ALU.add)
+                nc.vector.tensor_copy(dst, src)
 
-        def quantise_w1(a, b, half=None):
-            if (a, b) not in w1_codes:
-                w1_codes[a, b] = keep.tile([P, PASS], U32, name=code_names.get((a, b), "w1_codes%d%d" % (a, b)), align_bytes=64)
-            c0, c1 = (0, PASS) if half is None else (half * PASS // 2, (half + 1) * PASS // 2)
-            nc.vector.quantize_mx(
-                out=w1_codes[a, b][:, c0:c1].bitcast(FP8X4),
-                scales=w1_plane[a, b][:, c0:c1],
-                in_=w1_bf[a, b][:, PACK * c0 : PACK * c1],
-            )
+        def quantise_w1(a, b):
+            w1_codes[a, b] = late_tile([P, PASS], U32, "w1_codes%d%d" % (a, b))
+            nc.vector.quantize_mx(out=w1_codes[a, b][:].bitcast(FP8X4), scales=w1_plane[a, b][:], in_=w1_bf[a, b][:])
 
-        narrow = {(0, 2), (0, 3), (1, 2)}
+        banks = {}
 
-        def first_pass(bank, a, b, q):
-            jb, u = divmod(q, 2)
-            if (b, jb) in narrow:
-                cols = slice(q * P, (q + 1) * P)
-                for t in range(PACK):
-                    nc.tensor.matmul_mx(
-                        out=bank[:, t * P : (t + 1) * P],
-                        lhsT=w1_codes[a, b][:, t * P : (t + 1) * P].bitcast(FP8X4),
-                        lhsT_scale=w1_plane[a, b][:, t * P : (t + 1) * P],
-                        rhs=v_codes[a][:, cols].bitcast(FP8X4),
-                        rhs_scale=v_plane[4 * a :, cols],
-                        start=(a == 0 and t == 0),
-                        stop=(a == 1 and t == PACK - 1),
-                    )
-                return
+        def first_pass(a, b, jb, u):
+            if a == 0:
+                banks[b, jb, u] = psum.tile([P, 2 * JB], F32, name="bank")
             cols = slice(jb * JB, (jb + 1) * JB)
             for e in range(2):
                 t = 2 * u + e
                 nc.tensor.matmul_mx(
-                    out=bank[:, e * JB : (e + 1) * JB],
+                    out=banks[b, jb, u][:, e * JB : (e + 1) * JB],
                     lhsT=w1_codes[a, b][:, t * P : (t + 1) * P].bitcast(FP8X4),
                     lhsT_scale=w1_plane[a, b][:, t * P : (t + 1) * P],
                     rhs=v_codes[a][:, cols].bitcast(FP8X4),
@@ -186,57 +151,38 @@ def tile_list_floating_strike_payoffs_kernel(tc, tab_words, tab_scales, offs, w1
                 )
 
         halves = [(b, jc) for b in range(2) for jc in range(S // JC)]
-        th = {(b, jb): keep.tile([P, 2, JB, 2], F32, name="th%d%d" % (b, jb), align_bytes=64) for b in range(2) for jb in range(S // JB)}
+        th = {}
         h_bf = {}
-        reused = {(0, 2): "h_bf01", (1, 2): "h_bf03"}
-        h_codes = {k: keep.tile([P, JC], U32, name="h_codes%d%d" % k, align_bytes=64) for k in halves}
+        h_codes = {}
         h_plane = {k: keep.tile([P, JC], U8, name="h_plane%d%d" % k, align_bytes=64) for k in halves}
 
-        def saturate_bank(bank, b, q):
-            jb, u = divmod(q, 2)
-            if (b, jb) in narrow:
-                nc.scalar.activation(
-                    th[b, jb][:, u].rearrange("p j e -> p (j e)").rearrange("p (j t) -> p j t", t=PACK),
-                    bank[:].rearrange("p (t j) -> p j t", t=PACK),
-                    ACT.Tanh,
-                )
-                return
-            nc.scalar.activation(
-                th[b, jb][:, u, :, :], bank[:].rearrange("p (e j) -> p j e", e=2), ACT.Tanh
-            )
+        def open_block(b, jb):
+            for u in range(2):
+                first_pass(0, b, jb, u)
 
-        def cap_paths(b, j0, n, how="V"):
-            jb, inner = divmod(j0, JB)
-            if (b, jb) not in h_bf:
-                h_bf[b, jb] = keep.tile([P, JB * PACK], BF16, name=reused.get((b, jb), "h_bf%d%d" % (b, jb)), align_bytes=64)
-            dst = h_bf[b, jb][:, inner * PACK : (inner + n) * PACK].rearrange("p (j u e) -> p j u e", u=2, e=2)
-            src = th[b, jb][:, :, inner : inner + n, :].rearrange("p u j e -> p j u e")
-            if (b, jb) in narrow:
-                src = th[b, jb][:].rearrange("p x j e -> p (x j e)").rearrange("p (j u e) -> p j u e", u=2, e=2)[:, inner : inner + n]
-            if how == "W":
-                in_sbuf = caps[:, b : b + 1, 0:PACK].rearrange("p o (u e) -> p o u e", u=2).to_broadcast([P, n, 2, 2])
-                nc.vector.tensor_tensor(dst, src, in_sbuf, ALU.mult)
-            elif how == "V":
-                in_psum = caps_ps[:, b : b + 1, :].rearrange("p o (u e) -> p o u e", u=2).to_broadcast([P, n, 2, 2])
-                nc.vector.tensor_tensor(dst, src, in_psum, ALU.mult)
-            else:
-                rows = "p (x j) u e -> p x (j u e)"
-                nc.gpsimd.tensor_tensor(
-                    dst.rearrange(rows, j=REPEAT),
-                    src.rearrange(rows, j=REPEAT),
-                    caps[:, b : b + 1, :].to_broadcast([P, n // REPEAT, REPEAT * PACK]),
-                    ALU.mult,
-                )
+        def close_block(b, jb):
+            th[b, jb] = late_tile([P, 2, JB, 2], F32, "th%d%d" % (b, jb))
+            for u in range(2):
+                first_pass(1, b, jb, u)
+                nc.scalar.activation(th[b, jb][:, u, :, :], banks[b, jb, u][:].rearrange("p (e j) -> p j e", e=2), ACT.Tanh)
 
-        def quantise_h(b, jb):
+        def cap_block(b, jb):
             jc, part = divmod(jb, 2)
-            cols = slice(part * JB, (part + 1) * JB)
-            nc.vector.quantize_mx(out=h_codes[b, jc][:, cols].bitcast(FP8X4), scales=h_plane[b, jc][:, cols], in_=h_bf[b, jb][:])
+            if part == 0:
+                h_bf[b, jc] = late_tile([P, JC * PACK], BF16, "h_bf%d%d" % (b, jc))
+            dst = h_bf[b, jc][:, part * JB * PACK : (part + 1) * JB * PACK].rearrange("p (j u e) -> p j u e", u=2, e=2)
+            src = th[b, jb][:].rearrange("p u j e -> p j u e")
+            factor = caps[:, b : b + 1, :].rearrange("p o (u e) -> p o u e", u=2).to_broadcast([P, JB, 2, 2])
+            nc.vector.tensor_tensor(dst, src, factor, ALU.mult)
+
+        def quantise_h(b, jc):
+            h_codes[b, jc] = late_tile([P, JC], U32, "h_codes%d%d" % (b, jc))
+            nc.vector.quantize_mx(out=h_codes[b, jc][:].bitcast(FP8X4), scales=h_plane[b, jc][:], in_=h_bf[b, jc][:])
 
         prices = {}
 
         def second_stage(jc, n):
-            bank = ps2.tile([P, JC], F32, name="bank")
+            bank = psum.tile([P, JC], F32, name="bank")
             for b in range(2):
                 nc.tensor.matmul_mx(
                     out=bank[:],
@@ -250,98 +196,67 @@ def tile_list_floating_strike_payoffs_kernel(tc, tab_words, tab_scales, offs, w1
             prices[jc, n] = keep.tile([P, JC], F32, name="price%d%d" % (jc, n), align_bytes=64)
             nc.scalar.activation(prices[jc, n][:], bank[:], ACT.Exp)
 
-        def payoff(j0, n, width, how="S"):
+        def payoff(j0, n, width):
             jc, off = divmod(j0, JC)
-            gap = ring.tile([P, width], F32, name="gap", align_bytes=64, bufs=8)
-            nc.vector.tensor_tensor(gap[:], strikes[n][:].indirect(picks(j0, width)), prices[jc, n][:, off : off + width], ALU.subtract)
-            pay = ring.tile([P, width], F32, name="pay", align_bytes=64)
-            if how == "S":
-                nc.scalar.activation(pay[:], gap[:], ACT.Relu, scale=-1.0)
-            else:
-                nc.vector.tensor_scalar(pay[:], gap[:], -1.0, 0.0, ALU.mult, ALU.max)
-            nc.sync.dma_start(out=out[n * P : (n + 1) * P, j0 : j0 + width], in_=pay[:])
+            price = prices[jc, n][:, off : off + width]
+            gap = ring.tile([P, width], F32, name="gap", align_bytes=64)
+            nc.vector.tensor_tensor(gap[:], strikes[n][:].indirect(picks(j0, width)), price, ALU.subtract)
+            nc.scalar.activation(price, gap[:], ACT.Relu, scale=-1.0)
+            nc.sync.dma_start(out=out[n * P : (n + 1) * P, j0 : j0 + width], in_=price)
 
-        banks = {}
-
-        def open_bank(b, q):
-            banks[b, q] = ps1.tile([P, 2 * JB], F32, name="bank")
-            first_pass(banks[b, q], 0, b, q)
-
-        def close_bank(b, q):
-            if (b, q) not in banks:
-                open_bank(b, q)
-            first_pass(banks[b, q], 1, b, q)
-            saturate_bank(banks[b, q], b, q)
-
-        def close_block(b, jb):
-            close_bank(b, 2 * jb)
-            close_bank(b, 2 * jb + 1)
-
-        def gather_plane():
-            for q in range(4):
-                nc.vector.tensor_copy(tab_plane[32 * q : 32 * q + 8, :].bitcast(I32), tab_rows[32 * q : 32 * q + 8, :])
-            nc.vector.tensor_copy(v_plane[:], tab_plane[:].indirect(offsets[:]))
-
-        gather_plane()
-        gather_words(0, 0, S)
-        caps_to_psum()
         round_w1(0, 0, 0, 64, "S")
-        round_w1(0, 0, 64, 112, "S")
-        round_w1(0, 0, 112, 128, "V")
+        round_w1(0, 0, 64, 128, "S")
+        gather_plane()
         quantise_w1(0, 0)
-        for q in range(4):
-            open_bank(0, q)
-        gather_words(1, 0, S)
+        gather_words(0, 0, 512)
         round_w1(1, 0, 0, 64, "S")
-        round_w1(1, 0, 64, 96, "V")
-        round_w1(1, 0, 96, 128, "S")
-        quantise_w1(1, 0, 0)
-        quantise_w1(1, 0, 1)
-        round_w1(0, 1, 0, 64, "V")
-        round_w1(0, 1, 64, 128, "V")
+        open_block(0, 0)
+        open_block(0, 1)
+        gather_words(0, 512, 512)
+        round_w1(1, 0, 64, 128, "S")
+        open_block(0, 2)
+        open_block(0, 3)
+        quantise_w1(1, 0)
+        gather_words(1, 0, 256)
         close_block(0, 0)
+        gather_words(1, 256, 256)
         close_block(0, 1)
-        cap_paths(0, 0, 256, "W")
-        quantise_w1(0, 1)
-        round_w1(1, 1, 0, 64, "S")
+        gather_words(1, 512, 512)
         close_block(0, 2)
+        round_w1(0, 1, 0, 128, "V")
+        quantise_w1(0, 1)
+        cap_block(0, 0)
+        open_block(1, 0)
+        open_block(1, 1)
+        open_block(1, 2)
+        round_w1(1, 1, 0, 128, "S")
         close_block(0, 3)
-        for q in range(3):
-            open_bank(1, q)
-        cap_paths(0, 256, 256, "W")
-        round_w1(1, 1, 64, 128, "V")
+        cap_block(0, 1)
         quantise_h(0, 0)
-        quantise_w1(1, 1, 0)
-        quantise_w1(1, 1, 1)
-        for jb in range(4):
-            close_block(1, jb)
+        quantise_w1(1, 1)
+        close_block(1, 0)
+        close_block(1, 1)
+        cap_block(0, 2)
+        cap_block(0, 3)
+        open_block(1, 3)
+        close_block(1, 2)
+        close_block(1, 3)
+        cap_block(1, 0)
+        cap_block(1, 1)
         quantise_h(0, 1)
-        cap_paths(0, 512, 256, "G")
-        cap_paths(0, 768, 176)
-        cap_paths(0, 944, 80, "G")
-        cap_paths(1, 0, 256)
-        cap_paths(1, 256, 256)
         quantise_h(1, 0)
-        quantise_h(0, 2)
-        quantise_h(1, 1)
         for n in range(4):
             second_stage(0, n)
-        quantise_h(0, 3)
-        cap_paths(1, 512, 160, "G")
-        cap_paths(1, 768, 256)
-        cap_paths(1, 672, 96)
-        quantise_h(1, 3)
+        cap_block(1, 2)
+        cap_block(1, 3)
+        quantise_h(1, 1)
         payoff(0, 0, 512)
-        quantise_h(1, 2)
         for n in range(4):
             second_stage(1, n)
-
         for n in range(1, 4):
             payoff(0, n, 512)
-        for n in range(2):
+        for n in range(3):
             payoff(512, n, 512)
-        payoff(512, 2, 256)
-        payoff(768, 2, 256)
         payoff(512, 3, 256)
         payoff(768, 3, 128)
         payoff(896, 3, 128)

@@ -22,7 +22,7 @@ PASS = P * PACK
 JB = 256
 JC = 512
 LIST_ROWS = 16
-W1_CUTS = {(0, 0): (0, 64, 128), (1, 0): (0, 64, 128), (0, 1): (0, 128), (1, 1): (0, 128)}
+W1_CUTS = {(0, 0): (0, 128), (1, 0): (0, 128), (0, 1): (0, 128), (1, 1): (0, 128)}
 
 
 def tile_list_floating_strike_payoffs_kernel(tc, tab_words, tab_scales, offs, w1, cap, w4_words, w4_scales, gT, out):
@@ -39,6 +39,7 @@ def tile_list_floating_strike_payoffs_kernel(tc, tab_words, tab_scales, offs, w1
             return offsets[:, j0 // LIST_ROWS : (j0 + n) // LIST_ROWS]
 
         tab_plane = keep.tile([P, T], U8, name="tab_plane", align_bytes=64)
+        tab_rows = keep.tile([P, T // 4], I32, name="tab_rows", align_bytes=64)
         w4_plane = keep.tile([P, 2 * N], U8, name="w4_plane", align_bytes=64)
         nc.vector.memset(tab_plane[:].bitcast(I32), 0)
         nc.vector.memset(w4_plane[:].bitcast(I32), 0)
@@ -49,18 +50,18 @@ def tile_list_floating_strike_payoffs_kernel(tc, tab_words, tab_scales, offs, w1
             for (a, b), cuts in W1_CUTS.items() for m0, m1 in zip(cuts, cuts[1:])
         }
         strikes = [keep.tile([P, T], F32, name="strikes%d" % n, align_bytes=64) for n in range(N // P)]
-        caps = keep.tile([P, 2, PACK], F32, name="caps", align_bytes=64)
+        caps = keep.tile([P, 2, 2 * PACK], F32, name="caps", align_bytes=64)
         w4_codes = keep.tile([P, 2, 2 * N], U8, name="w4_codes", align_bytes=64)
 
         def load_tab_plane():
             for q in range(4):
                 nc.sync.dma_start(
-                    out=tab_plane[32 * q : 32 * q + 8, :].bitcast(I32),
+                    out=tab_rows[32 * q : 32 * q + 8, :],
                     in_=tab_scales[:, 4 * q : 4 * q + 4, :].bitcast(I32),
                 )
 
         def load_caps():
-            nc.sync.dma_start(out=caps[:], in_=cap.rearrange("(b p t) -> p b t", b=2, t=PACK))
+            nc.scalar.dma_start(out=caps[:, :, 0:PACK], in_=cap.rearrange("(b p t) -> p b t", b=2, t=PACK))
 
         def load_tab(a):
             nc.sync.dma_start(out=tab[a][:], in_=tab_words[a].rearrange("p t i -> p (t i)").bitcast(I32))
@@ -84,21 +85,19 @@ def tile_list_floating_strike_payoffs_kernel(tc, tab_words, tab_scales, offs, w1
         def load_strikes(n):
             nc.sync.dma_start(out=strikes[n][:], in_=gT[n * P : (n + 1) * P, :])
 
-        load_w1(0, 0, 0)
         load_tab_plane()
-        load_w1(0, 0, 64)
+        load_caps()
+        load_w1(0, 0, 0)
         load_tab(0)
         load_w1(1, 0, 0)
-        load_w1(1, 0, 64)
         load_tab(1)
-        load_caps()
         load_w1(0, 1)
         load_w1(1, 1)
         load_w4()
         for n in range(4):
             load_strikes(n)
 
-        tenants = {"w1_codes00": "tab_plane", "th03": "raw11_0", "h_bf01": "w1_bf11", "h_codes01": "th10", "h_bf11": "h_bf01", "h_bf00": "raw01_0"}
+        tenants = {"th03": "raw11_0", "h_bf01": "w1_bf11", "h_codes01": "th10", "h_bf11": "h_bf01", "h_bf00": "raw01_0", "v_codes0": "w1_bf00"}
 
         def late_tile(shape, dtype, name):
             return keep.tile(shape, dtype, name=tenants.get(name, name), align_bytes=64)
@@ -110,6 +109,8 @@ def tile_list_floating_strike_payoffs_kernel(tc, tab_words, tab_scales, offs, w1
         w1_plane = {k: keep.tile([P, PASS], U8, name="w1_plane%d%d" % k, align_bytes=64) for k in W1_CUTS}
 
         def gather_plane():
+            for q in range(4):
+                nc.vector.tensor_copy(tab_plane[32 * q : 32 * q + 8, :].bitcast(I32), tab_rows[32 * q : 32 * q + 8, :])
             nc.vector.tensor_copy(v_plane[:], tab_plane[:].indirect(offsets[:]))
 
         def gather_words(a, j0, n):
@@ -172,7 +173,7 @@ def tile_list_floating_strike_payoffs_kernel(tc, tab_words, tab_scales, offs, w1
                 h_bf[b, jc] = late_tile([P, JC * PACK], BF16, "h_bf%d%d" % (b, jc))
             dst = h_bf[b, jc][:, part * JB * PACK : (part + 1) * JB * PACK].rearrange("p (j u e) -> p j u e", u=2, e=2)
             src = th[b, jb][:].rearrange("p u j e -> p j u e")
-            factor = caps[:, b : b + 1, :].rearrange("p o (u e) -> p o u e", u=2).to_broadcast([P, JB, 2, 2])
+            factor = caps[:, b : b + 1, 0:PACK].rearrange("p o (u e) -> p o u e", u=2).to_broadcast([P, JB, 2, 2])
             nc.vector.tensor_tensor(dst, src, factor, ALU.mult)
 
         def quantise_h(b, jc):
@@ -204,16 +205,16 @@ def tile_list_floating_strike_payoffs_kernel(tc, tab_words, tab_scales, offs, w1
             nc.scalar.activation(price, gap[:], ACT.Relu, scale=-1.0)
             nc.sync.dma_start(out=out[n * P : (n + 1) * P, j0 : j0 + width], in_=price)
 
-        round_w1(0, 0, 0, 64, "S")
-        round_w1(0, 0, 64, 128, "S")
+        round_w1(0, 0, 0, 104, "S")
         gather_plane()
+        round_w1(0, 0, 104, 128, "V")
         quantise_w1(0, 0)
         gather_words(0, 0, 512)
-        round_w1(1, 0, 0, 64, "S")
+        round_w1(1, 0, 0, 88, "S")
         open_block(0, 0)
         open_block(0, 1)
         gather_words(0, 512, 512)
-        round_w1(1, 0, 64, 128, "S")
+        round_w1(1, 0, 88, 128, "V")
         open_block(0, 2)
         open_block(0, 3)
         quantise_w1(1, 0)

@@ -1,6 +1,7 @@
 from contextlib import ExitStack
 
 import concourse.mybir as mybir
+from concourse.masks import make_identity
 
 K, T, S, R, N = 1024, 2048, 1024, 1024, 512
 FLOPS = 2 * K * R * S + 2 * R * N * S
@@ -23,14 +24,28 @@ JB = 256
 JC = 512
 LIST_ROWS = 16
 W1_CUTS = {(0, 0): (0, 128), (1, 0): (0, 128), (0, 1): (0, 128), (1, 1): (0, 128)}
+SPLIT = ((0, 0),)
+NARROW = ((0, 1),)
+REPEAT = 16
+FIRST_BANKS = ((0, 1, 2, 3, 4, 5, 0, 1), (6, 2, 3, 4, 5, 0, 6, 3))
+SECOND_BANKS = ((1, 2, 4, 5), (0, 6, 3, 1))
 
 
 def tile_list_floating_strike_payoffs_kernel(tc, tab_words, tab_scales, offs, w1, cap, w4_words, w4_scales, gT, out):
     nc = tc.nc
     with ExitStack() as ctx:
         keep = ctx.enter_context(tc.tile_pool(name="keep", bufs=1))
+        shared = ctx.enter_context(tc.tile_pool(name="shared", bufs=1))
         ring = ctx.enter_context(tc.tile_pool(name="ring", bufs=8))
-        psum = ctx.enter_context(tc.psum_pool(name="psum", bufs=8))
+        psum = ctx.enter_context(tc.psum_pool(name="psum", bufs=1))
+
+        tenants = {"v_codes0": "w1_bf00", "h_codes01": "th10", "h_bf00_0": "raw01_0", "h_bf00_1": "w1_bf01", "h_bf11": "h_bf01"}
+        places = {"raw11_0": 0, "th03": 0, "h_codes00": 4096}
+
+        def late_tile(shape, dtype, name):
+            if name in places:
+                return shared.tile(shape, dtype, name=name, align_bytes=64, offset=places[name])
+            return keep.tile(shape, dtype, name=tenants.get(name, name), align_bytes=64)
 
         offsets = keep.tile([P, S // LIST_ROWS], U16, name="offsets")
         nc.sync.dma_start(offsets[:], offs)
@@ -46,11 +61,16 @@ def tile_list_floating_strike_payoffs_kernel(tc, tab_words, tab_scales, offs, w1
 
         tab = [keep.tile([P, T], I32, name="tab%d" % a, align_bytes=64) for a in range(2)]
         raw = {
-            (a, b, m0): keep.tile([P, PACK, PACK * (m1 - m0)], F32, name="raw%d%d_%d" % (a, b, m0), align_bytes=64)
+            (a, b, m0): late_tile([P, PACK, PACK * (m1 - m0)], F32, "raw%d%d_%d" % (a, b, m0))
             for (a, b), cuts in W1_CUTS.items() for m0, m1 in zip(cuts, cuts[1:])
         }
         strikes = [keep.tile([P, T], F32, name="strikes%d" % n, align_bytes=64) for n in range(N // P)]
-        caps = keep.tile([P, 2, 2 * PACK], F32, name="caps", align_bytes=64)
+        caps = keep.tile([P, 2, REPEAT * PACK], F32, name="caps", align_bytes=64)
+        cap_rows = keep.tile([P, PASS], F32, name="cap_rows", align_bytes=64)
+        identity = keep.tile([P, P], F32, name="identity", align_bytes=64)
+        caps_ps = psum.tile([P, P, PACK], F32, name="bank7")
+        nc.vector.memset(cap_rows[:], 0.0)
+        make_identity(nc, identity[:])
         w4_codes = keep.tile([P, 2, 2 * N], U8, name="w4_codes", align_bytes=64)
 
         def load_tab_plane():
@@ -61,7 +81,16 @@ def tile_list_floating_strike_payoffs_kernel(tc, tab_words, tab_scales, offs, w1
                 )
 
         def load_caps():
-            nc.scalar.dma_start(out=caps[:, :, 0:PACK], in_=cap.rearrange("(b p t) -> p b t", b=2, t=PACK))
+            nc.sync.dma_start(out=cap_rows[0:2, :], in_=cap.rearrange("(b c) -> b c", b=2))
+
+        def spread_caps():
+            for t in range(PACK):
+                nc.tensor.transpose(caps_ps[:, :, t], cap_rows[:, t:PASS:PACK], identity[:])
+            nc.scalar.activation(
+                caps[:].rearrange("p b (j t) -> p b j t", t=PACK),
+                caps_ps[:, 0:2, :].unsqueeze(2).to_broadcast([P, 2, REPEAT, PACK]),
+                ACT.Copy,
+            )
 
         def load_tab(a):
             nc.sync.dma_start(out=tab[a][:], in_=tab_words[a].rearrange("p t i -> p (t i)").bitcast(I32))
@@ -86,8 +115,8 @@ def tile_list_floating_strike_payoffs_kernel(tc, tab_words, tab_scales, offs, w1
             nc.sync.dma_start(out=strikes[n][:], in_=gT[n * P : (n + 1) * P, :])
 
         load_tab_plane()
-        load_caps()
         load_w1(0, 0, 0)
+        load_caps()
         load_tab(0)
         load_w1(1, 0, 0)
         load_tab(1)
@@ -96,11 +125,6 @@ def tile_list_floating_strike_payoffs_kernel(tc, tab_words, tab_scales, offs, w1
         load_w4()
         for n in range(4):
             load_strikes(n)
-
-        tenants = {"th03": "raw11_0", "h_bf01": "w1_bf11", "h_codes01": "th10", "h_bf11": "h_bf01", "h_bf00": "raw01_0", "v_codes0": "w1_bf00"}
-
-        def late_tile(shape, dtype, name):
-            return keep.tile(shape, dtype, name=tenants.get(name, name), align_bytes=64)
 
         v_codes = {}
         v_plane = keep.tile([P, S], U8, name="v_plane", align_bytes=64)
@@ -137,7 +161,20 @@ def tile_list_floating_strike_payoffs_kernel(tc, tab_words, tab_scales, offs, w1
 
         def first_pass(a, b, jb, u):
             if a == 0:
-                banks[b, jb, u] = psum.tile([P, 2 * JB], F32, name="bank")
+                banks[b, jb, u] = psum.tile([P, 2 * JB], F32, name="bank%d" % FIRST_BANKS[b][2 * jb + u])
+            if (b, jb) in NARROW:
+                cols = slice(jb * JB + u * P, jb * JB + (u + 1) * P)
+                for t in range(PACK):
+                    nc.tensor.matmul_mx(
+                        out=banks[b, jb, u][:, t * P : (t + 1) * P],
+                        lhsT=w1_codes[a, b][:, t * P : (t + 1) * P].bitcast(FP8X4),
+                        lhsT_scale=w1_plane[a, b][:, t * P : (t + 1) * P],
+                        rhs=v_codes[a][:, cols].bitcast(FP8X4),
+                        rhs_scale=v_plane[4 * a :, cols],
+                        start=(a == 0 and t == 0),
+                        stop=(a == 1 and t == PACK - 1),
+                    )
+                return
             cols = slice(jb * JB, (jb + 1) * JB)
             for e in range(2):
                 t = 2 * u + e
@@ -165,25 +202,59 @@ def tile_list_floating_strike_payoffs_kernel(tc, tab_words, tab_scales, offs, w1
             th[b, jb] = late_tile([P, 2, JB, 2], F32, "th%d%d" % (b, jb))
             for u in range(2):
                 first_pass(1, b, jb, u)
-                nc.scalar.activation(th[b, jb][:, u, :, :], banks[b, jb, u][:].rearrange("p (e j) -> p j e", e=2), ACT.Tanh)
+                if (b, jb) in NARROW:
+                    dst = th[b, jb][:, u].rearrange("p j e -> p (j e)").rearrange("p (j t) -> p j t", t=PACK)
+                    nc.scalar.activation(dst, banks[b, jb, u][:].rearrange("p (t j) -> p j t", t=PACK), ACT.Tanh)
+                else:
+                    nc.scalar.activation(th[b, jb][:, u, :, :], banks[b, jb, u][:].rearrange("p (e j) -> p j e", e=2), ACT.Tanh)
 
-        def cap_block(b, jb):
+        def h_block(b, jb):
             jc, part = divmod(jb, 2)
-            if part == 0:
+            if (b, jc) in SPLIT:
+                if (b, jc, part) not in h_bf:
+                    h_bf[b, jc, part] = late_tile([P, JB * PACK], BF16, "h_bf%d%d_%d" % (b, jc, part))
+                return h_bf[b, jc, part][:]
+            if (b, jc) not in h_bf:
                 h_bf[b, jc] = late_tile([P, JC * PACK], BF16, "h_bf%d%d" % (b, jc))
-            dst = h_bf[b, jc][:, part * JB * PACK : (part + 1) * JB * PACK].rearrange("p (j u e) -> p j u e", u=2, e=2)
-            src = th[b, jb][:].rearrange("p u j e -> p j u e")
-            factor = caps[:, b : b + 1, 0:PACK].rearrange("p o (u e) -> p o u e", u=2).to_broadcast([P, JB, 2, 2])
+            return h_bf[b, jc][:, part * JB * PACK : (part + 1) * JB * PACK]
+
+        def cap_block_gpsimd(b, jb):
+            row = REPEAT * PACK
+            dst = h_block(b, jb).rearrange("p (x c) -> p x c", c=row)
+            src = th[b, jb][:].rearrange("p u j e -> p (u j e)").rearrange("p (x c) -> p x c", c=row)
+            nc.gpsimd.tensor_tensor(dst, src, caps[:, b : b + 1, :].to_broadcast([P, JB // REPEAT, row]), ALU.mult)
+
+        def cap_block(b, jb, j0=0, j1=JB, source=caps):
+            dst = h_block(b, jb).rearrange("p (j u e) -> p j u e", u=2, e=2)[:, j0:j1]
+            src = th[b, jb][:].rearrange("p u j e -> p j u e")[:, j0:j1]
+            factor = source[:, b : b + 1, 0:PACK].rearrange("p o (u e) -> p o u e", u=2).to_broadcast([P, j1 - j0, 2, 2])
             nc.vector.tensor_tensor(dst, src, factor, ALU.mult)
 
-        def quantise_h(b, jc):
-            h_codes[b, jc] = late_tile([P, JC], U32, "h_codes%d%d" % (b, jc))
-            nc.vector.quantize_mx(out=h_codes[b, jc][:].bitcast(FP8X4), scales=h_plane[b, jc][:], in_=h_bf[b, jc][:])
+        scaled = {}
+
+        def scale_block(b, jb, j0=0, j1=JB):
+            scaled[b, jb] = late_tile([P, PACK, j1 - j0], BF16, "scaled%d%d" % (b, jb))
+            for t in range(PACK):
+                u, e = divmod(t, 2)
+                nc.scalar.activation(scaled[b, jb][:, t, :], th[b, jb][:, u, j0:j1, e], ACT.Copy, scale=caps[:, b, t : t + 1])
+
+        def weave_block(b, jb, j0=0, j1=JB):
+            dst = h_block(b, jb).rearrange("p (j t) -> p j t", t=PACK)[:, j0:j1]
+            nc.scalar.copy(dst, scaled[b, jb][:].rearrange("p t j -> p j t"))
+
+        def quantise_h(b, jc, part=None):
+            if (b, jc) not in h_codes:
+                h_codes[b, jc] = late_tile([P, JC], U32, "h_codes%d%d" % (b, jc))
+            if part is None:
+                nc.vector.quantize_mx(out=h_codes[b, jc][:].bitcast(FP8X4), scales=h_plane[b, jc][:], in_=h_bf[b, jc][:])
+            else:
+                cols = slice(part * JB, (part + 1) * JB)
+                nc.vector.quantize_mx(out=h_codes[b, jc][:, cols].bitcast(FP8X4), scales=h_plane[b, jc][:, cols], in_=h_block(b, 2 * jc + part))
 
         prices = {}
 
         def second_stage(jc, n):
-            bank = psum.tile([P, JC], F32, name="bank")
+            bank = psum.tile([P, JC], F32, name="bank%d" % SECOND_BANKS[jc][n])
             for b in range(2):
                 nc.tensor.matmul_mx(
                     out=bank[:],
@@ -209,6 +280,7 @@ def tile_list_floating_strike_payoffs_kernel(tc, tab_words, tab_scales, offs, w1
         gather_plane()
         round_w1(0, 0, 104, 128, "V")
         quantise_w1(0, 0)
+        spread_caps()
         gather_words(0, 0, 512)
         round_w1(1, 0, 0, 88, "S")
         open_block(0, 0)
@@ -216,7 +288,6 @@ def tile_list_floating_strike_payoffs_kernel(tc, tab_words, tab_scales, offs, w1
         gather_words(0, 512, 512)
         round_w1(1, 0, 88, 128, "V")
         open_block(0, 2)
-        open_block(0, 3)
         quantise_w1(1, 0)
         gather_words(1, 0, 256)
         close_block(0, 0)
@@ -224,34 +295,38 @@ def tile_list_floating_strike_payoffs_kernel(tc, tab_words, tab_scales, offs, w1
         close_block(0, 1)
         gather_words(1, 512, 512)
         close_block(0, 2)
+        open_block(0, 3)
         round_w1(0, 1, 0, 128, "V")
         quantise_w1(0, 1)
-        cap_block(0, 0)
-        open_block(1, 0)
-        open_block(1, 1)
-        open_block(1, 2)
+        cap_block_gpsimd(0, 1)
+        cap_block(0, 0, source=caps_ps)
+        cap_block(0, 2, source=caps_ps)
         round_w1(1, 1, 0, 128, "S")
         close_block(0, 3)
-        cap_block(0, 1)
-        quantise_h(0, 0)
+        open_block(1, 0)
+        open_block(1, 1)
         quantise_w1(1, 1)
         close_block(1, 0)
         close_block(1, 1)
-        cap_block(0, 2)
+        quantise_h(0, 0, 0)
+        quantise_h(0, 0, 1)
         cap_block(0, 3)
-        open_block(1, 3)
+        open_block(1, 2)
         close_block(1, 2)
+        open_block(1, 3)
         close_block(1, 3)
         cap_block(1, 0)
         cap_block(1, 1)
         quantise_h(0, 1)
         quantise_h(1, 0)
+        scale_block(1, 3, 128, 256)
+        weave_block(1, 3, 128, 256)
         for n in range(4):
             second_stage(0, n)
         cap_block(1, 2)
-        cap_block(1, 3)
-        quantise_h(1, 1)
+        cap_block(1, 3, 0, 128)
         payoff(0, 0, 512)
+        quantise_h(1, 1)
         for n in range(4):
             second_stage(1, n)
         for n in range(1, 4):

@@ -24,8 +24,9 @@ JB = 256
 JC = 512
 LIST_ROWS = 16
 W1_CUTS = {(0, 0): (0, 128), (1, 0): (0, 128), (0, 1): (0, 128), (1, 1): (0, 128)}
-SPLIT = ((0, 0),)
-NARROW = ((0, 1),)
+SPLIT = ((0, 0), (0, 1))
+NARROW = ((0, 3), (1, 2))
+PARTED = ()
 REPEAT = 16
 FIRST_BANKS = ((0, 1, 2, 3, 4, 5, 0, 1), (6, 2, 3, 4, 5, 0, 6, 3))
 SECOND_BANKS = ((1, 2, 4, 5), (0, 6, 3, 1))
@@ -39,8 +40,8 @@ def tile_list_floating_strike_payoffs_kernel(tc, tab_words, tab_scales, offs, w1
         ring = ctx.enter_context(tc.tile_pool(name="ring", bufs=8))
         psum = ctx.enter_context(tc.psum_pool(name="psum", bufs=1))
 
-        tenants = {"v_codes0": "w1_bf00", "h_codes01": "th10", "h_bf00_0": "raw01_0", "h_bf00_1": "w1_bf01", "h_bf11": "h_bf01"}
-        places = {"raw11_0": 0, "th03": 0, "h_codes00": 4096}
+        tenants = {"v_codes0": "w1_bf00", "h_codes01": "th10", "h_bf00_0": "raw01_0", "h_bf01_1": "h_bf00_1", "h_bf11": "h_bf10"}
+        places = {"raw11_0": 0, "th03": 0, "h_bf01_0": 4096, "h_codes00": 6144}
 
         def late_tile(shape, dtype, name):
             if name in places:
@@ -198,12 +199,15 @@ def tile_list_floating_strike_payoffs_kernel(tc, tab_words, tab_scales, offs, w1
             for u in range(2):
                 first_pass(0, b, jb, u)
 
-        def close_block(b, jb):
-            th[b, jb] = late_tile([P, 2, JB, 2], F32, "th%d%d" % (b, jb))
-            for u in range(2):
+        def close_block(b, jb, halves=(0, 1)):
+            if (b, jb) not in PARTED:
+                th[b, jb] = late_tile([P, 2, JB, 2], F32, "th%d%d" % (b, jb))
+            for u in halves:
                 first_pass(1, b, jb, u)
+                if (b, jb) in PARTED:
+                    th[b, jb, u] = late_tile([P, P * PACK], F32, "th%d%d_%d" % (b, jb, u))
                 if (b, jb) in NARROW:
-                    dst = th[b, jb][:, u].rearrange("p j e -> p (j e)").rearrange("p (j t) -> p j t", t=PACK)
+                    dst = narrow_values(b, jb, u * P, (u + 1) * P).rearrange("p (j t) -> p j t", t=PACK)
                     nc.scalar.activation(dst, banks[b, jb, u][:].rearrange("p (t j) -> p j t", t=PACK), ACT.Tanh)
                 else:
                     nc.scalar.activation(th[b, jb][:, u, :, :], banks[b, jb, u][:].rearrange("p (e j) -> p j e", e=2), ACT.Tanh)
@@ -218,15 +222,24 @@ def tile_list_floating_strike_payoffs_kernel(tc, tab_words, tab_scales, offs, w1
                 h_bf[b, jc] = late_tile([P, JC * PACK], BF16, "h_bf%d%d" % (b, jc))
             return h_bf[b, jc][:, part * JB * PACK : (part + 1) * JB * PACK]
 
-        def cap_block_gpsimd(b, jb):
+        def narrow_values(b, jb, j0, j1):
+            if (b, jb) in PARTED:
+                u = j0 // P
+                return th[b, jb, u][:, (j0 - u * P) * PACK : (j1 - u * P) * PACK]
+            return th[b, jb][:].rearrange("p u j e -> p (u j e)")[:, j0 * PACK : j1 * PACK]
+
+        def cap_block_gpsimd(b, jb, j0=0, j1=JB):
             row = REPEAT * PACK
-            dst = h_block(b, jb).rearrange("p (x c) -> p x c", c=row)
-            src = th[b, jb][:].rearrange("p u j e -> p (u j e)").rearrange("p (x c) -> p x c", c=row)
-            nc.gpsimd.tensor_tensor(dst, src, caps[:, b : b + 1, :].to_broadcast([P, JB // REPEAT, row]), ALU.mult)
+            dst = h_block(b, jb)[:, j0 * PACK : j1 * PACK].rearrange("p (x c) -> p x c", c=row)
+            src = narrow_values(b, jb, j0, j1).rearrange("p (x c) -> p x c", c=row)
+            nc.gpsimd.tensor_tensor(dst, src, caps[:, b : b + 1, :].to_broadcast([P, (j1 - j0) // REPEAT, row]), ALU.mult)
 
         def cap_block(b, jb, j0=0, j1=JB, source=caps):
             dst = h_block(b, jb).rearrange("p (j u e) -> p j u e", u=2, e=2)[:, j0:j1]
-            src = th[b, jb][:].rearrange("p u j e -> p j u e")[:, j0:j1]
+            if (b, jb) in NARROW:
+                src = narrow_values(b, jb, j0, j1).rearrange("p (j u e) -> p j u e", u=2, e=2)
+            else:
+                src = th[b, jb][:].rearrange("p u j e -> p j u e")[:, j0:j1]
             factor = source[:, b : b + 1, 0:PACK].rearrange("p o (u e) -> p o u e", u=2).to_broadcast([P, j1 - j0, 2, 2])
             nc.vector.tensor_tensor(dst, src, factor, ALU.mult)
 
@@ -268,6 +281,19 @@ def tile_list_floating_strike_payoffs_kernel(tc, tab_words, tab_scales, offs, w1
             prices[jc, n] = keep.tile([P, JC], F32, name="price%d%d" % (jc, n), align_bytes=64)
             nc.scalar.activation(prices[jc, n][:], bank[:], ACT.Exp)
 
+        picked = {}
+
+        def pick_strikes(jc, n):
+            picked[jc, n] = late_tile([P, JC], F32, "picked%d%d" % (jc, n))
+            nc.vector.tensor_copy(picked[jc, n][:], strikes[n][:].indirect(picks(jc * JC, JC)))
+
+        def settle(jc, n, engine, c0=0, c1=JC):
+            price = prices[jc, n][:, c0:c1]
+            gap = picked[jc, n][:, c0:c1]
+            engine.tensor_tensor(gap, price, gap, ALU.subtract)
+            nc.scalar.activation(price, gap, ACT.Relu)
+            nc.sync.dma_start(out=out[n * P : (n + 1) * P, jc * JC + c0 : jc * JC + c1], in_=price)
+
         def payoff(j0, n, width):
             jc, off = divmod(j0, JC)
             price = prices[jc, n][:, off : off + width]
@@ -298,9 +324,8 @@ def tile_list_floating_strike_payoffs_kernel(tc, tab_words, tab_scales, offs, w1
         open_block(0, 3)
         round_w1(0, 1, 0, 128, "V")
         quantise_w1(0, 1)
-        cap_block_gpsimd(0, 1)
-        cap_block(0, 0, source=caps_ps)
-        cap_block(0, 2, source=caps_ps)
+        cap_block(0, 1)
+        cap_block(0, 0)
         round_w1(1, 1, 0, 128, "S")
         close_block(0, 3)
         open_block(1, 0)
@@ -310,21 +335,22 @@ def tile_list_floating_strike_payoffs_kernel(tc, tab_words, tab_scales, offs, w1
         close_block(1, 1)
         quantise_h(0, 0, 0)
         quantise_h(0, 0, 1)
-        cap_block(0, 3)
+        cap_block_gpsimd(0, 3)
+        cap_block(0, 2, source=caps_ps)
         open_block(1, 2)
         close_block(1, 2)
         open_block(1, 3)
         close_block(1, 3)
-        cap_block(1, 0)
-        cap_block(1, 1)
-        quantise_h(0, 1)
+        cap_block(1, 0, source=caps_ps)
+        cap_block(1, 1, source=caps_ps)
+        quantise_h(0, 1, 0)
+        quantise_h(0, 1, 1)
         quantise_h(1, 0)
-        scale_block(1, 3, 128, 256)
-        weave_block(1, 3, 128, 256)
         for n in range(4):
             second_stage(0, n)
-        cap_block(1, 2)
-        cap_block(1, 3, 0, 128)
+        cap_block_gpsimd(1, 2, 128, 256)
+        cap_block(1, 2, 0, 128, source=caps_ps)
+        cap_block(1, 3, source=caps_ps)
         payoff(0, 0, 512)
         quantise_h(1, 1)
         for n in range(4):

@@ -24,12 +24,12 @@ JB = 256
 JC = 512
 LIST_ROWS = 16
 W1_CUTS = {(0, 0): (0, 128), (1, 0): (0, 128), (0, 1): (0, 128), (1, 1): (0, 128)}
-SPLIT = ((0, 0), (0, 1))
-NARROW = ((0, 3), (1, 2))
+SPLIT = ((0, 1),)
+NARROW = ((0, 2), (0, 3), (1, 1), (1, 2))
 PARTED = ()
 REPEAT = 16
-FIRST_BANKS = ((0, 1, 2, 3, 4, 5, 0, 1), (6, 2, 3, 4, 5, 0, 6, 3))
-SECOND_BANKS = ((1, 2, 4, 5), (0, 6, 3, 1))
+FIRST_BANKS = ((0, 1, 2, 3, 4, 5, 4, 5), (6, 0, 1, 2, 3, 4, 0, 2))
+SECOND_BANKS = ((5, 6, 1, 3), (4, 0, 2, 5))
 
 
 def tile_list_floating_strike_payoffs_kernel(tc, tab_words, tab_scales, offs, w1, cap, w4_words, w4_scales, gT, out):
@@ -40,8 +40,8 @@ def tile_list_floating_strike_payoffs_kernel(tc, tab_words, tab_scales, offs, w1
         ring = ctx.enter_context(tc.tile_pool(name="ring", bufs=8))
         psum = ctx.enter_context(tc.psum_pool(name="psum", bufs=1))
 
-        tenants = {"v_codes0": "w1_bf00", "h_codes01": "th10", "h_bf00_0": "raw01_0", "h_bf01_1": "h_bf00_1", "h_bf11": "h_bf10"}
-        places = {"raw11_0": 0, "th03": 0, "h_bf01_0": 4096, "h_codes00": 6144}
+        tenants = {"v_codes0": "w1_bf00", "h_bf00": "raw01_0", "h_bf01_0": "w1_bf01", "h_bf01_1": "raw01_0", "picked00": "w1_bf11", "h_codes01": "th11", "h_bf11": "h_bf10"}
+        places = {"raw11_0": 0, "th03": 0, "h_codes00": 6144}
 
         def late_tile(shape, dtype, name):
             if name in places:
@@ -123,8 +123,9 @@ def tile_list_floating_strike_payoffs_kernel(tc, tab_words, tab_scales, offs, w1
         load_tab(1)
         load_w1(0, 1)
         load_w1(1, 1)
+        load_strikes(0)
         load_w4()
-        for n in range(4):
+        for n in range(1, 4):
             load_strikes(n)
 
         v_codes = {}
@@ -151,6 +152,8 @@ def tile_list_floating_strike_payoffs_kernel(tc, tab_words, tab_scales, offs, w1
             src = raw[a, b, u][:].rearrange("p i (m t) -> p m i t", t=PACK)[:, m0 - u : m1 - u]
             if how == "S":
                 nc.scalar.activation(dst, src, ACT.Copy)
+            elif how == "G":
+                nc.gpsimd.tensor_copy(dst.rearrange("p m i t -> p t m i"), src.rearrange("p m i t -> p t m i"))
             else:
                 nc.vector.tensor_copy(dst, src)
 
@@ -195,8 +198,8 @@ def tile_list_floating_strike_payoffs_kernel(tc, tab_words, tab_scales, offs, w1
         h_codes = {}
         h_plane = {k: keep.tile([P, JC], U8, name="h_plane%d%d" % k, align_bytes=64) for k in halves}
 
-        def open_block(b, jb):
-            for u in range(2):
+        def open_block(b, jb, halves=(0, 1)):
+            for u in halves:
                 first_pass(0, b, jb, u)
 
         def close_block(b, jb, halves=(0, 1)):
@@ -294,13 +297,15 @@ def tile_list_floating_strike_payoffs_kernel(tc, tab_words, tab_scales, offs, w1
             nc.scalar.activation(price, gap, ACT.Relu)
             nc.sync.dma_start(out=out[n * P : (n + 1) * P, jc * JC + c0 : jc * JC + c1], in_=price)
 
-        def payoff(j0, n, width):
+        def payoff(j0, n, width, queue=nc.sync):
             jc, off = divmod(j0, JC)
             price = prices[jc, n][:, off : off + width]
             gap = ring.tile([P, width], F32, name="gap", align_bytes=64)
             nc.vector.tensor_tensor(gap[:], strikes[n][:].indirect(picks(j0, width)), price, ALU.subtract)
-            nc.scalar.activation(price, gap[:], ACT.Relu, scale=-1.0)
-            nc.sync.dma_start(out=out[n * P : (n + 1) * P, j0 : j0 + width], in_=price)
+            name = "pay%d_%d" % (j0, n)
+            pay = late_tile([P, width], F32, name)[:] if name in tenants or name in places else price
+            nc.scalar.activation(pay, gap[:], ACT.Relu, scale=-1.0)
+            queue.dma_start(out=out[n * P : (n + 1) * P, j0 : j0 + width], in_=pay)
 
         round_w1(0, 0, 0, 104, "S")
         gather_plane()
@@ -321,37 +326,39 @@ def tile_list_floating_strike_payoffs_kernel(tc, tab_words, tab_scales, offs, w1
         close_block(0, 1)
         gather_words(1, 512, 512)
         close_block(0, 2)
-        open_block(0, 3)
         round_w1(0, 1, 0, 128, "V")
         quantise_w1(0, 1)
-        cap_block(0, 1)
-        cap_block(0, 0)
+        cap_block_gpsimd(0, 2)
+        cap_block(0, 0, source=caps_ps)
+        cap_block(0, 1, source=caps_ps)
         round_w1(1, 1, 0, 128, "S")
-        close_block(0, 3)
         open_block(1, 0)
         open_block(1, 1)
+        open_block(1, 2, (0,))
+        open_block(0, 3)
+        close_block(0, 3)
         quantise_w1(1, 1)
         close_block(1, 0)
         close_block(1, 1)
-        quantise_h(0, 0, 0)
-        quantise_h(0, 0, 1)
+        quantise_h(0, 0)
         cap_block_gpsimd(0, 3)
-        cap_block(0, 2, source=caps_ps)
-        open_block(1, 2)
+        pick_strikes(0, 0)
+        open_block(1, 2, (1,))
         close_block(1, 2)
         open_block(1, 3)
         close_block(1, 3)
         cap_block(1, 0, source=caps_ps)
-        cap_block(1, 1, source=caps_ps)
+        cap_block_gpsimd(1, 1, 0, 64)
+        cap_block(1, 1, 64, 256, source=caps_ps)
+        quantise_h(1, 0)
         quantise_h(0, 1, 0)
         quantise_h(0, 1, 1)
-        quantise_h(1, 0)
         for n in range(4):
             second_stage(0, n)
-        cap_block_gpsimd(1, 2, 128, 256)
-        cap_block(1, 2, 0, 128, source=caps_ps)
+        cap_block_gpsimd(1, 2, 96, 256)
+        cap_block(1, 2, 0, 96, source=caps_ps)
         cap_block(1, 3, source=caps_ps)
-        payoff(0, 0, 512)
+        settle(0, 0, nc.vector)
         quantise_h(1, 1)
         for n in range(4):
             second_stage(1, n)
@@ -361,4 +368,4 @@ def tile_list_floating_strike_payoffs_kernel(tc, tab_words, tab_scales, offs, w1
             payoff(512, n, 512)
         payoff(512, 3, 256)
         payoff(768, 3, 128)
-        payoff(896, 3, 128)
+        payoff(896, 3, 128, nc.scalar)

@@ -29,7 +29,7 @@ NARROW = ((0, 2), (0, 3), (1, 1), (1, 2))
 PARTED = ()
 REPEAT = 16
 FIRST_BANKS = ((0, 1, 2, 3, 4, 5, 4, 5), (6, 0, 1, 2, 3, 4, 0, 2))
-SECOND_BANKS = ((5, 6, 1, 3), (4, 0, 2, 5))
+SECOND_BANKS = ((6, 1, 3, 4), (0, 2, 6, 1))
 
 
 def tile_list_floating_strike_payoffs_kernel(tc, tab_words, tab_scales, offs, w1, cap, w4_words, w4_scales, gT, out):
@@ -40,7 +40,7 @@ def tile_list_floating_strike_payoffs_kernel(tc, tab_words, tab_scales, offs, w1
         ring = ctx.enter_context(tc.tile_pool(name="ring", bufs=8))
         psum = ctx.enter_context(tc.psum_pool(name="psum", bufs=1))
 
-        tenants = {"v_codes0": "w1_bf00", "h_bf00": "raw01_0", "h_bf01_0": "w1_bf01", "h_bf01_1": "raw01_0", "picked00": "w1_bf11", "h_codes01": "th11", "h_bf11": "h_bf10"}
+        tenants = {"v_codes0": "w1_bf00", "h_bf00": "raw01_0", "h_bf01_0": "w1_bf01", "h_bf01_1": "raw01_0", "picked00": "w1_bf11", "h_codes01": "w1_codes11", "h_bf11": "h_bf10", "negated00": "w1_codes01", "pay00": "w1_bf11", "pay0_2": "h_codes11", "pay0_3": "w1_codes11"}
         places = {"raw11_0": 0, "th03": 0, "h_codes00": 6144}
 
         def late_tile(shape, dtype, name):
@@ -297,6 +297,44 @@ def tile_list_floating_strike_payoffs_kernel(tc, tab_words, tab_scales, offs, w1
             nc.scalar.activation(price, gap, ACT.Relu)
             nc.sync.dma_start(out=out[n * P : (n + 1) * P, jc * JC + c0 : jc * JC + c1], in_=price)
 
+        negated = {}
+
+        def turn_strikes(jc, n, bank_name):
+            bank = psum.tile([P, JC], F32, name=bank_name)
+            for q in range(JC // P):
+                nc.tensor.transpose(bank[:, q * P : (q + 1) * P], picked[jc, n][:, q * P : (q + 1) * P], identity[:])
+            negated[jc, n] = late_tile([P, JC], F32, "negated%d%d" % (jc, n))
+            nc.scalar.activation(negated[jc, n][:], bank[:], ACT.Copy, scale=-1.0)
+
+        def second_stage_turned(jc, n):
+            bank = psum.tile([P, JC], F32, name="bank%d" % SECOND_BANKS[jc][n])
+            for b in range(2):
+                for q in range(JC // P):
+                    nc.tensor.matmul_mx(
+                        out=bank[:, q * P : (q + 1) * P],
+                        lhsT=h_codes[b, jc][:, q * P : (q + 1) * P].bitcast(FP8X4),
+                        lhsT_scale=h_plane[b, jc][:, q * P : (q + 1) * P],
+                        rhs=w4_codes[:, b, 2 * n * P : 2 * (n + 1) * P].bitcast(FP4X4),
+                        rhs_scale=w4_plane[:, b * N + n * P : b * N + (n + 1) * P],
+                        start=(b == 0 and q == 0),
+                        stop=(b == 1 and q == JC // P - 1),
+                    )
+            prices[jc, n] = keep.tile([P, JC], F32, name="price%d%d" % (jc, n), align_bytes=64)
+            nc.scalar.activation(prices[jc, n][:], bank[:], ACT.Exp)
+
+        def settle_turned(jc, n, bank_name):
+            bank = psum.tile([P, JC], F32, name=bank_name)
+            terms = (negated[jc, n], prices[jc, n])
+            for k, term in enumerate(terms):
+                for q in range(JC // P):
+                    nc.tensor.matmul(
+                        bank[:, q * P : (q + 1) * P], term[:, q * P : (q + 1) * P], identity[:],
+                        start=(k == 0 and q == 0), stop=(k == 1 and q == JC // P - 1), is_transpose=True,
+                    )
+            pay = late_tile([P, JC], F32, "pay%d%d" % (jc, n))
+            nc.scalar.activation(pay[:], bank[:], ACT.Relu)
+            nc.sync.dma_start(out=out[n * P : (n + 1) * P, jc * JC : (jc + 1) * JC], in_=pay[:])
+
         def payoff(j0, n, width, queue=nc.sync):
             jc, off = divmod(j0, JC)
             price = prices[jc, n][:, off : off + width]
@@ -350,19 +388,22 @@ def tile_list_floating_strike_payoffs_kernel(tc, tab_words, tab_scales, offs, w1
         cap_block(1, 0, source=caps_ps)
         cap_block_gpsimd(1, 1, 0, 64)
         cap_block(1, 1, 64, 256, source=caps_ps)
-        quantise_h(1, 0)
+        turn_strikes(0, 0, "bank5")
         quantise_h(0, 1, 0)
+        quantise_h(1, 0)
         quantise_h(0, 1, 1)
-        for n in range(4):
+        for n in range(1, 4):
             second_stage(0, n)
-        cap_block_gpsimd(1, 2, 96, 256)
-        cap_block(1, 2, 0, 96, source=caps_ps)
+        second_stage_turned(0, 0)
+        settle_turned(0, 0, "bank5")
+        cap_block_gpsimd(1, 2, 112, 256)
+        cap_block(1, 2, 0, 112, source=caps_ps)
         cap_block(1, 3, source=caps_ps)
-        settle(0, 0, nc.vector)
+        payoff(0, 1, 512)
         quantise_h(1, 1)
         for n in range(4):
             second_stage(1, n)
-        for n in range(1, 4):
+        for n in range(2, 4):
             payoff(0, n, 512)
         for n in range(3):
             payoff(512, n, 512)

@@ -40,8 +40,8 @@ def tile_list_floating_strike_payoffs_kernel(tc, tab_words, tab_scales, offs, w1
         ring = ctx.enter_context(tc.tile_pool(name="ring", bufs=8))
         psum = ctx.enter_context(tc.psum_pool(name="psum", bufs=1))
 
-        tenants = {"v_codes0": "w1_bf00", "h_bf00": "raw01_0", "h_bf01_0": "w1_bf01", "h_bf01_1": "raw01_0", "picked00": "w1_bf11", "h_codes01": "w1_codes11", "h_bf11": "h_bf10", "negated00": "w1_codes01", "pay00": "w1_bf11", "pay0_2": "h_codes11", "pay0_3": "w1_codes11"}
-        places = {"raw11_0": 0, "th03": 0, "h_codes00": 6144}
+        tenants = {"v_codes0": "w1_bf00", "h_bf01_1": "w1_bf11", "h_codes01": "w1_codes11", "h_bf11": "h_bf10", "negated00": "w1_codes01", "pay0_2": "h_codes11", "pay0_3": "w1_codes11", "h_bf00": "raw01_0", "h_bf01_0": "w1_bf01"}
+        places = {"raw11_0": 0, "th03": 0, "picked00": 4096, "pay00": 4096, "h_codes00": 6144}
 
         def late_tile(shape, dtype, name):
             if name in places:
@@ -157,9 +157,15 @@ def tile_list_floating_strike_payoffs_kernel(tc, tab_words, tab_scales, offs, w1
             else:
                 nc.vector.tensor_copy(dst, src)
 
-        def quantise_w1(a, b):
+        def quantise_w1(a, b, pieces=1):
             w1_codes[a, b] = late_tile([P, PASS], U32, "w1_codes%d%d" % (a, b))
-            nc.vector.quantize_mx(out=w1_codes[a, b][:].bitcast(FP8X4), scales=w1_plane[a, b][:], in_=w1_bf[a, b][:])
+            width = PASS // pieces
+            for c0 in range(0, PASS, width):
+                nc.vector.quantize_mx(
+                    out=w1_codes[a, b][:, c0 : c0 + width].bitcast(FP8X4),
+                    scales=w1_plane[a, b][:, c0 : c0 + width],
+                    in_=w1_bf[a, b][:, PACK * c0 : PACK * (c0 + width)],
+                )
 
         banks = {}
 
@@ -350,9 +356,10 @@ def tile_list_floating_strike_payoffs_kernel(tc, tab_words, tab_scales, offs, w1
         round_w1(0, 0, 104, 128, "V")
         quantise_w1(0, 0)
         spread_caps()
-        gather_words(0, 0, 512)
-        round_w1(1, 0, 0, 88, "S")
+        gather_words(0, 0, 256)
         open_block(0, 0)
+        gather_words(0, 256, 256)
+        round_w1(1, 0, 0, 88, "S")
         open_block(0, 1)
         gather_words(0, 512, 512)
         round_w1(1, 0, 88, 128, "V")
@@ -366,16 +373,17 @@ def tile_list_floating_strike_payoffs_kernel(tc, tab_words, tab_scales, offs, w1
         close_block(0, 2)
         round_w1(0, 1, 0, 128, "V")
         quantise_w1(0, 1)
-        cap_block_gpsimd(0, 2)
+        cap_block_gpsimd(0, 2, 32, 256)
         cap_block(0, 0, source=caps_ps)
         cap_block(0, 1, source=caps_ps)
+        cap_block(0, 2, 0, 32, source=caps_ps)
         round_w1(1, 1, 0, 128, "S")
         open_block(1, 0)
         open_block(1, 1)
         open_block(1, 2, (0,))
         open_block(0, 3)
         close_block(0, 3)
-        quantise_w1(1, 1)
+        quantise_w1(1, 1, 2)
         close_block(1, 0)
         close_block(1, 1)
         quantise_h(0, 0)
@@ -396,8 +404,8 @@ def tile_list_floating_strike_payoffs_kernel(tc, tab_words, tab_scales, offs, w1
             second_stage(0, n)
         second_stage_turned(0, 0)
         settle_turned(0, 0, "bank5")
-        cap_block_gpsimd(1, 2, 112, 256)
-        cap_block(1, 2, 0, 112, source=caps_ps)
+        cap_block_gpsimd(1, 2, 96, 256)
+        cap_block(1, 2, 0, 96, source=caps_ps)
         cap_block(1, 3, source=caps_ps)
         payoff(0, 1, 512)
         quantise_h(1, 1)

@@ -20,69 +20,117 @@ ALU = mybir.AluOpType
 P = 128
 PACK = 4
 PASS = P * PACK
-JB = 256
-JC = 512
+BLOCK = 256
+SPAN = 512
 LIST_ROWS = 16
-W1_CUTS = {(0, 0): (0, 128), (1, 0): (0, 128), (0, 1): (0, 128), (1, 1): (0, 128)}
-SPLIT = ((0, 1),)
-NARROW = ((0, 2), (0, 3), (1, 1), (1, 2))
-PARTED = ()
 REPEAT = 16
-FIRST_BANKS = ((0, 1, 2, 3, 4, 5, 4, 5), (6, 0, 1, 2, 3, 4, 0, 2))
-SECOND_BANKS = ((6, 1, 3, 4), (0, 2, 6, 1))
+W1_LOADS = {(0, 0): (0, 128), (1, 0): (0, 128), (0, 1): (0, 64, 128), (1, 1): (0, 128)}
+WIDE = ((0, 0), (0, 1), (1, 0))
+FIRST_BANKS = ((0, 1, 2, 3, 4, 5, 0, 1), (6, 2, 3, 4, 5, 0, 1, 6))
+SECOND_BANKS = ((0, 5, 1, 6), (5, 0, 1, 6))
+OPENED_AHEAD = ((1, 0), (0, 1, 2, 3))
+TURNED = (0,)
+TURN_BANKS = (3, 4)
+SUM_BANKS = (2, 3)
+TENANTS = {
+    "v_words0": "w1_bf00",
+    "h_bf00": "raw01_64",
+    "h_bf01_0": "raw01_64",
+    "w1_bf11": "w1_bf01",
+    "h_bf01_1": "w1_bf01",
+    "h_codes00": "raw11_0",
+    "h_codes01": "th10",
+    "h_bf11": "h_bf10",
+    "pay0_2": "h_codes11",
+    "pay0_3": "th10",
+    "price10": "gap0_1",
+}
 
 
 def tile_list_floating_strike_payoffs_kernel(tc, tab_words, tab_scales, offs, w1, cap, w4_words, w4_scales, gT, out):
     nc = tc.nc
     with ExitStack() as ctx:
         keep = ctx.enter_context(tc.tile_pool(name="keep", bufs=1))
-        shared = ctx.enter_context(tc.tile_pool(name="shared", bufs=1))
-        ring = ctx.enter_context(tc.tile_pool(name="ring", bufs=8))
         psum = ctx.enter_context(tc.psum_pool(name="psum", bufs=1))
 
-        tenants = {"v_codes0": "w1_bf00", "h_bf01_1": "w1_bf11", "h_codes01": "w1_codes11", "h_bf11": "h_bf10", "negated00": "w1_codes01", "pay0_2": "h_codes11", "pay0_3": "w1_codes11", "h_bf00": "raw01_0", "h_bf01_0": "w1_bf01"}
-        places = {"raw11_0": 0, "th03": 0, "picked00": 4096, "pay00": 4096, "h_codes00": 6144}
+        def sbuf(shape, dtype, name):
+            return keep.tile(shape, dtype, name=TENANTS.get(name, name), align_bytes=64)
 
-        def late_tile(shape, dtype, name):
-            if name in places:
-                return shared.tile(shape, dtype, name=name, align_bytes=64, offset=places[name])
-            return keep.tile(shape, dtype, name=tenants.get(name, name), align_bytes=64)
+        def bank(index):
+            return psum.tile([P, PASS], F32, name="bank%d" % index)
 
         offsets = keep.tile([P, S // LIST_ROWS], U16, name="offsets")
-        nc.sync.dma_start(offsets[:], offs)
+        tab_plane = sbuf([P, T], U8, "tab_plane")
+        w4_plane = sbuf([P, 2 * N], U8, "w4_plane")
+        w4_codes = sbuf([P, 2, 2 * N], U8, "w4_codes")
+        cap_rows = sbuf([P, PASS], F32, "cap_rows")
+        caps = sbuf([P, 2, REPEAT * PACK], F32, "caps")
+        identity = sbuf([P, P], F32, "identity")
+        table = [sbuf([P, T], I32, "table%d" % a) for a in range(2)]
+        strikes = [sbuf([P, T], F32, "strikes%d" % n) for n in range(N // P)]
+        raw = {
+            (a, b, m0): sbuf([P, PACK, PACK * (m1 - m0)], F32, "raw%d%d_%d" % (a, b, m0))
+            for (a, b), cuts in W1_LOADS.items() for m0, m1 in zip(cuts, cuts[1:])
+        }
+        caps_ps = psum.tile([P, P, PACK], F32, name="bank7")
+
+        nc.vector.memset(tab_plane[:].bitcast(I32), 0)
+        nc.vector.memset(cap_rows[:], 0.0)
+        nc.vector.memset(w4_plane[:].bitcast(I32), 0)
+        make_identity(nc, identity[:])
 
         def picks(j0, n):
             return offsets[:, j0 // LIST_ROWS : (j0 + n) // LIST_ROWS]
 
-        tab_plane = keep.tile([P, T], U8, name="tab_plane", align_bytes=64)
-        tab_rows = keep.tile([P, T // 4], I32, name="tab_rows", align_bytes=64)
-        w4_plane = keep.tile([P, 2 * N], U8, name="w4_plane", align_bytes=64)
-        nc.vector.memset(tab_plane[:].bitcast(I32), 0)
-        nc.vector.memset(w4_plane[:].bitcast(I32), 0)
+        def load_w1(a, b, m0):
+            c0 = b * PASS + PACK * m0
+            rows = w1[a * PASS : (a + 1) * PASS, c0 : c0 + raw[a, b, m0].shape[2]]
+            nc.sync.dma_start(out=raw[a, b, m0][:], in_=rows.rearrange("(p i) c -> p i c", i=PACK))
 
-        tab = [keep.tile([P, T], I32, name="tab%d" % a, align_bytes=64) for a in range(2)]
-        raw = {
-            (a, b, m0): late_tile([P, PACK, PACK * (m1 - m0)], F32, "raw%d%d_%d" % (a, b, m0))
-            for (a, b), cuts in W1_CUTS.items() for m0, m1 in zip(cuts, cuts[1:])
-        }
-        strikes = [keep.tile([P, T], F32, name="strikes%d" % n, align_bytes=64) for n in range(N // P)]
-        caps = keep.tile([P, 2, REPEAT * PACK], F32, name="caps", align_bytes=64)
-        cap_rows = keep.tile([P, PASS], F32, name="cap_rows", align_bytes=64)
-        identity = keep.tile([P, P], F32, name="identity", align_bytes=64)
-        caps_ps = psum.tile([P, P, PACK], F32, name="bank7")
-        nc.vector.memset(cap_rows[:], 0.0)
-        make_identity(nc, identity[:])
-        w4_codes = keep.tile([P, 2, 2 * N], U8, name="w4_codes", align_bytes=64)
+        def load_table(a):
+            nc.sync.dma_start(out=table[a][:], in_=tab_words[a].rearrange("p t i -> p (t i)").bitcast(I32))
 
-        def load_tab_plane():
-            for q in range(4):
-                nc.sync.dma_start(
-                    out=tab_rows[32 * q : 32 * q + 8, :],
-                    in_=tab_scales[:, 4 * q : 4 * q + 4, :].bitcast(I32),
-                )
+        def load_strikes(n):
+            nc.sync.dma_start(out=strikes[n][:], in_=gT[n * P : (n + 1) * P, :])
 
-        def load_caps():
-            nc.sync.dma_start(out=cap_rows[0:2, :], in_=cap.rearrange("(b c) -> b c", b=2))
+        load_w1(0, 0, 0)
+        nc.sync.dma_start(offsets[:], offs)
+        for q in range(4):
+            nc.sync.dma_start(out=tab_plane[32 * q : 32 * q + 8, :].bitcast(I32), in_=tab_scales[:, 4 * q : 4 * q + 4, :].bitcast(I32))
+        load_table(0)
+        load_w1(1, 0, 0)
+        nc.sync.dma_start(out=cap_rows[0:2, :], in_=cap.rearrange("(b c) -> b c", b=2))
+        load_table(1)
+        load_w1(0, 1, 0)
+        load_w1(0, 1, 64)
+        load_w1(1, 1, 0)
+        load_strikes(0)
+        load_strikes(1)
+        nc.sync.dma_start(out=w4_codes[:].bitcast(I32), in_=w4_words.rearrange("a p c -> p a c").bitcast(I32))
+        for q in range(4):
+            nc.sync.dma_start(
+                out=w4_plane[32 * q : 32 * q + 4, :].rearrange("p (a c) -> p a c", a=2).bitcast(I32),
+                in_=w4_scales[:, 4 * q : 4 * q + 4, :].rearrange("a r c -> r a c").bitcast(I32),
+            )
+        load_strikes(2)
+        load_strikes(3)
+
+        v_plane = sbuf([P, S], U8, "v_plane")
+        v_words, w1_bf, w1_codes, w1_plane = {}, {}, {}, {}
+        sums, th, h_bf, h_codes, h_plane = {}, {}, {}, {}, {}
+        logs, prices, picked, negated = {}, {}, {}, {}
+
+        def once(store, key, shape, dtype, name):
+            if key not in store:
+                store[key] = sbuf(shape, dtype, name)
+            return store[key]
+
+        def gather_plane():
+            nc.vector.tensor_copy(v_plane[:], tab_plane[:].indirect(offsets[:]))
+
+        def gather_words(a, j0, n):
+            words = once(v_words, a, [P, S], U32, "v_words%d" % a)
+            nc.vector.tensor_copy(words[:, j0 : j0 + n], table[a][:].bitcast(U32).indirect(picks(j0, n)))
 
         def spread_caps():
             for t in range(PACK):
@@ -93,327 +141,231 @@ def tile_list_floating_strike_payoffs_kernel(tc, tab_words, tab_scales, offs, w1
                 ACT.Copy,
             )
 
-        def load_tab(a):
-            nc.sync.dma_start(out=tab[a][:], in_=tab_words[a].rearrange("p t i -> p (t i)").bitcast(I32))
-
-        def load_w1(a, b, m0=0):
-            width = raw[a, b, m0].shape[2]
-            c0 = b * PASS + PACK * m0
-            nc.sync.dma_start(
-                out=raw[a, b, m0][:],
-                in_=w1[a * PASS : (a + 1) * PASS, c0 : c0 + width].rearrange("(p i) c -> p i c", i=PACK),
-            )
-
-        def load_w4():
-            nc.sync.dma_start(out=w4_codes[:].bitcast(I32), in_=w4_words.rearrange("a p c -> p a c").bitcast(I32))
-            for q in range(4):
-                nc.sync.dma_start(
-                    out=w4_plane[32 * q : 32 * q + 4, :].rearrange("p (a c) -> p a c", a=2).bitcast(I32),
-                    in_=w4_scales[:, 4 * q : 4 * q + 4, :].rearrange("a r c -> r a c").bitcast(I32),
-                )
-
-        def load_strikes(n):
-            nc.sync.dma_start(out=strikes[n][:], in_=gT[n * P : (n + 1) * P, :])
-
-        load_tab_plane()
-        load_w1(0, 0, 0)
-        load_caps()
-        load_tab(0)
-        load_w1(1, 0, 0)
-        load_tab(1)
-        load_w1(0, 1)
-        load_w1(1, 1)
-        load_strikes(0)
-        load_w4()
-        for n in range(1, 4):
-            load_strikes(n)
-
-        v_codes = {}
-        v_plane = keep.tile([P, S], U8, name="v_plane", align_bytes=64)
-        w1_bf = {}
-        w1_codes = {}
-        w1_plane = {k: keep.tile([P, PASS], U8, name="w1_plane%d%d" % k, align_bytes=64) for k in W1_CUTS}
-
-        def gather_plane():
-            for q in range(4):
-                nc.vector.tensor_copy(tab_plane[32 * q : 32 * q + 8, :].bitcast(I32), tab_rows[32 * q : 32 * q + 8, :])
-            nc.vector.tensor_copy(v_plane[:], tab_plane[:].indirect(offsets[:]))
-
-        def gather_words(a, j0, n):
-            if a not in v_codes:
-                v_codes[a] = late_tile([P, S], U32, "v_codes%d" % a)
-            nc.vector.tensor_copy(v_codes[a][:, j0 : j0 + n], tab[a][:].bitcast(U32).indirect(picks(j0, n)))
-
-        def round_w1(a, b, m0, m1, how):
-            if (a, b) not in w1_bf:
-                w1_bf[a, b] = late_tile([P, PASS * PACK], BF16, "w1_bf%d%d" % (a, b))
-            u = max(c for c in W1_CUTS[a, b] if c <= m0)
-            dst = w1_bf[a, b][:].rearrange("p (t m i) -> p m i t", t=PACK, i=PACK)[:, m0:m1]
-            src = raw[a, b, u][:].rearrange("p i (m t) -> p m i t", t=PACK)[:, m0 - u : m1 - u]
-            if how == "S":
+        def round_w1(a, b, m0, m1, engine):
+            rounded = once(w1_bf, (a, b), [P, PASS * PACK], BF16, "w1_bf%d%d" % (a, b))
+            first = max(c for c in W1_LOADS[a, b] if c <= m0)
+            dst = rounded[:].rearrange("p (t m i) -> p m i t", t=PACK, i=PACK)[:, m0:m1]
+            src = raw[a, b, first][:].rearrange("p i (m t) -> p m i t", t=PACK)[:, m0 - first : m1 - first]
+            if engine is nc.scalar:
                 nc.scalar.activation(dst, src, ACT.Copy)
-            elif how == "G":
-                nc.gpsimd.tensor_copy(dst.rearrange("p m i t -> p t m i"), src.rearrange("p m i t -> p t m i"))
+            elif engine is nc.gpsimd:
+                nc.gpsimd.tensor_scalar(dst.rearrange("p m i t -> p m t i"), src.rearrange("p m i t -> p m t i"), 1.0, 0.0, ALU.mult, ALU.add)
             else:
                 nc.vector.tensor_copy(dst, src)
 
+        def quantise(codes, plane, values):
+            nc.vector.quantize_mx(out=codes.bitcast(FP8X4), scales=plane, in_=values)
+
         def quantise_w1(a, b, pieces=1):
-            w1_codes[a, b] = late_tile([P, PASS], U32, "w1_codes%d%d" % (a, b))
+            w1_codes[a, b] = sbuf([P, PASS], U32, "w1_codes%d%d" % (a, b))
+            w1_plane[a, b] = sbuf([P, PASS], U8, "w1_plane%d%d" % (a, b))
             width = PASS // pieces
             for c0 in range(0, PASS, width):
-                nc.vector.quantize_mx(
-                    out=w1_codes[a, b][:, c0 : c0 + width].bitcast(FP8X4),
-                    scales=w1_plane[a, b][:, c0 : c0 + width],
-                    in_=w1_bf[a, b][:, PACK * c0 : PACK * (c0 + width)],
-                )
-
-        banks = {}
+                quantise(w1_codes[a, b][:, c0 : c0 + width], w1_plane[a, b][:, c0 : c0 + width], w1_bf[a, b][:, PACK * c0 : PACK * (c0 + width)])
 
         def first_pass(a, b, jb, u):
             if a == 0:
-                banks[b, jb, u] = psum.tile([P, 2 * JB], F32, name="bank%d" % FIRST_BANKS[b][2 * jb + u])
-            if (b, jb) in NARROW:
-                cols = slice(jb * JB + u * P, jb * JB + (u + 1) * P)
-                for t in range(PACK):
-                    nc.tensor.matmul_mx(
-                        out=banks[b, jb, u][:, t * P : (t + 1) * P],
-                        lhsT=w1_codes[a, b][:, t * P : (t + 1) * P].bitcast(FP8X4),
-                        lhsT_scale=w1_plane[a, b][:, t * P : (t + 1) * P],
-                        rhs=v_codes[a][:, cols].bitcast(FP8X4),
-                        rhs_scale=v_plane[4 * a :, cols],
-                        start=(a == 0 and t == 0),
-                        stop=(a == 1 and t == PACK - 1),
-                    )
-                return
-            cols = slice(jb * JB, (jb + 1) * JB)
-            for e in range(2):
-                t = 2 * u + e
+                sums[b, jb, u] = bank(FIRST_BANKS[b][2 * jb + u])
+            if (b, jb) in WIDE:
+                slots, j0, width = (2 * u, 2 * u + 1), jb * BLOCK, BLOCK
+            else:
+                slots, j0, width = range(PACK), jb * BLOCK + u * P, P
+            for e, t in enumerate(slots):
                 nc.tensor.matmul_mx(
-                    out=banks[b, jb, u][:, e * JB : (e + 1) * JB],
+                    out=sums[b, jb, u][:, e * width : (e + 1) * width],
                     lhsT=w1_codes[a, b][:, t * P : (t + 1) * P].bitcast(FP8X4),
                     lhsT_scale=w1_plane[a, b][:, t * P : (t + 1) * P],
-                    rhs=v_codes[a][:, cols].bitcast(FP8X4),
-                    rhs_scale=v_plane[4 * a :, cols],
+                    rhs=v_words[a][:, j0 : j0 + width].bitcast(FP8X4),
+                    rhs_scale=v_plane[4 * a :, j0 : j0 + width],
                     start=(a == 0 and e == 0),
-                    stop=(a == 1 and e == 1),
+                    stop=(a == 1 and e == len(slots) - 1),
                 )
-
-        halves = [(b, jc) for b in range(2) for jc in range(S // JC)]
-        th = {}
-        h_bf = {}
-        h_codes = {}
-        h_plane = {k: keep.tile([P, JC], U8, name="h_plane%d%d" % k, align_bytes=64) for k in halves}
 
         def open_block(b, jb, halves=(0, 1)):
             for u in halves:
                 first_pass(0, b, jb, u)
 
-        def close_block(b, jb, halves=(0, 1)):
-            if (b, jb) not in PARTED:
-                th[b, jb] = late_tile([P, 2, JB, 2], F32, "th%d%d" % (b, jb))
-            for u in halves:
+        def close_block(b, jb):
+            th[b, jb] = sbuf([P, 2, PASS], F32, "th%d%d" % (b, jb))
+            slots = 2 if (b, jb) in WIDE else PACK
+            for u in range(2):
                 first_pass(1, b, jb, u)
-                if (b, jb) in PARTED:
-                    th[b, jb, u] = late_tile([P, P * PACK], F32, "th%d%d_%d" % (b, jb, u))
-                if (b, jb) in NARROW:
-                    dst = narrow_values(b, jb, u * P, (u + 1) * P).rearrange("p (j t) -> p j t", t=PACK)
-                    nc.scalar.activation(dst, banks[b, jb, u][:].rearrange("p (t j) -> p j t", t=PACK), ACT.Tanh)
-                else:
-                    nc.scalar.activation(th[b, jb][:, u, :, :], banks[b, jb, u][:].rearrange("p (e j) -> p j e", e=2), ACT.Tanh)
+                nc.scalar.activation(
+                    th[b, jb][:, u, :].rearrange("p (j e) -> p j e", e=slots),
+                    sums[b, jb, u][:].rearrange("p (e j) -> p j e", e=slots),
+                    ACT.Tanh,
+                )
 
         def h_block(b, jb):
             jc, part = divmod(jb, 2)
-            if (b, jc) in SPLIT:
-                if (b, jc, part) not in h_bf:
-                    h_bf[b, jc, part] = late_tile([P, JB * PACK], BF16, "h_bf%d%d_%d" % (b, jc, part))
-                return h_bf[b, jc, part][:]
-            if (b, jc) not in h_bf:
-                h_bf[b, jc] = late_tile([P, JC * PACK], BF16, "h_bf%d%d" % (b, jc))
-            return h_bf[b, jc][:, part * JB * PACK : (part + 1) * JB * PACK]
+            if (b, jc) == (0, 1):
+                return once(h_bf, (b, jc, part), [P, BLOCK * PACK], BF16, "h_bf%d%d_%d" % (b, jc, part))[:]
+            whole = once(h_bf, (b, jc), [P, SPAN * PACK], BF16, "h_bf%d%d" % (b, jc))
+            return whole[:, part * BLOCK * PACK : (part + 1) * BLOCK * PACK]
 
-        def narrow_values(b, jb, j0, j1):
-            if (b, jb) in PARTED:
-                u = j0 // P
-                return th[b, jb, u][:, (j0 - u * P) * PACK : (j1 - u * P) * PACK]
-            return th[b, jb][:].rearrange("p u j e -> p (u j e)")[:, j0 * PACK : j1 * PACK]
-
-        def cap_block_gpsimd(b, jb, j0=0, j1=JB):
+        def cap_gpsimd(b, jb, j0=0, j1=BLOCK):
             row = REPEAT * PACK
             dst = h_block(b, jb)[:, j0 * PACK : j1 * PACK].rearrange("p (x c) -> p x c", c=row)
-            src = narrow_values(b, jb, j0, j1).rearrange("p (x c) -> p x c", c=row)
+            src = th[b, jb][:].rearrange("p u c -> p (u c)")[:, j0 * PACK : j1 * PACK].rearrange("p (x c) -> p x c", c=row)
             nc.gpsimd.tensor_tensor(dst, src, caps[:, b : b + 1, :].to_broadcast([P, (j1 - j0) // REPEAT, row]), ALU.mult)
 
-        def cap_block(b, jb, j0=0, j1=JB, source=caps):
+        def cap_vector(b, jb, j0=0, j1=BLOCK):
             dst = h_block(b, jb).rearrange("p (j u e) -> p j u e", u=2, e=2)[:, j0:j1]
-            if (b, jb) in NARROW:
-                src = narrow_values(b, jb, j0, j1).rearrange("p (j u e) -> p j u e", u=2, e=2)
+            if (b, jb) in WIDE:
+                src = th[b, jb][:].rearrange("p u (j e) -> p j u e", e=2)[:, j0:j1]
             else:
-                src = th[b, jb][:].rearrange("p u j e -> p j u e")[:, j0:j1]
-            factor = source[:, b : b + 1, 0:PACK].rearrange("p o (u e) -> p o u e", u=2).to_broadcast([P, j1 - j0, 2, 2])
+                src = th[b, jb][:].rearrange("p u (j v e) -> p (u j) v e", v=2, e=2)[:, j0:j1]
+            factor = caps_ps[:, b : b + 1, :].rearrange("p o (u e) -> p o u e", u=2).to_broadcast([P, j1 - j0, 2, 2])
             nc.vector.tensor_tensor(dst, src, factor, ALU.mult)
 
-        scaled = {}
-
-        def scale_block(b, jb, j0=0, j1=JB):
-            scaled[b, jb] = late_tile([P, PACK, j1 - j0], BF16, "scaled%d%d" % (b, jb))
-            for t in range(PACK):
-                u, e = divmod(t, 2)
-                nc.scalar.activation(scaled[b, jb][:, t, :], th[b, jb][:, u, j0:j1, e], ACT.Copy, scale=caps[:, b, t : t + 1])
-
-        def weave_block(b, jb, j0=0, j1=JB):
-            dst = h_block(b, jb).rearrange("p (j t) -> p j t", t=PACK)[:, j0:j1]
-            nc.scalar.copy(dst, scaled[b, jb][:].rearrange("p t j -> p j t"))
-
         def quantise_h(b, jc, part=None):
-            if (b, jc) not in h_codes:
-                h_codes[b, jc] = late_tile([P, JC], U32, "h_codes%d%d" % (b, jc))
+            codes = once(h_codes, (b, jc), [P, SPAN], U32, "h_codes%d%d" % (b, jc))
+            plane = once(h_plane, (b, jc), [P, SPAN], U8, "h_plane%d%d" % (b, jc))
             if part is None:
-                nc.vector.quantize_mx(out=h_codes[b, jc][:].bitcast(FP8X4), scales=h_plane[b, jc][:], in_=h_bf[b, jc][:])
+                quantise(codes[:], plane[:], h_bf[b, jc][:])
             else:
-                cols = slice(part * JB, (part + 1) * JB)
-                nc.vector.quantize_mx(out=h_codes[b, jc][:, cols].bitcast(FP8X4), scales=h_plane[b, jc][:, cols], in_=h_block(b, 2 * jc + part))
+                cols = slice(part * BLOCK, (part + 1) * BLOCK)
+                quantise(codes[:, cols], plane[:, cols], h_block(b, 2 * jc + part))
 
-        prices = {}
+        def w4_operand(b, n):
+            return w4_codes[:, b, 2 * n * P : 2 * (n + 1) * P].bitcast(FP4X4), w4_plane[:, b * N + n * P : b * N + (n + 1) * P]
+
+        def second_pass(b, jc, n):
+            if b == 0:
+                logs[jc, n] = bank(SECOND_BANKS[jc][n])
+            codes, plane = w4_operand(b, n)
+            if n in TURNED:
+                for q in range(PACK):
+                    cols = slice(q * P, (q + 1) * P)
+                    nc.tensor.matmul_mx(
+                        out=logs[jc, n][:, cols], lhsT=h_codes[b, jc][:, cols].bitcast(FP8X4), lhsT_scale=h_plane[b, jc][:, cols],
+                        rhs=codes, rhs_scale=plane,
+                        start=(b == 0 and q == 0), stop=(b == 1 and q == PACK - 1),
+                    )
+            else:
+                nc.tensor.matmul_mx(
+                    out=logs[jc, n][:], lhsT=codes, lhsT_scale=plane,
+                    rhs=h_codes[b, jc][:].bitcast(FP8X4), rhs_scale=h_plane[b, jc][:],
+                    start=(b == 0), stop=(b == 1),
+                )
+
+        def open_span(jc):
+            for n in OPENED_AHEAD[jc]:
+                second_pass(0, jc, n)
 
         def second_stage(jc, n):
-            bank = psum.tile([P, JC], F32, name="bank%d" % SECOND_BANKS[jc][n])
-            for b in range(2):
-                nc.tensor.matmul_mx(
-                    out=bank[:],
-                    lhsT=w4_codes[:, b, 2 * n * P : 2 * (n + 1) * P].bitcast(FP4X4),
-                    lhsT_scale=w4_plane[:, b * N + n * P : b * N + (n + 1) * P],
-                    rhs=h_codes[b, jc][:].bitcast(FP8X4),
-                    rhs_scale=h_plane[b, jc][:],
-                    start=(b == 0),
-                    stop=(b == 1),
-                )
-            prices[jc, n] = keep.tile([P, JC], F32, name="price%d%d" % (jc, n), align_bytes=64)
-            nc.scalar.activation(prices[jc, n][:], bank[:], ACT.Exp)
-
-        picked = {}
+            if n not in OPENED_AHEAD[jc]:
+                second_pass(0, jc, n)
+            second_pass(1, jc, n)
+            prices[jc, n] = sbuf([P, SPAN], F32, "price%d%d" % (jc, n))
+            nc.scalar.activation(prices[jc, n][:], logs[jc, n][:], ACT.Exp)
 
         def pick_strikes(jc, n):
-            picked[jc, n] = late_tile([P, JC], F32, "picked%d%d" % (jc, n))
-            nc.vector.tensor_copy(picked[jc, n][:], strikes[n][:].indirect(picks(jc * JC, JC)))
+            picked[jc, n] = sbuf([P, SPAN], F32, "picked%d%d" % (jc, n))
+            nc.vector.tensor_copy(picked[jc, n][:], strikes[n][:].indirect(picks(jc * SPAN, SPAN)))
 
-        def settle(jc, n, engine, c0=0, c1=JC):
-            price = prices[jc, n][:, c0:c1]
-            gap = picked[jc, n][:, c0:c1]
-            engine.tensor_tensor(gap, price, gap, ALU.subtract)
-            nc.scalar.activation(price, gap, ACT.Relu)
-            nc.sync.dma_start(out=out[n * P : (n + 1) * P, jc * JC + c0 : jc * JC + c1], in_=price)
+        def turn_strikes(jc, n):
+            turned = bank(TURN_BANKS[jc])
+            for q in range(PACK):
+                cols = slice(q * P, (q + 1) * P)
+                nc.tensor.transpose(turned[:, cols], picked[jc, n][:, cols], identity[:])
+            negated[jc, n] = sbuf([P, SPAN], F32, "negated%d%d" % (jc, n))
+            nc.scalar.activation(negated[jc, n][:], turned[:], ACT.Copy, scale=-1.0)
 
-        negated = {}
-
-        def turn_strikes(jc, n, bank_name):
-            bank = psum.tile([P, JC], F32, name=bank_name)
-            for q in range(JC // P):
-                nc.tensor.transpose(bank[:, q * P : (q + 1) * P], picked[jc, n][:, q * P : (q + 1) * P], identity[:])
-            negated[jc, n] = late_tile([P, JC], F32, "negated%d%d" % (jc, n))
-            nc.scalar.activation(negated[jc, n][:], bank[:], ACT.Copy, scale=-1.0)
-
-        def second_stage_turned(jc, n):
-            bank = psum.tile([P, JC], F32, name="bank%d" % SECOND_BANKS[jc][n])
-            for b in range(2):
-                for q in range(JC // P):
-                    nc.tensor.matmul_mx(
-                        out=bank[:, q * P : (q + 1) * P],
-                        lhsT=h_codes[b, jc][:, q * P : (q + 1) * P].bitcast(FP8X4),
-                        lhsT_scale=h_plane[b, jc][:, q * P : (q + 1) * P],
-                        rhs=w4_codes[:, b, 2 * n * P : 2 * (n + 1) * P].bitcast(FP4X4),
-                        rhs_scale=w4_plane[:, b * N + n * P : b * N + (n + 1) * P],
-                        start=(b == 0 and q == 0),
-                        stop=(b == 1 and q == JC // P - 1),
-                    )
-            prices[jc, n] = keep.tile([P, JC], F32, name="price%d%d" % (jc, n), align_bytes=64)
-            nc.scalar.activation(prices[jc, n][:], bank[:], ACT.Exp)
-
-        def settle_turned(jc, n, bank_name):
-            bank = psum.tile([P, JC], F32, name=bank_name)
-            terms = (negated[jc, n], prices[jc, n])
-            for k, term in enumerate(terms):
-                for q in range(JC // P):
+        def payoff_turned(jc, n):
+            gap = bank(SUM_BANKS[jc])
+            for k, term in enumerate((negated[jc, n], prices[jc, n])):
+                for q in range(PACK):
+                    cols = slice(q * P, (q + 1) * P)
                     nc.tensor.matmul(
-                        bank[:, q * P : (q + 1) * P], term[:, q * P : (q + 1) * P], identity[:],
-                        start=(k == 0 and q == 0), stop=(k == 1 and q == JC // P - 1), is_transpose=True,
+                        gap[:, cols], term[:, cols], identity[:],
+                        start=(k == 0 and q == 0), stop=(k == 1 and q == PACK - 1), is_transpose=True,
                     )
-            pay = late_tile([P, JC], F32, "pay%d%d" % (jc, n))
-            nc.scalar.activation(pay[:], bank[:], ACT.Relu)
-            nc.sync.dma_start(out=out[n * P : (n + 1) * P, jc * JC : (jc + 1) * JC], in_=pay[:])
+            pay = sbuf([P, SPAN], F32, "pay_turned%d%d" % (jc, n))
+            nc.scalar.activation(pay[:], gap[:], ACT.Relu)
+            nc.sync.dma_start(out=out[n * P : (n + 1) * P, jc * SPAN : (jc + 1) * SPAN], in_=pay[:])
 
         def payoff(j0, n, width, queue=nc.sync):
-            jc, off = divmod(j0, JC)
+            jc, off = divmod(j0, SPAN)
             price = prices[jc, n][:, off : off + width]
-            gap = ring.tile([P, width], F32, name="gap", align_bytes=64)
+            gap = sbuf([P, width], F32, "gap%d_%d" % (j0, n))
             nc.vector.tensor_tensor(gap[:], strikes[n][:].indirect(picks(j0, width)), price, ALU.subtract)
             name = "pay%d_%d" % (j0, n)
-            pay = late_tile([P, width], F32, name)[:] if name in tenants or name in places else price
+            pay = sbuf([P, width], F32, name)[:] if name in TENANTS else price
             nc.scalar.activation(pay, gap[:], ACT.Relu, scale=-1.0)
             queue.dma_start(out=out[n * P : (n + 1) * P, j0 : j0 + width], in_=pay)
 
-        round_w1(0, 0, 0, 104, "S")
+        round_w1(0, 0, 0, 128, nc.scalar)
         gather_plane()
-        round_w1(0, 0, 104, 128, "V")
         quantise_w1(0, 0)
-        spread_caps()
         gather_words(0, 0, 256)
         open_block(0, 0)
         gather_words(0, 256, 256)
-        round_w1(1, 0, 0, 88, "S")
+        round_w1(1, 0, 0, 104, nc.scalar)
         open_block(0, 1)
         gather_words(0, 512, 512)
-        round_w1(1, 0, 88, 128, "V")
+        round_w1(1, 0, 104, 128, nc.vector)
         open_block(0, 2)
         quantise_w1(1, 0)
+        spread_caps()
         gather_words(1, 0, 256)
         close_block(0, 0)
         gather_words(1, 256, 256)
         close_block(0, 1)
         gather_words(1, 512, 512)
         close_block(0, 2)
-        round_w1(0, 1, 0, 128, "V")
+        open_block(0, 3)
+        close_block(0, 3)
+        round_w1(0, 1, 0, 64, nc.gpsimd)
+        round_w1(0, 1, 64, 128, nc.vector)
         quantise_w1(0, 1)
-        cap_block_gpsimd(0, 2, 32, 256)
-        cap_block(0, 0, source=caps_ps)
-        cap_block(0, 1, source=caps_ps)
-        cap_block(0, 2, 0, 32, source=caps_ps)
-        round_w1(1, 1, 0, 128, "S")
+        round_w1(1, 1, 0, 80, nc.gpsimd)
+        cap_vector(0, 0)
+        cap_vector(0, 1)
+        round_w1(1, 1, 80, 128, nc.scalar)
         open_block(1, 0)
         open_block(1, 1)
         open_block(1, 2, (0,))
-        open_block(0, 3)
-        close_block(0, 3)
         quantise_w1(1, 1, 2)
         close_block(1, 0)
         close_block(1, 1)
         quantise_h(0, 0)
-        cap_block_gpsimd(0, 3)
+        cap_gpsimd(0, 2)
+        cap_gpsimd(0, 3, 48, 256)
         pick_strikes(0, 0)
+        pick_strikes(1, 0)
         open_block(1, 2, (1,))
         close_block(1, 2)
+        turn_strikes(0, 0)
+        turn_strikes(1, 0)
         open_block(1, 3)
         close_block(1, 3)
-        cap_block(1, 0, source=caps_ps)
-        cap_block_gpsimd(1, 1, 0, 64)
-        cap_block(1, 1, 64, 256, source=caps_ps)
-        turn_strikes(0, 0, "bank5")
+        open_span(0)
+        cap_vector(0, 3, 0, 48)
+        cap_vector(1, 0)
+        cap_vector(1, 1)
         quantise_h(0, 1, 0)
         quantise_h(1, 0)
         quantise_h(0, 1, 1)
-        for n in range(1, 4):
-            second_stage(0, n)
-        second_stage_turned(0, 0)
-        settle_turned(0, 0, "bank5")
-        cap_block_gpsimd(1, 2, 96, 256)
-        cap_block(1, 2, 0, 96, source=caps_ps)
-        cap_block(1, 3, source=caps_ps)
+        second_stage(0, 1)
+        second_stage(0, 0)
+        second_stage(0, 2)
+        payoff_turned(0, 0)
+        second_stage(0, 3)
+        open_span(1)
+        cap_gpsimd(1, 2, 96, 256)
+        cap_vector(1, 2, 0, 96)
+        cap_vector(1, 3)
         payoff(0, 1, 512)
         quantise_h(1, 1)
-        for n in range(4):
+        second_stage(1, 0)
+        second_stage(1, 1)
+        payoff_turned(1, 0)
+        for n in range(2, 4):
             second_stage(1, n)
         for n in range(2, 4):
             payoff(0, n, 512)
-        for n in range(3):
+        for n in range(1, 3):
             payoff(512, n, 512)
         payoff(512, 3, 256)
         payoff(768, 3, 128)

@@ -24,36 +24,37 @@ BLOCK = 256
 SPAN = 512
 LIST_ROWS = 16
 REPEAT = 16
-W1_LOADS = {(0, 0): (0, 128), (1, 0): (0, 128), (0, 1): (0, 64, 128), (1, 1): (0, 128)}
-WIDE = ((0, 0), (0, 1), (1, 0))
-FIRST_BANKS = ((0, 1, 2, 3, 4, 5, 0, 1), (6, 2, 3, 4, 5, 0, 1, 6))
-SECOND_BANKS = ((0, 5, 1, 6), (5, 0, 1, 6))
-OPENED_AHEAD = ((1, 0), (0, 1, 2, 3))
-TURNED = (0,)
-TURN_BANKS = (3, 4)
-SUM_BANKS = (2, 3)
+W1_LOADS = {(0, 0): (0, 128), (1, 0): (0, 128), (0, 1): (0, 128), (1, 1): (0, 64, 128)}
+WIDE = ((0, 0), (0, 1), (1, 0), (1, 3))
+FIRST_BANKS = ((0, 1, 2, 3, 4, 5, 4, 5), (6, 0, 1, 2, 3, 4, 0, 2))
+SECOND_BANKS = ((6, 1, 3, 4), (0, 2, 6, 1))
+TURNED = (0, 0)
+TURN_BANK = 5
 TENANTS = {
     "v_words0": "w1_bf00",
-    "h_bf00": "raw01_64",
-    "h_bf01_0": "raw01_64",
-    "w1_bf11": "w1_bf01",
-    "h_bf01_1": "w1_bf01",
-    "h_codes00": "raw11_0",
-    "h_codes01": "th10",
+    "h_bf00": "raw01_0",
+    "h_bf01_0": "w1_bf01",
+    "h_bf01_1": "w1_bf11",
+    "h_codes01": "w1_codes11",
     "h_bf11": "h_bf10",
+    "negated00": "w1_codes01",
     "pay0_2": "h_codes11",
-    "pay0_3": "th10",
-    "price10": "gap0_1",
+    "pay0_3": "w1_codes11",
 }
+PLACES = {"raw11_0": 0, "raw11_64": 4096, "th03": 6144, "picked00": 0, "pay_turned00": 0, "h_codes00": 4096}
 
 
 def tile_list_floating_strike_payoffs_kernel(tc, tab_words, tab_scales, offs, w1, cap, w4_words, w4_scales, gT, out):
     nc = tc.nc
     with ExitStack() as ctx:
         keep = ctx.enter_context(tc.tile_pool(name="keep", bufs=1))
+        shared = ctx.enter_context(tc.tile_pool(name="shared", bufs=1))
+        ring = ctx.enter_context(tc.tile_pool(name="ring", bufs=8))
         psum = ctx.enter_context(tc.psum_pool(name="psum", bufs=1))
 
         def sbuf(shape, dtype, name):
+            if name in PLACES:
+                return shared.tile(shape, dtype, name=name, align_bytes=64, offset=PLACES[name])
             return keep.tile(shape, dtype, name=TENANTS.get(name, name), align_bytes=64)
 
         def bank(index):
@@ -102,16 +103,16 @@ def tile_list_floating_strike_payoffs_kernel(tc, tab_words, tab_scales, offs, w1
         nc.sync.dma_start(out=cap_rows[0:2, :], in_=cap.rearrange("(b c) -> b c", b=2))
         load_table(1)
         load_w1(0, 1, 0)
-        load_w1(0, 1, 64)
         load_w1(1, 1, 0)
+        load_w1(1, 1, 64)
         load_strikes(0)
-        load_strikes(1)
         nc.sync.dma_start(out=w4_codes[:].bitcast(I32), in_=w4_words.rearrange("a p c -> p a c").bitcast(I32))
         for q in range(4):
             nc.sync.dma_start(
                 out=w4_plane[32 * q : 32 * q + 4, :].rearrange("p (a c) -> p a c", a=2).bitcast(I32),
                 in_=w4_scales[:, 4 * q : 4 * q + 4, :].rearrange("a r c -> r a c").bitcast(I32),
             )
+        load_strikes(1)
         load_strikes(2)
         load_strikes(3)
 
@@ -148,8 +149,6 @@ def tile_list_floating_strike_payoffs_kernel(tc, tab_words, tab_scales, offs, w1
             src = raw[a, b, first][:].rearrange("p i (m t) -> p m i t", t=PACK)[:, m0 - first : m1 - first]
             if engine is nc.scalar:
                 nc.scalar.activation(dst, src, ACT.Copy)
-            elif engine is nc.gpsimd:
-                nc.gpsimd.tensor_scalar(dst.rearrange("p m i t -> p m t i"), src.rearrange("p m i t -> p m t i"), 1.0, 0.0, ALU.mult, ALU.add)
             else:
                 nc.vector.tensor_copy(dst, src)
 
@@ -234,7 +233,7 @@ def tile_list_floating_strike_payoffs_kernel(tc, tab_words, tab_scales, offs, w1
             if b == 0:
                 logs[jc, n] = bank(SECOND_BANKS[jc][n])
             codes, plane = w4_operand(b, n)
-            if n in TURNED:
+            if (jc, n) == TURNED:
                 for q in range(PACK):
                     cols = slice(q * P, (q + 1) * P)
                     nc.tensor.matmul_mx(
@@ -249,14 +248,9 @@ def tile_list_floating_strike_payoffs_kernel(tc, tab_words, tab_scales, offs, w1
                     start=(b == 0), stop=(b == 1),
                 )
 
-        def open_span(jc):
-            for n in OPENED_AHEAD[jc]:
-                second_pass(0, jc, n)
-
         def second_stage(jc, n):
-            if n not in OPENED_AHEAD[jc]:
-                second_pass(0, jc, n)
-            second_pass(1, jc, n)
+            for b in range(2):
+                second_pass(b, jc, n)
             prices[jc, n] = sbuf([P, SPAN], F32, "price%d%d" % (jc, n))
             nc.scalar.activation(prices[jc, n][:], logs[jc, n][:], ACT.Exp)
 
@@ -265,7 +259,7 @@ def tile_list_floating_strike_payoffs_kernel(tc, tab_words, tab_scales, offs, w1
             nc.vector.tensor_copy(picked[jc, n][:], strikes[n][:].indirect(picks(jc * SPAN, SPAN)))
 
         def turn_strikes(jc, n):
-            turned = bank(TURN_BANKS[jc])
+            turned = bank(TURN_BANK)
             for q in range(PACK):
                 cols = slice(q * P, (q + 1) * P)
                 nc.tensor.transpose(turned[:, cols], picked[jc, n][:, cols], identity[:])
@@ -273,7 +267,7 @@ def tile_list_floating_strike_payoffs_kernel(tc, tab_words, tab_scales, offs, w1
             nc.scalar.activation(negated[jc, n][:], turned[:], ACT.Copy, scale=-1.0)
 
         def payoff_turned(jc, n):
-            gap = bank(SUM_BANKS[jc])
+            gap = bank(TURN_BANK)
             for k, term in enumerate((negated[jc, n], prices[jc, n])):
                 for q in range(PACK):
                     cols = slice(q * P, (q + 1) * P)
@@ -288,7 +282,7 @@ def tile_list_floating_strike_payoffs_kernel(tc, tab_words, tab_scales, offs, w1
         def payoff(j0, n, width, queue=nc.sync):
             jc, off = divmod(j0, SPAN)
             price = prices[jc, n][:, off : off + width]
-            gap = sbuf([P, width], F32, "gap%d_%d" % (j0, n))
+            gap = ring.tile([P, width], F32, name="gap", align_bytes=64)
             nc.vector.tensor_tensor(gap[:], strikes[n][:].indirect(picks(j0, width)), price, ALU.subtract)
             name = "pay%d_%d" % (j0, n)
             pay = sbuf([P, width], F32, name)[:] if name in TENANTS else price
@@ -314,58 +308,50 @@ def tile_list_floating_strike_payoffs_kernel(tc, tab_words, tab_scales, offs, w1
         close_block(0, 1)
         gather_words(1, 512, 512)
         close_block(0, 2)
-        open_block(0, 3)
-        close_block(0, 3)
-        round_w1(0, 1, 0, 64, nc.gpsimd)
-        round_w1(0, 1, 64, 128, nc.vector)
+        round_w1(0, 1, 0, 128, nc.vector)
         quantise_w1(0, 1)
-        round_w1(1, 1, 0, 80, nc.gpsimd)
+        cap_gpsimd(0, 2, 32, 256)
         cap_vector(0, 0)
         cap_vector(0, 1)
-        round_w1(1, 1, 80, 128, nc.scalar)
+        cap_vector(0, 2, 0, 32)
+        round_w1(1, 1, 0, 64, nc.scalar)
+        round_w1(1, 1, 64, 128, nc.scalar)
         open_block(1, 0)
         open_block(1, 1)
         open_block(1, 2, (0,))
+        open_block(0, 3)
+        close_block(0, 3)
         quantise_w1(1, 1, 2)
         close_block(1, 0)
         close_block(1, 1)
         quantise_h(0, 0)
-        cap_gpsimd(0, 2)
-        cap_gpsimd(0, 3, 48, 256)
+        cap_gpsimd(0, 3)
         pick_strikes(0, 0)
-        pick_strikes(1, 0)
         open_block(1, 2, (1,))
         close_block(1, 2)
-        turn_strikes(0, 0)
-        turn_strikes(1, 0)
         open_block(1, 3)
         close_block(1, 3)
-        open_span(0)
-        cap_vector(0, 3, 0, 48)
         cap_vector(1, 0)
-        cap_vector(1, 1)
+        cap_gpsimd(1, 1, 0, 64)
+        cap_vector(1, 1, 64, 256)
+        turn_strikes(0, 0)
         quantise_h(0, 1, 0)
         quantise_h(1, 0)
         quantise_h(0, 1, 1)
-        second_stage(0, 1)
+        for n in range(1, 4):
+            second_stage(0, n)
         second_stage(0, 0)
-        second_stage(0, 2)
         payoff_turned(0, 0)
-        second_stage(0, 3)
-        open_span(1)
         cap_gpsimd(1, 2, 96, 256)
         cap_vector(1, 2, 0, 96)
         cap_vector(1, 3)
         payoff(0, 1, 512)
         quantise_h(1, 1)
-        second_stage(1, 0)
-        second_stage(1, 1)
-        payoff_turned(1, 0)
-        for n in range(2, 4):
+        for n in range(4):
             second_stage(1, n)
         for n in range(2, 4):
             payoff(0, n, 512)
-        for n in range(1, 3):
+        for n in range(3):
             payoff(512, n, 512)
         payoff(512, 3, 256)
         payoff(768, 3, 128)

@@ -31,7 +31,7 @@ SECOND_BANKS = ((6, 1, 3, 4), (0, 2, 6, 1))
 TURNED = (0, 0)
 TURN_BANK = 5
 TENANTS = {
-    "v_words0": "w1_bf00",
+    "v_words0": "raw00_0",
     "h_bf00": "raw01_0",
     "h_bf01_0": "w1_bf01",
     "h_bf01_1": "w1_bf11",
@@ -61,6 +61,7 @@ def tile_list_floating_strike_payoffs_kernel(tc, tab_words, tab_scales, offs, w1
             return psum.tile([P, PASS], F32, name="bank%d" % index)
 
         offsets = keep.tile([P, S // LIST_ROWS], U16, name="offsets")
+        tab_rows = sbuf([P, T // 4], I32, "tab_rows")
         tab_plane = sbuf([P, T], U8, "tab_plane")
         w4_plane = sbuf([P, 2 * N], U8, "w4_plane")
         w4_codes = sbuf([P, 2, 2 * N], U8, "w4_codes")
@@ -94,13 +95,13 @@ def tile_list_floating_strike_payoffs_kernel(tc, tab_words, tab_scales, offs, w1
         def load_strikes(n):
             nc.sync.dma_start(out=strikes[n][:], in_=gT[n * P : (n + 1) * P, :])
 
-        load_w1(0, 0, 0)
         nc.sync.dma_start(offsets[:], offs)
         for q in range(4):
-            nc.sync.dma_start(out=tab_plane[32 * q : 32 * q + 8, :].bitcast(I32), in_=tab_scales[:, 4 * q : 4 * q + 4, :].bitcast(I32))
+            nc.sync.dma_start(out=tab_rows[32 * q : 32 * q + 8, :], in_=tab_scales[:, 4 * q : 4 * q + 4, :].bitcast(I32))
+        load_w1(0, 0, 0)
+        nc.sync.dma_start(out=cap_rows[0:2, :], in_=cap.rearrange("(b c) -> b c", b=2))
         load_table(0)
         load_w1(1, 0, 0)
-        nc.sync.dma_start(out=cap_rows[0:2, :], in_=cap.rearrange("(b c) -> b c", b=2))
         load_table(1)
         load_w1(0, 1, 0)
         load_w1(1, 1, 0)
@@ -127,6 +128,8 @@ def tile_list_floating_strike_payoffs_kernel(tc, tab_words, tab_scales, offs, w1
             return store[key]
 
         def gather_plane():
+            for q in range(4):
+                nc.vector.tensor_copy(tab_plane[32 * q : 32 * q + 8, :].bitcast(I32), tab_rows[32 * q : 32 * q + 8, :])
             nc.vector.tensor_copy(v_plane[:], tab_plane[:].indirect(offsets[:]))
 
         def gather_words(a, j0, n):
@@ -289,19 +292,20 @@ def tile_list_floating_strike_payoffs_kernel(tc, tab_words, tab_scales, offs, w1
             nc.scalar.activation(pay, gap[:], ACT.Relu, scale=-1.0)
             queue.dma_start(out=out[n * P : (n + 1) * P, j0 : j0 + width], in_=pay)
 
-        round_w1(0, 0, 0, 128, nc.scalar)
+        round_w1(0, 0, 0, 88, nc.scalar)
         gather_plane()
+        round_w1(0, 0, 88, 128, nc.vector)
         quantise_w1(0, 0)
+        spread_caps()
         gather_words(0, 0, 256)
         open_block(0, 0)
         gather_words(0, 256, 256)
-        round_w1(1, 0, 0, 104, nc.scalar)
+        round_w1(1, 0, 0, 64, nc.scalar)
         open_block(0, 1)
         gather_words(0, 512, 512)
-        round_w1(1, 0, 104, 128, nc.vector)
+        round_w1(1, 0, 64, 128, nc.vector)
         open_block(0, 2)
         quantise_w1(1, 0)
-        spread_caps()
         gather_words(1, 0, 256)
         close_block(0, 0)
         gather_words(1, 256, 256)

@@ -25,7 +25,7 @@ SPAN = 512
 LIST_ROWS = 16
 REPEAT = 16
 W1_LOADS = {(0, 0): (0, 128), (1, 0): (0, 128), (0, 1): (0, 128), (1, 1): (0, 64, 128)}
-WIDE = ((0, 0), (0, 1), (1, 0), (1, 3))
+WIDE = ((0, 1), (1, 0), (1, 3))
 FIRST_BANKS = ((0, 1, 2, 3, 4, 5, 4, 5), (6, 0, 1, 2, 3, 4, 0, 2))
 SECOND_BANKS = ((6, 1, 3, 4), (0, 2, 6, 1))
 TURNED = (0, 0)
@@ -145,11 +145,11 @@ def tile_list_floating_strike_payoffs_kernel(tc, tab_words, tab_scales, offs, w1
                 ACT.Copy,
             )
 
-        def round_w1(a, b, m0, m1, engine):
+        def round_w1(a, b, m0, m1, engine, slots=slice(0, PACK)):
             rounded = once(w1_bf, (a, b), [P, PASS * PACK], BF16, "w1_bf%d%d" % (a, b))
             first = max(c for c in W1_LOADS[a, b] if c <= m0)
-            dst = rounded[:].rearrange("p (t m i) -> p m i t", t=PACK, i=PACK)[:, m0:m1]
-            src = raw[a, b, first][:].rearrange("p i (m t) -> p m i t", t=PACK)[:, m0 - first : m1 - first]
+            dst = rounded[:].rearrange("p (t m i) -> p m i t", t=PACK, i=PACK)[:, m0:m1, :, slots]
+            src = raw[a, b, first][:].rearrange("p i (m t) -> p m i t", t=PACK)[:, m0 - first : m1 - first, :, slots]
             if engine is nc.scalar:
                 nc.scalar.activation(dst, src, ACT.Copy)
             else:
@@ -306,14 +306,16 @@ def tile_list_floating_strike_payoffs_kernel(tc, tab_words, tab_scales, offs, w1
         round_w1(1, 0, 64, 128, nc.vector)
         open_block(0, 2)
         quantise_w1(1, 0)
-        gather_words(1, 0, 256)
+        gather_words(1, 0, 128)
+        gather_words(1, 128, 128)
         close_block(0, 0)
         gather_words(1, 256, 256)
         close_block(0, 1)
         gather_words(1, 512, 512)
         close_block(0, 2)
-        round_w1(0, 1, 0, 128, nc.vector)
-        quantise_w1(0, 1)
+        round_w1(0, 1, 0, 128, nc.vector, slice(0, 2))
+        round_w1(0, 1, 0, 128, nc.vector, slice(2, 4))
+        quantise_w1(0, 1, 2)
         cap_gpsimd(0, 2, 32, 256)
         cap_vector(0, 0)
         cap_vector(0, 1)

@@ -25,6 +25,8 @@ SPAN = 512
 LIST_ROWS = 16
 REPEAT = 16
 W1_LOADS = {(0, 0): (0, 128), (1, 0): (0, 128), (0, 1): (0, 128), (1, 1): (0, 64, 128)}
+H_CUTS = ((0, 256, 512, 768, 1024), (0, 512, 1024))
+CODE_CUTS = ((0, 256, 512, 1024), (0, 512, 1024))
 WIDE = ((0, 1), (1, 0), (1, 3))
 FIRST_BANKS = ((0, 1, 2, 3, 4, 5, 4, 5), (6, 0, 1, 2, 3, 4, 0, 2))
 SECOND_BANKS = ((6, 1, 3, 4), (0, 2, 6, 1))
@@ -32,16 +34,15 @@ TURNED = (0, 0)
 TURN_BANK = 5
 TENANTS = {
     "v_words0": "raw00_0",
-    "h_bf00": "raw01_0",
-    "h_bf01_0": "w1_bf01",
-    "h_bf01_1": "w1_bf11",
-    "h_codes01": "w1_codes11",
-    "h_bf11": "h_bf10",
+    "h_bf0_0": "w1_bf01", "h_bf0_256": "raw01_0",
+    "h_bf0_768": "w1_bf11",
+    "h_codes0_512": "th10",
+    "h_bf1_512": "h_bf1_0",
     "negated00": "w1_codes01",
-    "pay0_2": "h_codes11",
-    "pay0_3": "w1_codes11",
+    "pay0_2": "h_codes1_512",
+    "pay0_3": "th10",
 }
-PLACES = {"raw11_0": 0, "raw11_64": 4096, "th03": 6144, "picked00": 0, "pay_turned00": 0, "h_codes00": 4096}
+PLACES = {"raw11_0": 0, "raw11_64": 4096, "th03": 6144, "picked00": 0, "pay_turned00": 0, "h_codes0_0": 4096}
 
 
 def tile_list_floating_strike_payoffs_kernel(tc, tab_words, tab_scales, offs, w1, cap, w4_words, w4_scales, gT, out):
@@ -188,46 +189,46 @@ def tile_list_floating_strike_payoffs_kernel(tc, tab_words, tab_scales, offs, w1
                 first_pass(0, b, jb, u)
 
         def close_block(b, jb):
-            th[b, jb] = sbuf([P, 2, PASS], F32, "th%d%d" % (b, jb))
+            th[b, jb] = sbuf([P, 2 * PASS], F32, "th%d%d" % (b, jb))
             slots = 2 if (b, jb) in WIDE else PACK
             for u in range(2):
                 first_pass(1, b, jb, u)
                 nc.scalar.activation(
-                    th[b, jb][:, u, :].rearrange("p (j e) -> p j e", e=slots),
+                    th[b, jb][:, u * PASS : (u + 1) * PASS].rearrange("p (j e) -> p j e", e=slots),
                     sums[b, jb, u][:].rearrange("p (e j) -> p j e", e=slots),
                     ACT.Tanh,
                 )
 
-        def h_block(b, jb):
-            jc, part = divmod(jb, 2)
-            if (b, jc) == (0, 1):
-                return once(h_bf, (b, jc, part), [P, BLOCK * PACK], BF16, "h_bf%d%d_%d" % (b, jc, part))[:]
-            whole = once(h_bf, (b, jc), [P, SPAN * PACK], BF16, "h_bf%d%d" % (b, jc))
-            return whole[:, part * BLOCK * PACK : (part + 1) * BLOCK * PACK]
+        def h_values(b, j0, j1):
+            first = max(c for c in H_CUTS[b] if c <= j0)
+            end = min(c for c in H_CUTS[b] if c > j0)
+            piece = once(h_bf, (b, first), [P, (end - first) * PACK], BF16, "h_bf%d_%d" % (b, first))
+            return piece[:, (j0 - first) * PACK : (j1 - first) * PACK]
 
         def cap_gpsimd(b, jb, j0=0, j1=BLOCK):
             row = REPEAT * PACK
-            dst = h_block(b, jb)[:, j0 * PACK : j1 * PACK].rearrange("p (x c) -> p x c", c=row)
-            src = th[b, jb][:].rearrange("p u c -> p (u c)")[:, j0 * PACK : j1 * PACK].rearrange("p (x c) -> p x c", c=row)
+            dst = h_values(b, jb * BLOCK + j0, jb * BLOCK + j1).rearrange("p (x c) -> p x c", c=row)
+            src = th[b, jb][:, j0 * PACK : j1 * PACK].rearrange("p (x c) -> p x c", c=row)
             nc.gpsimd.tensor_tensor(dst, src, caps[:, b : b + 1, :].to_broadcast([P, (j1 - j0) // REPEAT, row]), ALU.mult)
 
         def cap_vector(b, jb, j0=0, j1=BLOCK):
-            dst = h_block(b, jb).rearrange("p (j u e) -> p j u e", u=2, e=2)[:, j0:j1]
+            dst = h_values(b, jb * BLOCK + j0, jb * BLOCK + j1).rearrange("p (j u e) -> p j u e", u=2, e=2)
             if (b, jb) in WIDE:
-                src = th[b, jb][:].rearrange("p u (j e) -> p j u e", e=2)[:, j0:j1]
+                src = th[b, jb][:].rearrange("p (u j e) -> p j u e", u=2, e=2)[:, j0:j1]
             else:
-                src = th[b, jb][:].rearrange("p u (j v e) -> p (u j) v e", v=2, e=2)[:, j0:j1]
+                src = th[b, jb][:, j0 * PACK : j1 * PACK].rearrange("p (j u e) -> p j u e", u=2, e=2)
             factor = caps_ps[:, b : b + 1, :].rearrange("p o (u e) -> p o u e", u=2).to_broadcast([P, j1 - j0, 2, 2])
             nc.vector.tensor_tensor(dst, src, factor, ALU.mult)
 
-        def quantise_h(b, jc, part=None):
-            codes = once(h_codes, (b, jc), [P, SPAN], U32, "h_codes%d%d" % (b, jc))
-            plane = once(h_plane, (b, jc), [P, SPAN], U8, "h_plane%d%d" % (b, jc))
-            if part is None:
-                quantise(codes[:], plane[:], h_bf[b, jc][:])
-            else:
-                cols = slice(part * BLOCK, (part + 1) * BLOCK)
-                quantise(codes[:, cols], plane[:, cols], h_block(b, 2 * jc + part))
+        def h_operand(b, j0, j1):
+            first = max(c for c in CODE_CUTS[b] if c <= j0)
+            end = min(c for c in CODE_CUTS[b] if c > j0)
+            codes = once(h_codes, (b, first), [P, end - first], U32, "h_codes%d_%d" % (b, first))
+            plane = once(h_plane, (b, first), [P, end - first], U8, "h_plane%d_%d" % (b, first))
+            return codes[:, j0 - first : j1 - first], plane[:, j0 - first : j1 - first]
+
+        def quantise_h(b, j0, j1):
+            quantise(*h_operand(b, j0, j1), h_values(b, j0, j1))
 
         def w4_operand(b, n):
             return w4_codes[:, b, 2 * n * P : 2 * (n + 1) * P].bitcast(FP4X4), w4_plane[:, b * N + n * P : b * N + (n + 1) * P]
@@ -238,18 +239,21 @@ def tile_list_floating_strike_payoffs_kernel(tc, tab_words, tab_scales, offs, w1
             codes, plane = w4_operand(b, n)
             if (jc, n) == TURNED:
                 for q in range(PACK):
-                    cols = slice(q * P, (q + 1) * P)
+                    h_words, h_scales = h_operand(b, jc * SPAN + q * P, jc * SPAN + (q + 1) * P)
                     nc.tensor.matmul_mx(
-                        out=logs[jc, n][:, cols], lhsT=h_codes[b, jc][:, cols].bitcast(FP8X4), lhsT_scale=h_plane[b, jc][:, cols],
+                        out=logs[jc, n][:, q * P : (q + 1) * P], lhsT=h_words.bitcast(FP8X4), lhsT_scale=h_scales,
                         rhs=codes, rhs_scale=plane,
                         start=(b == 0 and q == 0), stop=(b == 1 and q == PACK - 1),
                     )
             else:
-                nc.tensor.matmul_mx(
-                    out=logs[jc, n][:], lhsT=codes, lhsT_scale=plane,
-                    rhs=h_codes[b, jc][:].bitcast(FP8X4), rhs_scale=h_plane[b, jc][:],
-                    start=(b == 0), stop=(b == 1),
-                )
+                cuts = [c for c in CODE_CUTS[b] if jc * SPAN <= c <= (jc + 1) * SPAN]
+                for j0, j1 in zip(cuts, cuts[1:]):
+                    h_words, h_scales = h_operand(b, j0, j1)
+                    nc.tensor.matmul_mx(
+                        out=logs[jc, n][:, j0 - jc * SPAN : j1 - jc * SPAN], lhsT=codes, lhsT_scale=plane,
+                        rhs=h_words.bitcast(FP8X4), rhs_scale=h_scales,
+                        start=(b == 0 and j0 == cuts[0]), stop=(b == 1 and j1 == cuts[-1]),
+                    )
 
         def second_stage(jc, n):
             for b in range(2):
@@ -316,10 +320,10 @@ def tile_list_floating_strike_payoffs_kernel(tc, tab_words, tab_scales, offs, w1
         round_w1(0, 1, 0, 128, nc.vector, slice(0, 2))
         round_w1(0, 1, 0, 128, nc.vector, slice(2, 4))
         quantise_w1(0, 1, 2)
-        cap_gpsimd(0, 2, 32, 256)
-        cap_vector(0, 0)
+        cap_gpsimd(0, 0, 16, 256)
         cap_vector(0, 1)
-        cap_vector(0, 2, 0, 32)
+        cap_vector(0, 2)
+        cap_vector(0, 0, 0, 16)
         round_w1(1, 1, 0, 64, nc.scalar)
         round_w1(1, 1, 64, 128, nc.scalar)
         open_block(1, 0)
@@ -327,23 +331,25 @@ def tile_list_floating_strike_payoffs_kernel(tc, tab_words, tab_scales, offs, w1
         open_block(1, 2, (0,))
         open_block(0, 3)
         close_block(0, 3)
+        quantise_h(0, 256, 512)
         quantise_w1(1, 1, 2)
         close_block(1, 0)
         close_block(1, 1)
-        quantise_h(0, 0)
-        cap_gpsimd(0, 3)
+        quantise_h(0, 0, 256)
+        cap_gpsimd(0, 3, 32, 256)
         pick_strikes(0, 0)
+        cap_vector(0, 3, 0, 32)
         open_block(1, 2, (1,))
         close_block(1, 2)
         open_block(1, 3)
         close_block(1, 3)
         cap_vector(1, 0)
-        cap_gpsimd(1, 1, 0, 64)
-        cap_vector(1, 1, 64, 256)
+        cap_gpsimd(1, 1, 0, 80)
+        cap_vector(1, 1, 80, 256)
         turn_strikes(0, 0)
-        quantise_h(0, 1, 0)
-        quantise_h(1, 0)
-        quantise_h(0, 1, 1)
+        quantise_h(0, 512, 768)
+        quantise_h(1, 0, 512)
+        quantise_h(0, 768, 1024)
         for n in range(1, 4):
             second_stage(0, n)
         second_stage(0, 0)
@@ -352,7 +358,7 @@ def tile_list_floating_strike_payoffs_kernel(tc, tab_words, tab_scales, offs, w1
         cap_vector(1, 2, 0, 96)
         cap_vector(1, 3)
         payoff(0, 1, 512)
-        quantise_h(1, 1)
+        quantise_h(1, 512, 1024)
         for n in range(4):
             second_stage(1, n)
         for n in range(2, 4):

@@ -24,7 +24,7 @@ BLOCK = 256
 SPAN = 512
 LIST_ROWS = 16
 REPEAT = 16
-W1_LOADS = {(0, 0): (0, 128), (1, 0): (0, 128), (0, 1): (0, 128), (1, 1): (0, 64, 128)}
+W1_LOADS = {(0, 0): (0, 128), (1, 0): (0, 64, 128), (0, 1): (0, 128), (1, 1): (0, 64, 128)}
 H_CUTS = ((0, 256, 512, 768, 1024), (0, 512, 1024))
 CODE_CUTS = ((0, 256, 512, 1024), (0, 512, 1024))
 WIDE = ((0, 1), (1, 0), (1, 3))
@@ -33,8 +33,6 @@ SECOND_BANKS = ((6, 1, 3, 4), (0, 2, 6, 1))
 TURNED = (0, 0)
 TURN_BANK = 5
 TENANTS = {
-    "v_words0": "raw00_0",
-    "h_bf0_0": "w1_bf01", "h_bf0_256": "raw01_0",
     "h_bf0_768": "w1_bf11",
     "h_codes0_512": "th10",
     "h_bf1_512": "h_bf1_0",
@@ -42,7 +40,16 @@ TENANTS = {
     "pay0_2": "h_codes1_512",
     "pay0_3": "th10",
 }
-PLACES = {"raw11_0": 0, "raw11_64": 4096, "th03": 6144, "picked00": 0, "pay_turned00": 0, "h_codes0_0": 4096}
+KB = 1024
+ROWS_AT = 96
+PLACES = {
+    "table0": 0, "raw11_0": 0, "raw11_64": 4 * KB, "th03": 6 * KB, "picked00": 0, "pay_turned00": 0, "h_codes0_0": 4 * KB,
+    "raw10_0": 10 * KB, "raw10_64": 14 * KB, "strikes0": 10 * KB,
+    "tab_rows": 17 * KB, "table1": 18 * KB, "strikes1": 18 * KB,
+    "raw00_0": 26 * KB, "v_words0": 26 * KB, "raw01_0": 30 * KB, "h_bf0_256": 30 * KB, "strikes2": 32 * KB,
+    "w1_bf10": 40 * KB, "w4_codes": 40 * KB, "w4_plane": 42 * KB,
+    "w1_bf01": 44 * KB, "h_bf0_0": 44 * KB, "strikes3": 46 * KB,
+}
 
 
 def tile_list_floating_strike_payoffs_kernel(tc, tab_words, tab_scales, offs, w1, cap, w4_words, w4_scales, gT, out):
@@ -62,63 +69,64 @@ def tile_list_floating_strike_payoffs_kernel(tc, tab_words, tab_scales, offs, w1
             return psum.tile([P, PASS], F32, name="bank%d" % index)
 
         offsets = keep.tile([P, S // LIST_ROWS], U16, name="offsets")
-        tab_rows = sbuf([P, T // 4], I32, "tab_rows")
-        tab_plane = sbuf([P, T], U8, "tab_plane")
-        w4_plane = sbuf([P, 2 * N], U8, "w4_plane")
-        w4_codes = sbuf([P, 2, 2 * N], U8, "w4_codes")
+        tab_rows = sbuf([P, T], U8, "tab_rows")
+        v_rows = sbuf([P, S], U8, "v_rows")
+        v_plane = [sbuf([P, S], U8, "v_plane%d" % a) for a in range(2)]
         cap_rows = sbuf([P, PASS], F32, "cap_rows")
         caps = sbuf([P, 2, REPEAT * PACK], F32, "caps")
         identity = sbuf([P, P], F32, "identity")
-        table = [sbuf([P, T], I32, "table%d" % a) for a in range(2)]
-        strikes = [sbuf([P, T], F32, "strikes%d" % n) for n in range(N // P)]
-        raw = {
-            (a, b, m0): sbuf([P, PACK, PACK * (m1 - m0)], F32, "raw%d%d_%d" % (a, b, m0))
-            for (a, b), cuts in W1_LOADS.items() for m0, m1 in zip(cuts, cuts[1:])
-        }
         caps_ps = psum.tile([P, P, PACK], F32, name="bank7")
+        table, strikes, raw, w4 = {}, {}, {}, {}
 
-        nc.vector.memset(tab_plane[:].bitcast(I32), 0)
         nc.vector.memset(cap_rows[:], 0.0)
-        nc.vector.memset(w4_plane[:].bitcast(I32), 0)
+        nc.vector.memset(tab_rows[0:ROWS_AT, :].bitcast(I32), 0)
+        for a in range(2):
+            nc.gpsimd.memset(v_plane[a][:].bitcast(I32), 0)
         make_identity(nc, identity[:])
 
         def picks(j0, n):
             return offsets[:, j0 // LIST_ROWS : (j0 + n) // LIST_ROWS]
 
         def load_w1(a, b, m0):
+            m1 = min(c for c in W1_LOADS[a, b] if c > m0)
+            raw[a, b, m0] = sbuf([P, PACK, PACK * (m1 - m0)], F32, "raw%d%d_%d" % (a, b, m0))
             c0 = b * PASS + PACK * m0
             rows = w1[a * PASS : (a + 1) * PASS, c0 : c0 + raw[a, b, m0].shape[2]]
             nc.sync.dma_start(out=raw[a, b, m0][:], in_=rows.rearrange("(p i) c -> p i c", i=PACK))
 
         def load_table(a):
+            table[a] = sbuf([P, T], I32, "table%d" % a)
             nc.sync.dma_start(out=table[a][:], in_=tab_words[a].rearrange("p t i -> p (t i)").bitcast(I32))
 
         def load_strikes(n):
+            strikes[n] = sbuf([P, T], F32, "strikes%d" % n)
             nc.sync.dma_start(out=strikes[n][:], in_=gT[n * P : (n + 1) * P, :])
 
+        def load_w4():
+            w4["codes"] = sbuf([P, 2, 2 * N], U8, "w4_codes")
+            w4["plane"] = sbuf([P, 2 * N], U8, "w4_plane")
+            nc.gpsimd.memset(w4["plane"][:].bitcast(I32), 0)
+            nc.sync.dma_start(out=w4["codes"][:].bitcast(I32), in_=w4_words.rearrange("a p c -> p a c").bitcast(I32))
+            for q in range(4):
+                nc.sync.dma_start(
+                    out=w4["plane"][32 * q : 32 * q + 4, :].rearrange("p (a c) -> p a c", a=2).bitcast(I32),
+                    in_=w4_scales[:, 4 * q : 4 * q + 4, :].rearrange("a r c -> r a c").bitcast(I32),
+                )
+
+        def move_scales(a):
+            for q in range(4):
+                nc.sync.dma_start(
+                    out=v_plane[a][32 * q : 32 * q + 4, :].bitcast(I32),
+                    in_=v_rows[ROWS_AT + 16 * a + 4 * q : ROWS_AT + 16 * a + 4 * q + 4, :].bitcast(I32),
+                )
+
         nc.sync.dma_start(offsets[:], offs)
-        for q in range(4):
-            nc.sync.dma_start(out=tab_rows[32 * q : 32 * q + 8, :], in_=tab_scales[:, 4 * q : 4 * q + 4, :].bitcast(I32))
+        nc.sync.dma_start(out=tab_rows[ROWS_AT:P, :].bitcast(I32), in_=tab_scales.rearrange("a q t -> (a q) t").bitcast(I32))
         load_w1(0, 0, 0)
         nc.sync.dma_start(out=cap_rows[0:2, :], in_=cap.rearrange("(b c) -> b c", b=2))
         load_table(0)
         load_w1(1, 0, 0)
-        load_table(1)
-        load_w1(0, 1, 0)
-        load_w1(1, 1, 0)
-        load_w1(1, 1, 64)
-        load_strikes(0)
-        nc.sync.dma_start(out=w4_codes[:].bitcast(I32), in_=w4_words.rearrange("a p c -> p a c").bitcast(I32))
-        for q in range(4):
-            nc.sync.dma_start(
-                out=w4_plane[32 * q : 32 * q + 4, :].rearrange("p (a c) -> p a c", a=2).bitcast(I32),
-                in_=w4_scales[:, 4 * q : 4 * q + 4, :].rearrange("a r c -> r a c").bitcast(I32),
-            )
-        load_strikes(1)
-        load_strikes(2)
-        load_strikes(3)
 
-        v_plane = sbuf([P, S], U8, "v_plane")
         v_words, w1_bf, w1_codes, w1_plane = {}, {}, {}, {}
         sums, th, h_bf, h_codes, h_plane = {}, {}, {}, {}, {}
         logs, prices, picked, negated = {}, {}, {}, {}
@@ -129,9 +137,7 @@ def tile_list_floating_strike_payoffs_kernel(tc, tab_words, tab_scales, offs, w1
             return store[key]
 
         def gather_plane():
-            for q in range(4):
-                nc.vector.tensor_copy(tab_plane[32 * q : 32 * q + 8, :].bitcast(I32), tab_rows[32 * q : 32 * q + 8, :])
-            nc.vector.tensor_copy(v_plane[:], tab_plane[:].indirect(offsets[:]))
+            nc.vector.tensor_copy(v_rows[:], tab_rows[:].indirect(offsets[:]))
 
         def gather_words(a, j0, n):
             words = once(v_words, a, [P, S], U32, "v_words%d" % a)
@@ -179,7 +185,7 @@ def tile_list_floating_strike_payoffs_kernel(tc, tab_words, tab_scales, offs, w1
                     lhsT=w1_codes[a, b][:, t * P : (t + 1) * P].bitcast(FP8X4),
                     lhsT_scale=w1_plane[a, b][:, t * P : (t + 1) * P],
                     rhs=v_words[a][:, j0 : j0 + width].bitcast(FP8X4),
-                    rhs_scale=v_plane[4 * a :, j0 : j0 + width],
+                    rhs_scale=v_plane[a][:, j0 : j0 + width],
                     start=(a == 0 and e == 0),
                     stop=(a == 1 and e == len(slots) - 1),
                 )
@@ -231,7 +237,7 @@ def tile_list_floating_strike_payoffs_kernel(tc, tab_words, tab_scales, offs, w1
             quantise(*h_operand(b, j0, j1), h_values(b, j0, j1))
 
         def w4_operand(b, n):
-            return w4_codes[:, b, 2 * n * P : 2 * (n + 1) * P].bitcast(FP4X4), w4_plane[:, b * N + n * P : b * N + (n + 1) * P]
+            return w4["codes"][:, b, 2 * n * P : 2 * (n + 1) * P].bitcast(FP4X4), w4["plane"][:, b * N + n * P : b * N + (n + 1) * P]
 
         def second_pass(b, jc, n):
             if b == 0:
@@ -296,9 +302,14 @@ def tile_list_floating_strike_payoffs_kernel(tc, tab_words, tab_scales, offs, w1
             nc.scalar.activation(pay, gap[:], ACT.Relu, scale=-1.0)
             queue.dma_start(out=out[n * P : (n + 1) * P, j0 : j0 + width], in_=pay)
 
-        round_w1(0, 0, 0, 88, nc.scalar)
+        round_w1(0, 0, 0, 64, nc.scalar)
         gather_plane()
-        round_w1(0, 0, 88, 128, nc.vector)
+        move_scales(0)
+        load_w1(1, 0, 64)
+        load_table(1)
+        move_scales(1)
+        round_w1(0, 0, 64, 128, nc.vector)
+        load_w1(0, 1, 0)
         quantise_w1(0, 0)
         spread_caps()
         gather_words(0, 0, 256)
@@ -307,19 +318,26 @@ def tile_list_floating_strike_payoffs_kernel(tc, tab_words, tab_scales, offs, w1
         round_w1(1, 0, 0, 64, nc.scalar)
         open_block(0, 1)
         gather_words(0, 512, 512)
+        load_w1(1, 1, 0)
+        load_w1(1, 1, 64)
         round_w1(1, 0, 64, 128, nc.vector)
+        load_strikes(0)
         open_block(0, 2)
         quantise_w1(1, 0)
+        load_w4()
         gather_words(1, 0, 128)
         gather_words(1, 128, 128)
         close_block(0, 0)
         gather_words(1, 256, 256)
         close_block(0, 1)
         gather_words(1, 512, 512)
+        load_strikes(1)
         close_block(0, 2)
         round_w1(0, 1, 0, 128, nc.vector, slice(0, 2))
         round_w1(0, 1, 0, 128, nc.vector, slice(2, 4))
+        load_strikes(2)
         quantise_w1(0, 1, 2)
+        load_strikes(3)
         cap_gpsimd(0, 0, 16, 256)
         cap_vector(0, 1)
         cap_vector(0, 2)

from contextlib import ExitStack

import concourse.mybir as mybir
from concourse.masks import make_identity

K, T, S, R, N = 1024, 2048, 1024, 1024, 512
FLOPS = 2 * K * R * S + 2 * R * N * S

F32 = mybir.dt.float32
BF16 = mybir.dt.bfloat16
I32 = mybir.dt.int32
U32 = mybir.dt.uint32
U16 = mybir.dt.uint16
U8 = mybir.dt.uint8
FP8X4 = mybir.dt.float8_e4m3fn_x4
FP4X4 = mybir.dt.float4_e2m1fn_x4
ACT = mybir.ActivationFunctionType
ALU = mybir.AluOpType

P = 128
PACK = 4
PASS = P * PACK
BLOCK = 256
SPAN = 512
LIST_ROWS = 16
REPEAT = 16
W1_LOADS = {(0, 0): (0, 128), (1, 0): (0, 64, 128), (0, 1): (0, 128), (1, 1): (0, 64, 128)}
H_CUTS = ((0, 256, 512, 768, 1024), (0, 512, 1024))
CODE_CUTS = ((0, 256, 512, 1024), (0, 512, 1024))
WIDE = ((0, 1), (1, 0), (1, 3))
FIRST_BANKS = ((0, 1, 2, 3, 4, 5, 4, 5), (6, 0, 1, 2, 3, 4, 0, 2))
SECOND_BANKS = ((6, 1, 3, 4), (0, 2, 6, 1))
TURNED = (0, 0)
TURN_BANK = 5
TENANTS = {
    "h_bf0_768": "w1_bf11",
    "h_codes0_512": "th10",
    "h_bf1_512": "h_bf1_0",
    "negated00": "w1_codes01",
    "pay0_2": "h_codes1_512",
    "pay0_3": "th10",
}
KB = 1024
ROWS_AT = 96
PLACES = {
    "table0": 0, "raw11_0": 0, "raw11_64": 4 * KB, "th03": 6 * KB, "picked00": 0, "pay_turned00": 0, "h_codes0_0": 4 * KB,
    "raw10_0": 10 * KB, "raw10_64": 14 * KB, "strikes0": 10 * KB,
    "tab_rows": 17 * KB, "table1": 18 * KB, "strikes1": 18 * KB,
    "raw00_0": 26 * KB, "v_words0": 26 * KB, "raw01_0": 30 * KB, "h_bf0_256": 30 * KB, "strikes2": 32 * KB,
    "w1_bf10": 40 * KB, "w4_codes": 40 * KB, "w4_plane": 42 * KB,
    "w1_bf01": 44 * KB, "h_bf0_0": 44 * KB, "strikes3": 46 * KB,
}


def tile_list_floating_strike_payoffs_kernel(tc, tab_words, tab_scales, offs, w1, cap, w4_words, w4_scales, gT, out):
    nc = tc.nc
    with ExitStack() as ctx:
        keep = ctx.enter_context(tc.tile_pool(name="keep", bufs=1))
        shared = ctx.enter_context(tc.tile_pool(name="shared", bufs=1))
        ring = ctx.enter_context(tc.tile_pool(name="ring", bufs=8))
        psum = ctx.enter_context(tc.psum_pool(name="psum", bufs=1))

        def sbuf(shape, dtype, name):
            if name in PLACES:
                return shared.tile(shape, dtype, name=name, align_bytes=64, offset=PLACES[name])
            return keep.tile(shape, dtype, name=TENANTS.get(name, name), align_bytes=64)

        def bank(index):
            return psum.tile([P, PASS], F32, name="bank%d" % index)

        offsets = keep.tile([P, S // LIST_ROWS], U16, name="offsets")
        tab_rows = sbuf([P, T], U8, "tab_rows")
        v_rows = sbuf([P, S], U8, "v_rows")
        v_plane = [sbuf([P, S], U8, "v_plane%d" % a) for a in range(2)]
        cap_rows = sbuf([P, PASS], F32, "cap_rows")
        caps = sbuf([P, 2, REPEAT * PACK], F32, "caps")
        identity = sbuf([P, P], F32, "identity")
        caps_ps = psum.tile([P, P, PACK], F32, name="bank7")
        table, strikes, raw, w4 = {}, {}, {}, {}

        nc.vector.memset(cap_rows[:], 0.0)
        nc.vector.memset(tab_rows[0:ROWS_AT, :].bitcast(I32), 0)
        for a in range(2):
            nc.gpsimd.memset(v_plane[a][:].bitcast(I32), 0)
        make_identity(nc, identity[:])

        def picks(j0, n):
            return offsets[:, j0 // LIST_ROWS : (j0 + n) // LIST_ROWS]

        def load_w1(a, b, m0):
            m1 = min(c for c in W1_LOADS[a, b] if c > m0)
            raw[a, b, m0] = sbuf([P, PACK, PACK * (m1 - m0)], F32, "raw%d%d_%d" % (a, b, m0))
            c0 = b * PASS + PACK * m0
            rows = w1[a * PASS : (a + 1) * PASS, c0 : c0 + raw[a, b, m0].shape[2]]
            nc.sync.dma_start(out=raw[a, b, m0][:], in_=rows.rearrange("(p i) c -> p i c", i=PACK))

        def load_table(a):
            table[a] = sbuf([P, T], I32, "table%d" % a)
            nc.sync.dma_start(out=table[a][:], in_=tab_words[a].rearrange("p t i -> p (t i)").bitcast(I32))

        def load_strikes(n):
            strikes[n] = sbuf([P, T], F32, "strikes%d" % n)
            nc.sync.dma_start(out=strikes[n][:], in_=gT[n * P : (n + 1) * P, :])

        def load_w4():
            w4["codes"] = sbuf([P, 2, 2 * N], U8, "w4_codes")
            w4["plane"] = sbuf([P, 2 * N], U8, "w4_plane")
            nc.gpsimd.memset(w4["plane"][:].bitcast(I32), 0)
            nc.sync.dma_start(out=w4["codes"][:].bitcast(I32), in_=w4_words.rearrange("a p c -> p a c").bitcast(I32))
            for q in range(4):
                nc.sync.dma_start(
                    out=w4["plane"][32 * q : 32 * q + 4, :].rearrange("p (a c) -> p a c", a=2).bitcast(I32),
                    in_=w4_scales[:, 4 * q : 4 * q + 4, :].rearrange("a r c -> r a c").bitcast(I32),
                )

        def move_scales(a):
            for q in range(4):
                nc.sync.dma_start(
                    out=v_plane[a][32 * q : 32 * q + 4, :].bitcast(I32),
                    in_=v_rows[ROWS_AT + 16 * a + 4 * q : ROWS_AT + 16 * a + 4 * q + 4, :].bitcast(I32),
                )

        nc.sync.dma_start(offsets[:], offs)
        nc.sync.dma_start(out=tab_rows[ROWS_AT:P, :].bitcast(I32), in_=tab_scales.rearrange("a q t -> (a q) t").bitcast(I32))
        load_w1(0, 0, 0)
        nc.sync.dma_start(out=cap_rows[0:2, :], in_=cap.rearrange("(b c) -> b c", b=2))
        load_table(0)
        load_w1(1, 0, 0)

        v_words, w1_bf, w1_codes, w1_plane = {}, {}, {}, {}
        sums, th, h_bf, h_codes, h_plane = {}, {}, {}, {}, {}
        logs, prices, picked, negated = {}, {}, {}, {}

        def once(store, key, shape, dtype, name):
            if key not in store:
                store[key] = sbuf(shape, dtype, name)
            return store[key]

        def gather_plane():
            nc.vector.tensor_copy(v_rows[:], tab_rows[:].indirect(offsets[:]))

        def gather_words(a, j0, n):
            words = once(v_words, a, [P, S], U32, "v_words%d" % a)
            nc.vector.tensor_copy(words[:, j0 : j0 + n], table[a][:].bitcast(U32).indirect(picks(j0, n)))

        def spread_caps():
            for t in range(PACK):
                nc.tensor.transpose(caps_ps[:, :, t], cap_rows[:, t:PASS:PACK], identity[:])
            nc.scalar.activation(
                caps[:].rearrange("p b (j t) -> p b j t", t=PACK),
                caps_ps[:, 0:2, :].unsqueeze(2).to_broadcast([P, 2, REPEAT, PACK]),
                ACT.Copy,
            )

        def round_w1(a, b, m0, m1, engine, slots=slice(0, PACK)):
            rounded = once(w1_bf, (a, b), [P, PASS * PACK], BF16, "w1_bf%d%d" % (a, b))
            first = max(c for c in W1_LOADS[a, b] if c <= m0)
            dst = rounded[:].rearrange("p (t m i) -> p m i t", t=PACK, i=PACK)[:, m0:m1, :, slots]
            src = raw[a, b, first][:].rearrange("p i (m t) -> p m i t", t=PACK)[:, m0 - first : m1 - first, :, slots]
            if engine is nc.scalar:
                nc.scalar.activation(dst, src, ACT.Copy)
            else:
                nc.vector.tensor_copy(dst, src)

        def quantise(codes, plane, values):
            nc.vector.quantize_mx(out=codes.bitcast(FP8X4), scales=plane, in_=values)

        def quantise_w1(a, b, pieces=1):
            w1_codes[a, b] = sbuf([P, PASS], U32, "w1_codes%d%d" % (a, b))
            w1_plane[a, b] = sbuf([P, PASS], U8, "w1_plane%d%d" % (a, b))
            width = PASS // pieces
            for c0 in range(0, PASS, width):
                quantise(w1_codes[a, b][:, c0 : c0 + width], w1_plane[a, b][:, c0 : c0 + width], w1_bf[a, b][:, PACK * c0 : PACK * (c0 + width)])

        def first_pass(a, b, jb, u):
            if a == 0:
                sums[b, jb, u] = bank(FIRST_BANKS[b][2 * jb + u])
            if (b, jb) in WIDE:
                slots, j0, width = (2 * u, 2 * u + 1), jb * BLOCK, BLOCK
            else:
                slots, j0, width = range(PACK), jb * BLOCK + u * P, P
            for e, t in enumerate(slots):
                nc.tensor.matmul_mx(
                    out=sums[b, jb, u][:, e * width : (e + 1) * width],
                    lhsT=w1_codes[a, b][:, t * P : (t + 1) * P].bitcast(FP8X4),
                    lhsT_scale=w1_plane[a, b][:, t * P : (t + 1) * P],
                    rhs=v_words[a][:, j0 : j0 + width].bitcast(FP8X4),
                    rhs_scale=v_plane[a][:, j0 : j0 + width],
                    start=(a == 0 and e == 0),
                    stop=(a == 1 and e == len(slots) - 1),
                )

        def open_block(b, jb, halves=(0, 1)):
            for u in halves:
                first_pass(0, b, jb, u)

        def close_block(b, jb):
            th[b, jb] = sbuf([P, 2 * PASS], F32, "th%d%d" % (b, jb))
            slots = 2 if (b, jb) in WIDE else PACK
            for u in range(2):
                first_pass(1, b, jb, u)
                nc.scalar.activation(
                    th[b, jb][:, u * PASS : (u + 1) * PASS].rearrange("p (j e) -> p j e", e=slots),
                    sums[b, jb, u][:].rearrange("p (e j) -> p j e", e=slots),
                    ACT.Tanh,
                )

        def h_values(b, j0, j1):
            first = max(c for c in H_CUTS[b] if c <= j0)
            end = min(c for c in H_CUTS[b] if c > j0)
            piece = once(h_bf, (b, first), [P, (end - first) * PACK], BF16, "h_bf%d_%d" % (b, first))
            return piece[:, (j0 - first) * PACK : (j1 - first) * PACK]

        def cap_gpsimd(b, jb, j0=0, j1=BLOCK):
            row = REPEAT * PACK
            dst = h_values(b, jb * BLOCK + j0, jb * BLOCK + j1).rearrange("p (x c) -> p x c", c=row)
            src = th[b, jb][:, j0 * PACK : j1 * PACK].rearrange("p (x c) -> p x c", c=row)
            nc.gpsimd.tensor_tensor(dst, src, caps[:, b : b + 1, :].to_broadcast([P, (j1 - j0) // REPEAT, row]), ALU.mult)

        def cap_vector(b, jb, j0=0, j1=BLOCK):
            dst = h_values(b, jb * BLOCK + j0, jb * BLOCK + j1).rearrange("p (j u e) -> p j u e", u=2, e=2)
            if (b, jb) in WIDE:
                src = th[b, jb][:].rearrange("p (u j e) -> p j u e", u=2, e=2)[:, j0:j1]
            else:
                src = th[b, jb][:, j0 * PACK : j1 * PACK].rearrange("p (j u e) -> p j u e", u=2, e=2)
            factor = caps_ps[:, b : b + 1, :].rearrange("p o (u e) -> p o u e", u=2).to_broadcast([P, j1 - j0, 2, 2])
            nc.vector.tensor_tensor(dst, src, factor, ALU.mult)

        def h_operand(b, j0, j1):
            first = max(c for c in CODE_CUTS[b] if c <= j0)
            end = min(c for c in CODE_CUTS[b] if c > j0)
            codes = once(h_codes, (b, first), [P, end - first], U32, "h_codes%d_%d" % (b, first))
            plane = once(h_plane, (b, first), [P, end - first], U8, "h_plane%d_%d" % (b, first))
            return codes[:, j0 - first : j1 - first], plane[:, j0 - first : j1 - first]

        def quantise_h(b, j0, j1):
            quantise(*h_operand(b, j0, j1), h_values(b, j0, j1))

        def w4_operand(b, n):
            return w4["codes"][:, b, 2 * n * P : 2 * (n + 1) * P].bitcast(FP4X4), w4["plane"][:, b * N + n * P : b * N + (n + 1) * P]

        def second_pass(b, jc, n):
            if b == 0:
                logs[jc, n] = bank(SECOND_BANKS[jc][n])
            codes, plane = w4_operand(b, n)
            if (jc, n) == TURNED:
                for q in range(PACK):
                    h_words, h_scales = h_operand(b, jc * SPAN + q * P, jc * SPAN + (q + 1) * P)
                    nc.tensor.matmul_mx(
                        out=logs[jc, n][:, q * P : (q + 1) * P], lhsT=h_words.bitcast(FP8X4), lhsT_scale=h_scales,
                        rhs=codes, rhs_scale=plane,
                        start=(b == 0 and q == 0), stop=(b == 1 and q == PACK - 1),
                    )
            else:
                cuts = [c for c in CODE_CUTS[b] if jc * SPAN <= c <= (jc + 1) * SPAN]
                for j0, j1 in zip(cuts, cuts[1:]):
                    h_words, h_scales = h_operand(b, j0, j1)
                    nc.tensor.matmul_mx(
                        out=logs[jc, n][:, j0 - jc * SPAN : j1 - jc * SPAN], lhsT=codes, lhsT_scale=plane,
                        rhs=h_words.bitcast(FP8X4), rhs_scale=h_scales,
                        start=(b == 0 and j0 == cuts[0]), stop=(b == 1 and j1 == cuts[-1]),
                    )

        def second_stage(jc, n):
            for b in range(2):
                second_pass(b, jc, n)
            prices[jc, n] = sbuf([P, SPAN], F32, "price%d%d" % (jc, n))
            nc.scalar.activation(prices[jc, n][:], logs[jc, n][:], ACT.Exp)

        def pick_strikes(jc, n):
            picked[jc, n] = sbuf([P, SPAN], F32, "picked%d%d" % (jc, n))
            nc.vector.tensor_copy(picked[jc, n][:], strikes[n][:].indirect(picks(jc * SPAN, SPAN)))

        def turn_strikes(jc, n):
            turned = bank(TURN_BANK)
            for q in range(PACK):
                cols = slice(q * P, (q + 1) * P)
                nc.tensor.transpose(turned[:, cols], picked[jc, n][:, cols], identity[:])
            negated[jc, n] = sbuf([P, SPAN], F32, "negated%d%d" % (jc, n))
            nc.scalar.activation(negated[jc, n][:], turned[:], ACT.Copy, scale=-1.0)

        def payoff_turned(jc, n):
            gap = bank(TURN_BANK)
            for k, term in enumerate((negated[jc, n], prices[jc, n])):
                for q in range(PACK):
                    cols = slice(q * P, (q + 1) * P)
                    nc.tensor.matmul(
                        gap[:, cols], term[:, cols], identity[:],
                        start=(k == 0 and q == 0), stop=(k == 1 and q == PACK - 1), is_transpose=True,
                    )
            pay = sbuf([P, SPAN], F32, "pay_turned%d%d" % (jc, n))
            nc.scalar.activation(pay[:], gap[:], ACT.Relu)
            nc.sync.dma_start(out=out[n * P : (n + 1) * P, jc * SPAN : (jc + 1) * SPAN], in_=pay[:])

        def payoff(j0, n, width, queue=nc.sync):
            jc, off = divmod(j0, SPAN)
            price = prices[jc, n][:, off : off + width]
            gap = ring.tile([P, width], F32, name="gap", align_bytes=64)
            nc.vector.tensor_tensor(gap[:], strikes[n][:].indirect(picks(j0, width)), price, ALU.subtract)
            name = "pay%d_%d" % (j0, n)
            pay = sbuf([P, width], F32, name)[:] if name in TENANTS else price
            nc.scalar.activation(pay, gap[:], ACT.Relu, scale=-1.0)
            queue.dma_start(out=out[n * P : (n + 1) * P, j0 : j0 + width], in_=pay)

        round_w1(0, 0, 0, 64, nc.scalar)
        gather_plane()
        move_scales(0)
        load_w1(1, 0, 64)
        load_table(1)
        move_scales(1)
        round_w1(0, 0, 64, 128, nc.vector)
        load_w1(0, 1, 0)
        quantise_w1(0, 0)
        spread_caps()
        gather_words(0, 0, 256)
        open_block(0, 0)
        gather_words(0, 256, 256)
        round_w1(1, 0, 0, 64, nc.scalar)
        open_block(0, 1)
        gather_words(0, 512, 512)
        load_w1(1, 1, 0)
        load_w1(1, 1, 64)
        round_w1(1, 0, 64, 128, nc.vector)
        load_strikes(0)
        open_block(0, 2)
        quantise_w1(1, 0)
        load_w4()
        gather_words(1, 0, 128)
        gather_words(1, 128, 128)
        close_block(0, 0)
        gather_words(1, 256, 256)
        close_block(0, 1)
        gather_words(1, 512, 512)
        load_strikes(1)
        close_block(0, 2)
        round_w1(0, 1, 0, 128, nc.vector, slice(0, 2))
        round_w1(0, 1, 0, 128, nc.vector, slice(2, 4))
        load_strikes(2)
        quantise_w1(0, 1, 2)
        load_strikes(3)
        cap_gpsimd(0, 0, 16, 256)
        cap_vector(0, 1)
        cap_vector(0, 2)
        cap_vector(0, 0, 0, 16)
        round_w1(1, 1, 0, 64, nc.scalar)
        round_w1(1, 1, 64, 128, nc.scalar)
        open_block(1, 0)
        open_block(1, 1)
        open_block(1, 2, (0,))
        open_block(0, 3)
        close_block(0, 3)
        quantise_h(0, 256, 512)
        quantise_w1(1, 1, 2)
        close_block(1, 0)
        close_block(1, 1)
        quantise_h(0, 0, 256)
        cap_gpsimd(0, 3, 32, 256)
        pick_strikes(0, 0)
        cap_vector(0, 3, 0, 32)
        open_block(1, 2, (1,))
        close_block(1, 2)
        open_block(1, 3)
        close_block(1, 3)
        cap_vector(1, 0)
        cap_gpsimd(1, 1, 0, 80)
        cap_vector(1, 1, 80, 256)
        turn_strikes(0, 0)
        quantise_h(0, 512, 768)
        quantise_h(1, 0, 512)
        quantise_h(0, 768, 1024)
        for n in range(1, 4):
            second_stage(0, n)
        second_stage(0, 0)
        payoff_turned(0, 0)
        cap_gpsimd(1, 2, 96, 256)
        cap_vector(1, 2, 0, 96)
        cap_vector(1, 3)
        payoff(0, 1, 512)
        quantise_h(1, 512, 1024)
        for n in range(4):
            second_stage(1, n)
        for n in range(2, 4):
            payoff(0, n, 512)
        for n in range(3):
            payoff(512, n, 512)
        payoff(512, 3, 256)
        payoff(768, 3, 128)
        payoff(896, 3, 128, nc.scalar)
